import numpy as np
import ml_dtypes


def mxq(x, axis, fmt="e4m3"):
    dtype, down = {"e4m3": (ml_dtypes.float8_e4m3fn, 7), "e5m2": (ml_dtypes.float8_e5m2, 14)}[fmt]
    v = np.moveaxis(np.asarray(x, np.float32).astype(ml_dtypes.bfloat16).astype(np.float64), axis, -1)
    blocks = v.reshape(v.shape[:-1] + (-1, 32))
    amax = np.abs(blocks).max(-1, keepdims=True)
    byte = np.maximum(np.where(amax > 0, np.frexp(amax)[1] - 1 + 127, 0) - down, 1)
    scale = np.exp2(byte - 127.0)
    codes = (blocks / scale).astype(np.float32).astype(dtype).astype(np.float64)
    return np.moveaxis((codes * scale).reshape(v.shape), -1, axis)


WIDE = False


def mx_kscale(k):
    if not WIDE:
        return np.ones(k)
    levels = np.array([10, -10, 5, -5, 0])
    if k % 512:
        return np.exp2(np.random.permutation(np.resize(levels, k // 32))).repeat(32)
    a = np.empty((k // 512, 16))
    for p in range(k // 512):
        a[p, :8] = np.random.permutation(np.resize(levels, 8))
        for g in range(8):
            far = levels[np.abs(levels - a[p, g]) >= 10]
            a[p, g + 8] = far[np.random.randint(len(far))]
    return np.exp2(a.ravel()).repeat(32)


def f64(x):
    return np.asarray(x).astype(np.float64)


def striped(idx):
    return np.tile(np.asarray(idx).reshape(-1, 16).T, (8, 1)).astype(np.uint16)


def unstriped(offs):
    return offs[:16].T.reshape(-1).astype(np.int64)


E2M1 = np.array([0.0, 0.5, 1.0, 1.5, 2.0, 3.0, 4.0, 6.0, -0.0, -0.5, -1.0, -1.5, -2.0, -3.0, -4.0, -6.0])


def pack_weight(w, fmt):
    k, n = w.shape
    w = f64(np.asarray(w, np.float32).astype(ml_dtypes.bfloat16)).reshape(k // 32, 32, n)
    amax = np.abs(w).max(1)
    if fmt == "e4m3":
        byte = np.frexp(amax)[1] - 1 + 127 - 7
    else:
        mant, ex = np.frexp(amax / 6.0)
        byte = np.where(mant > 0.5, ex, ex - 1) + 127
    byte = np.clip(np.where(amax > 0, byte, 1), 1, 254)
    scaled = (w * np.exp2(127.0 - byte)[:, None, :]).reshape(k, n).astype(np.float32)
    by_word = np.ascontiguousarray(scaled.reshape(k // 512, 128, 4, n).transpose(0, 1, 3, 2))
    if fmt == "e4m3":
        words = by_word.astype(ml_dtypes.float8_e4m3fn).view(np.uint8)
    else:
        c = by_word.astype(ml_dtypes.float4_e2m1fn).view(np.uint8) & 0xF
        words = (c[..., 0::2] | (c[..., 1::2] << 4)).reshape(k // 512, 128, 2 * n)
    return np.ascontiguousarray(words), np.ascontiguousarray(byte.astype(np.uint8).reshape(k // 512, 16, n))


def unpack_weight(words, scales, fmt):
    g, _, n = scales.shape
    words = np.ascontiguousarray(words).reshape(g, 128, n, -1)
    if fmt == "e4m3":
        vals = words.view(ml_dtypes.float8_e4m3fn).astype(np.float64)
    else:
        nib = np.empty((g, 128, n, 4), np.uint8)
        nib[..., 0::2] = words & 0xF
        nib[..., 1::2] = words >> 4
        vals = E2M1[nib]
    vals = vals * np.repeat(np.exp2(scales.astype(np.float64) - 127.0), 8, axis=1)[..., None]
    return vals.transpose(0, 1, 3, 2).reshape(g * 512, n)


B, N, T, D, DV, NQ = 2, 512, 2048, 1024, 256, 256
PAGE = 64


def setup_inputs():
    n = np.random.standard_normal
    pages = np.random.permutation(T // PAGE)[:B * N // PAGE]
    idx = (pages[:, None] * PAGE + np.arange(PAGE)[None, :]).reshape(-1)
    s = mx_kscale(D)[:, None]
    u = np.ones(T)
    u[idx] = mx_kscale(B * N)
    r = np.random.uniform(0.5, 2.0, T)
    qp = [pack_weight(x, "e4m3") for x in n((B, D, NQ)) * s * (1.00 / np.sqrt(D))]
    k = n((D, T)) / s
    v = n((DV, T)) / (u * r)
    kp = pack_weight(k, "e4m3")
    return {
        "q_words": np.stack([x[0] for x in qp]),
        "q_scales": np.stack([x[1] for x in qp]),
        "k_words": kp[0],
        "k_scales": kp[1],
        "vT": v.astype(np.float32),
        "vs": np.tile(u * r, (128, 1)).astype(np.float32),
        "og": n((B, NQ, DV)).astype(np.float32),
        "offs": striped(idx),
    }


def reference(q_words, q_scales, k_words, k_scales, vT, vs, og, offs):
    idx = unstriped(offs)
    k = unpack_weight(k_words, k_scales, "e4m3")
    v = f64(vT)
    pick = lambda x: x[:, idx].reshape(x.shape[0], B, N).transpose(1, 0, 2)
    q = np.stack([unpack_weight(q_words[b], q_scales[b], "e4m3") for b in range(B)])
    score = q.transpose(0, 2, 1) @ pick(k)
    p = np.square(np.maximum(score, 0.0))
    total = p.sum(-1, keepdims=True) + 1.0
    w = p * pick(f64(vs))[:, :1, :]
    y = mxq(w, 2, "e4m3") @ mxq(pick(v).transpose(0, 2, 1), 1, "e4m3")
    y = y / total
    y = y / (1.0 + np.exp(-f64(og)))
    return y

@@ -1,0 +1,201 @@
+from contextlib import ExitStack
+
+import concourse.mybir as mybir
+from concourse.masks import make_identity
+
+B, N, T, D, DV, NQ = 2, 512, 2048, 1024, 256, 256
+FLOPS = 2 * B * NQ * N * (D + DV)
+
+F32 = mybir.dt.float32
+BF16 = mybir.dt.bfloat16
+I32 = mybir.dt.int32
+U32 = mybir.dt.uint32
+U16 = mybir.dt.uint16
+U8 = mybir.dt.uint8
+FP8X4 = mybir.dt.float8_e4m3fn_x4
+ACT = mybir.ActivationFunctionType
+ALU = mybir.AluOpType
+
+P = 128
+PASSES = D // 512
+QB = NQ // P
+EB = DV // P
+LIST_COLS = N // 16
+K_PLANE0 = 8
+
+
+def tile_attend_rel2_gate_pgb2q256n512t2048_kernel(tc, q_words, q_scales, k_words, k_scales, vT, vs, og, offs, out):
+    nc = tc.nc
+    with ExitStack() as ctx:
+        keep = ctx.enter_context(tc.tile_pool(name="keep", bufs=1))
+        work = ctx.enter_context(tc.tile_pool(name="work", bufs=2))
+        psum = ctx.enter_context(tc.psum_pool(name="psum", bufs=2))
+
+        offsets = keep.tile([P, B * LIST_COLS], U16, name="offsets")
+        k_pool = [keep.tile([P, T], I32, name="k_pool%d" % o) for o in range(PASSES)]
+        ks_pool = keep.tile([P, T], U8, name="ks_pool")
+        vs_pool = keep.tile([P, T], F32, name="vs_pool")
+        v_pool = [keep.tile([P, T], F32, name="v_pool%d" % h) for h in range(EB)]
+        q_codes = [keep.tile([P, PASSES, NQ], I32, name="q_codes%d" % b, align_bytes=64) for b in range(B)]
+        q_plane = keep.tile([P, NQ], U8, name="q_plane", align_bytes=64)
+        gate_in = keep.tile([P, B * QB, DV], F32, name="gate_in")
+        ident = keep.tile([P, P], F32, name="ident")
+        warm = keep.tile([P, 8], F32, name="warm")
+
+        nc.vector.memset(ks_pool[:].bitcast(I32), 0)
+        nc.vector.memset(vs_pool[:], 0.0)
+        nc.vector.memset(q_plane[:].bitcast(I32), 0)
+        make_identity(nc, ident[:])
+        nc.scalar.activation(warm[:], ident[:, 0:8], ACT.Sigmoid)
+
+        nc.sync.dma_start(offsets[:], offs)
+        nc.sync.dma_start(k_pool[0][:], k_words[0].rearrange("p t r -> p (t r)").bitcast(I32))
+        for quad in range(4):
+            nc.sync.dma_start(
+                ks_pool[32 * quad + K_PLANE0 : 32 * quad + K_PLANE0 + 8, :].bitcast(I32),
+                k_scales[:, 4 * quad : 4 * quad + 4, :].bitcast(I32),
+            )
+        nc.sync.dma_start(vs_pool[0:1, :], vs[0:1, :])
+        nc.sync.dma_start(k_pool[1][:], k_words[1].rearrange("p t r -> p (t r)").bitcast(I32))
+        for quad in range(4):
+            nc.sync.dma_start(
+                q_plane[32 * quad : 32 * quad + 16, :].bitcast(I32),
+                q_scales.rearrange("b o f q -> (b o) f q")[:, 4 * quad : 4 * quad + 4, :].bitcast(I32),
+            )
+        for b in range(B):
+            nc.sync.dma_start(q_codes[b][:], q_words[b].rearrange("o p q r -> p o (q r)").bitcast(I32))
+        for h in range(EB):
+            nc.sync.dma_start(v_pool[h][:], vT[h * P : (h + 1) * P, :])
+        nc.sync.dma_start(
+            gate_in[:].rearrange("p (b j) e -> p b j e", b=B), og.rearrange("b (j p) e -> p b j e", p=P)
+        )
+
+        def seq_list(b):
+            return offsets[:, b * LIST_COLS : (b + 1) * LIST_COLS]
+
+        ks_g = keep.tile([P, B * N], U8, name="ks_g", align_bytes=64)
+        vs_g = keep.tile([P, B * N], F32, name="vs_g")
+        k_g = [keep.tile([P, B * N], U32, name="k_g%d" % o, align_bytes=64) for o in range(PASSES)]
+        nc.vector.tensor_copy(k_g[0][:], k_pool[0][:].bitcast(U32).indirect(offsets[:]))
+        nc.vector.tensor_copy(ks_g[:], ks_pool[:].indirect(offsets[:]))
+        nc.vector.tensor_copy(vs_g[:], vs_pool[:].indirect(offsets[:]))
+        for b in range(B):
+            nc.vector.tensor_copy(k_g[1][:, b * N : (b + 1) * N], k_pool[1][:].bitcast(U32).indirect(seq_list(b)))
+
+        vs_perm = keep.tile([P, B * N], F32, name="vs_perm")
+        vs_t = keep.tile([P, B, 1, 4], F32, name="vs_t")
+        for b in range(B):
+            for u in range(2):
+                nc.scalar.copy(
+                    vs_perm[:, b * N + u * 256 : b * N + (u + 1) * 256].rearrange("p (h g r) -> p h g r", h=2, g=16),
+                    vs_g[:, b * N : (b + 1) * N].rearrange("p (g u r h) -> p u h g r", g=16, u=2, r=8)[:, u],
+                )
+            vs_ps = psum.tile([P, 4, P], F32, name="vs_ps", tag="late")
+            for t in range(4):
+                nc.tensor.transpose(vs_ps[:, t, :], vs_perm[:, b * N + t * P : b * N + (t + 1) * P], ident[:])
+            nc.scalar.copy(vs_t[:, b, 0, :], vs_ps[:, :, 0])
+
+        row_sum = keep.tile([P, B * QB], F32, name="row_sum")
+        w_codes = keep.tile([P, B * QB, P], U32, name="w_codes", align_bytes=64)
+        w_plane = keep.tile([P, B * QB, P], U8, name="w_plane", align_bytes=64)
+        v_codes = keep.tile([P, B, DV], U32, name="v_codes", align_bytes=64)
+        v_plane = keep.tile([P, B, DV], U8, name="v_plane", align_bytes=64)
+
+        pos = [keep.tile([P, QB, N], F32, name="pos%d" % b) for b in range(B)]
+        probs = [keep.tile([P, N], F32, name="prob%d" % blk) for blk in range(B * QB)]
+
+        def weights(b, j):
+            blk = b * QB + j
+            score = psum.tile([P, N], F32, name="score")
+            for o in range(PASSES):
+                nc.tensor.matmul_mx(
+                    out=score[:],
+                    lhsT=q_codes[b][:, o, j * P : (j + 1) * P].bitcast(FP8X4),
+                    lhsT_scale=q_plane[4 * (b * PASSES + o) : P, j * P : (j + 1) * P],
+                    rhs=k_g[o][:, b * N : (b + 1) * N].bitcast(FP8X4),
+                    rhs_scale=ks_g[K_PLANE0 + 4 * o : P, b * N : (b + 1) * N],
+                    start=(o == 0),
+                    stop=(o == PASSES - 1),
+                )
+            pos_out = pos[b][:, j, :].rearrange("p (u g x) -> p u g x", u=2, g=16)
+            score_in = score[:].rearrange("p (g u x) -> p u g x", g=16, u=2)
+            if b == 0:
+                nc.vector.tensor_scalar_max(pos_out, score_in, 0.0)
+            else:
+                nc.scalar.activation(pos_out, score_in, ACT.Relu)
+            prob = probs[blk]
+            nc.scalar.activation(
+                prob[:].rearrange("p (u h m) -> p u h m", u=2, h=2),
+                pos[b][:, j, :].rearrange("p (u m h) -> p u h m", u=2, h=2),
+                ACT.Square,
+                accum_out=row_sum[:, blk : blk + 1],
+            )
+            prob_t = psum.tile([P, 4, P], F32, name="prob_t")
+            for t in range(4):
+                nc.tensor.transpose(prob_t[:, t, :], prob[:, t * P : (t + 1) * P], ident[:])
+            w_bf = work.tile([P, P, 4], BF16, name="w_bf", align_bytes=64)
+            nc.vector.tensor_tensor(
+                w_bf[:], prob_t[:].rearrange("p t q -> p q t"), vs_t[:, b, :, :].to_broadcast([P, P, 4]), ALU.mult
+            )
+            return w_bf
+
+        def quantise_weights(blk, w_bf):
+            nc.vector.quantize_mx(
+                out=w_codes[:, blk, :].bitcast(FP8X4), scales=w_plane[:, blk, :], in_=w_bf[:].rearrange("p q t -> p (q t)")
+            )
+
+        def values(b, h):
+            v_words = probs[h * B + b][:, 0 : N // 2]
+            nc.vector.tensor_copy(
+                v_words.bitcast(BF16).rearrange("p (u g x) -> p g u x", u=2, g=16), v_pool[h][:].indirect(seq_list(b))
+            )
+            v_ps = psum.tile([P, 2, P], F32, name="v_ps")
+            for u in range(2):
+                nc.tensor.transpose(v_ps[:, u, :], v_words[:, u * P : (u + 1) * P], ident[:])
+            v_bf = work.tile([P, P * 4], BF16, name="v_bf", align_bytes=64)
+            nc.scalar.copy(v_bf[:].bitcast(F32).rearrange("p (e u) -> p e u", u=2), v_ps[:].rearrange("p u e -> p e u"))
+            return v_bf
+
+        def quantise_values(b, h, v_bf):
+            nc.vector.quantize_mx(
+                out=v_codes[:, b, h * P : (h + 1) * P].bitcast(FP8X4), scales=v_plane[:, b, h * P : (h + 1) * P], in_=v_bf[:]
+            )
+
+        v_waiting = None
+        for blk in range(B * QB):
+            w_bf = weights(blk // QB, blk % QB)
+            v_bf = values(blk % B, blk // B)
+            quantise_weights(blk, w_bf)
+            if v_waiting is not None:
+                quantise_values(*v_waiting)
+            v_waiting = (blk % B, blk // B, v_bf)
+
+        inv_sum = keep.tile([P, B * QB], F32, name="inv_sum")
+        one_plus = keep.tile([P, B * QB], F32, name="one_plus")
+        nc.gpsimd.tensor_scalar(one_plus[:], row_sum[:], 1.0, 1.0, ALU.add, ALU.mult)
+        nc.vector.reciprocal(inv_sum[:], one_plus[:])
+
+        result = keep.tile([P, B * QB, DV], F32, name="result")
+        for b in range(B):
+            gate = pos[1][:, :, b * DV : (b + 1) * DV]
+            nc.scalar.activation(gate, gate_in[:, b * QB : (b + 1) * QB, :], ACT.Sigmoid)
+            if b == B - 1:
+                quantise_values(*v_waiting)
+            y = psum.tile([P, QB, DV], F32, name="y", tag="late")
+            for j in range(QB):
+                blk = b * QB + j
+                nc.tensor.matmul_mx(
+                    out=y[:, j, :],
+                    lhsT=w_codes[:, blk, :].bitcast(FP8X4),
+                    lhsT_scale=w_plane[:, blk, :],
+                    rhs=v_codes[:, b, :].bitcast(FP8X4),
+                    rhs_scale=v_plane[:, b, :],
+                    start=True,
+                    stop=True,
+                )
+            for j in range(QB):
+                blk = b * QB + j
+                nc.vector.scalar_tensor_tensor(
+                    result[:, blk, :], y[:, j, :], inv_sum[:, blk : blk + 1], gate[:, j, :], ALU.mult, ALU.mult
+                )
+                nc.sync.dma_start(out[b, j * P : (j + 1) * P, :], result[:, blk, :])

@@ -49,14 +49,16 @@ def tile_attend_rel2_gate_pgb2q256n512t2048_kernel(tc, q_words, q_scales, k_word
         nc.scalar.activation(warm[:], ident[:, 0:8], ACT.Sigmoid)
 
         nc.sync.dma_start(offsets[:], offs)
-        nc.sync.dma_start(k_pool[0][:], k_words[0].rearrange("p t r -> p (t r)").bitcast(I32))
         for quad in range(4):
             nc.sync.dma_start(
                 ks_pool[32 * quad + K_PLANE0 : 32 * quad + K_PLANE0 + 8, :].bitcast(I32),
                 k_scales[:, 4 * quad : 4 * quad + 4, :].bitcast(I32),
             )
+        nc.sync.dma_start(v_pool[0][:, 0 : T // 2], vT[0:P, 0 : T // 2])
+        nc.sync.dma_start(v_pool[0][:, T // 2 : T], vT[0:P, T // 2 : T])
         nc.sync.dma_start(vs_pool[0:1, :], vs[0:1, :])
-        nc.sync.dma_start(k_pool[1][:], k_words[1].rearrange("p t r -> p (t r)").bitcast(I32))
+        for o in range(PASSES):
+            nc.sync.dma_start(k_pool[o][:], k_words[o].rearrange("p t r -> p (t r)").bitcast(I32))
         for quad in range(4):
             nc.sync.dma_start(
                 q_plane[32 * quad : 32 * quad + 16, :].bitcast(I32),
@@ -64,8 +66,7 @@ def tile_attend_rel2_gate_pgb2q256n512t2048_kernel(tc, q_words, q_scales, k_word
             )
         for b in range(B):
             nc.sync.dma_start(q_codes[b][:], q_words[b].rearrange("o p q r -> p o (q r)").bitcast(I32))
-        for h in range(EB):
-            nc.sync.dma_start(v_pool[h][:], vT[h * P : (h + 1) * P, :])
+        nc.sync.dma_start(v_pool[1][:], vT[P : 2 * P, :])
         nc.sync.dma_start(
             gate_in[:].rearrange("p (b j) e -> p b j e", b=B), og.rearrange("b (j p) e -> p b j e", p=P)
         )
@@ -76,25 +77,18 @@ def tile_attend_rel2_gate_pgb2q256n512t2048_kernel(tc, q_words, q_scales, k_word
         ks_g = keep.tile([P, B * N], U8, name="ks_g", align_bytes=64)
         vs_g = keep.tile([P, B * N], F32, name="vs_g")
         k_g = [keep.tile([P, B * N], U32, name="k_g%d" % o, align_bytes=64) for o in range(PASSES)]
-        nc.vector.tensor_copy(k_g[0][:], k_pool[0][:].bitcast(U32).indirect(offsets[:]))
         nc.vector.tensor_copy(ks_g[:], ks_pool[:].indirect(offsets[:]))
         nc.vector.tensor_copy(vs_g[:], vs_pool[:].indirect(offsets[:]))
+        nc.vector.tensor_copy(k_g[0][:], k_pool[0][:].bitcast(U32).indirect(offsets[:]))
         for b in range(B):
             nc.vector.tensor_copy(k_g[1][:, b * N : (b + 1) * N], k_pool[1][:].bitcast(U32).indirect(seq_list(b)))
 
-        vs_perm = keep.tile([P, B * N], F32, name="vs_perm")
-        vs_t = keep.tile([P, B, 1, 4], F32, name="vs_t")
-        for b in range(B):
-            for u in range(2):
-                nc.scalar.copy(
-                    vs_perm[:, b * N + u * 256 : b * N + (u + 1) * 256].rearrange("p (h g r) -> p h g r", h=2, g=16),
-                    vs_g[:, b * N : (b + 1) * N].rearrange("p (g u r h) -> p u h g r", g=16, u=2, r=8)[:, u],
-                )
-            vs_ps = psum.tile([P, 4, P], F32, name="vs_ps", tag="late")
-            for t in range(4):
-                nc.tensor.transpose(vs_ps[:, t, :], vs_perm[:, b * N + t * P : b * N + (t + 1) * P], ident[:])
-            nc.scalar.copy(vs_t[:, b, 0, :], vs_ps[:, :, 0])
+        v_pool_bf = keep.tile([P, T], BF16, name="v_pool_bf")
+        for c in range(2):
+            cols = slice(c * T // 2, (c + 1) * T // 2)
+            nc.scalar.copy(v_pool_bf[:, cols], v_pool[0][:, cols])
 
+        vs_t = keep.tile([P, B, 1, 4], F32, name="vs_t")
         row_sum = keep.tile([P, B * QB], F32, name="row_sum")
         w_codes = keep.tile([P, B * QB, P], U32, name="w_codes", align_bytes=64)
         w_plane = keep.tile([P, B * QB, P], U8, name="w_plane", align_bytes=64)
@@ -104,9 +98,10 @@ def tile_attend_rel2_gate_pgb2q256n512t2048_kernel(tc, q_words, q_scales, k_word
         pos = [keep.tile([P, QB, N], F32, name="pos%d" % b) for b in range(B)]
         probs = [keep.tile([P, N], F32, name="prob%d" % blk) for blk in range(B * QB)]
 
-        def weights(b, j):
-            blk = b * QB + j
-            score = psum.tile([P, N], F32, name="score")
+        turned = [psum.tile([P, 4, P], F32, name="turned%d" % i, bufs=1) for i in range(4)]
+
+        def scores(b, j):
+            score = psum.tile([P, N], F32, name="score", tag="mx", bufs=4)
             for o in range(PASSES):
                 nc.tensor.matmul_mx(
                     out=score[:],
@@ -117,25 +112,27 @@ def tile_attend_rel2_gate_pgb2q256n512t2048_kernel(tc, q_words, q_scales, k_word
                     start=(o == 0),
                     stop=(o == PASSES - 1),
                 )
-            pos_out = pos[b][:, j, :].rearrange("p (u g x) -> p u g x", u=2, g=16)
-            score_in = score[:].rearrange("p (g u x) -> p u g x", g=16, u=2)
-            if b == 0:
-                nc.vector.tensor_scalar_max(pos_out, score_in, 0.0)
-            else:
-                nc.scalar.activation(pos_out, score_in, ACT.Relu)
-            prob = probs[blk]
+            return score
+
+        def positive_part(blk):
+            b, j = divmod(blk, QB)
             nc.scalar.activation(
-                prob[:].rearrange("p (u h m) -> p u h m", u=2, h=2),
-                pos[b][:, j, :].rearrange("p (u m h) -> p u h m", u=2, h=2),
-                ACT.Square,
-                accum_out=row_sum[:, blk : blk + 1],
+                pos[b][:, j, :].rearrange("p (t m) -> p t m", t=4),
+                score_banks[blk][:].rearrange("p (m t) -> p t m", t=4),
+                ACT.Relu,
             )
-            prob_t = psum.tile([P, 4, P], F32, name="prob_t")
+
+        def square(blk):
+            b, j = divmod(blk, QB)
+            nc.scalar.activation(probs[blk][:], pos[b][:, j, :], ACT.Square, accum_out=row_sum[:, blk : blk + 1])
+
+        def weights(blk):
+            prob_t = turned[blk]
             for t in range(4):
-                nc.tensor.transpose(prob_t[:, t, :], prob[:, t * P : (t + 1) * P], ident[:])
+                nc.tensor.transpose(prob_t[:, t, :], probs[blk][:, t * P : (t + 1) * P], ident[:])
             w_bf = work.tile([P, P, 4], BF16, name="w_bf", align_bytes=64)
             nc.vector.tensor_tensor(
-                w_bf[:], prob_t[:].rearrange("p t q -> p q t"), vs_t[:, b, :, :].to_broadcast([P, P, 4]), ALU.mult
+                w_bf[:], prob_t[:].rearrange("p t q -> p q t"), vs_t[:, blk // QB, :, :].to_broadcast([P, P, 4]), ALU.mult
             )
             return w_bf
 
@@ -144,31 +141,61 @@ def tile_attend_rel2_gate_pgb2q256n512t2048_kernel(tc, q_words, q_scales, k_word
                 out=w_codes[:, blk, :].bitcast(FP8X4), scales=w_plane[:, blk, :], in_=w_bf[:].rearrange("p q t -> p (q t)")
             )
 
-        def values(b, h):
-            v_words = probs[h * B + b][:, 0 : N // 2]
-            nc.vector.tensor_copy(
-                v_words.bitcast(BF16).rearrange("p (u g x) -> p g u x", u=2, g=16), v_pool[h][:].indirect(seq_list(b))
-            )
-            v_ps = psum.tile([P, 2, P], F32, name="v_ps")
+        v_bf = [keep.tile([P, EB, P * 4], BF16, name="v_bf%d" % b, align_bytes=64) for b in range(B)]
+
+        def gather_values(b, h, v_words):
+            gathered = v_words.bitcast(BF16).rearrange("p (u m h) -> p m u h", u=2, h=2)
+            if h == 0:
+                nc.scalar.activation(gathered, v_pool_bf[:].indirect(seq_list(b)), ACT.Copy)
+            else:
+                nc.vector.tensor_copy(gathered, v_pool[h][:].indirect(seq_list(b)))
+
+        def turn_values(b, h, v_words):
+            v_ps = turned[b + 2 * (1 - h)]
             for u in range(2):
                 nc.tensor.transpose(v_ps[:, u, :], v_words[:, u * P : (u + 1) * P], ident[:])
-            v_bf = work.tile([P, P * 4], BF16, name="v_bf", align_bytes=64)
-            nc.scalar.copy(v_bf[:].bitcast(F32).rearrange("p (e u) -> p e u", u=2), v_ps[:].rearrange("p u e -> p e u"))
-            return v_bf
-
-        def quantise_values(b, h, v_bf):
-            nc.vector.quantize_mx(
-                out=v_codes[:, b, h * P : (h + 1) * P].bitcast(FP8X4), scales=v_plane[:, b, h * P : (h + 1) * P], in_=v_bf[:]
+            nc.scalar.copy(
+                v_bf[b][:, h, :].bitcast(F32).rearrange("p (e u) -> p e u", u=2), v_ps[:, 0:2, :].rearrange("p u e -> p e u")
             )
 
-        v_waiting = None
-        for blk in range(B * QB):
-            w_bf = weights(blk // QB, blk % QB)
-            v_bf = values(blk % B, blk // B)
-            quantise_weights(blk, w_bf)
-            if v_waiting is not None:
-                quantise_values(*v_waiting)
-            v_waiting = (blk % B, blk // B, v_bf)
+        def quantise_values(b):
+            nc.vector.quantize_mx(
+                out=v_codes[:, b, :].bitcast(FP8X4), scales=v_plane[:, b, :], in_=v_bf[b][:].rearrange("p h x -> p (h x)")
+            )
+
+        v_first = keep.tile([P, B, N // 2], F32, name="v_first")
+        v_second = keep.tile([P, B, N // 2], F32, name="v_second")
+        for b in range(B):
+            gather_values(b, 0, v_first[:, b, :])
+            turn_values(b, 0, v_first[:, b, :])
+        for b in range(B):
+            vs_ps = turned[b]
+            for t in range(4):
+                nc.tensor.transpose(vs_ps[:, t, :], vs_g[:, b * N + t : (b + 1) * N : 4], ident[:])
+            nc.scalar.copy(vs_t[:, b, 0, :], vs_ps[:, :, 0])
+        score_banks = [scores(b, j) for b in range(B) for j in range(QB)]
+        positive_part(0)
+        positive_part(1)
+        square(0)
+        positive_part(2)
+        square(1)
+        positive_part(3)
+        square(2)
+        square(3)
+        for b in range(B):
+            gather_values(b, 1, v_second[:, b, :])
+        w0 = weights(0)
+        w1 = weights(1)
+        turn_values(0, 1, v_second[:, 0, :])
+        quantise_weights(0, w0)
+        turn_values(1, 1, v_second[:, 1, :])
+        quantise_weights(1, w1)
+        w2 = weights(2)
+        quantise_values(0)
+        w3 = weights(3)
+        quantise_weights(2, w2)
+        quantise_values(1)
+        quantise_weights(3, w3)
 
         inv_sum = keep.tile([P, B * QB], F32, name="inv_sum")
         one_plus = keep.tile([P, B * QB], F32, name="one_plus")
@@ -179,9 +206,7 @@ def tile_attend_rel2_gate_pgb2q256n512t2048_kernel(tc, q_words, q_scales, k_word
         for b in range(B):
             gate = pos[1][:, :, b * DV : (b + 1) * DV]
             nc.scalar.activation(gate, gate_in[:, b * QB : (b + 1) * QB, :], ACT.Sigmoid)
-            if b == B - 1:
-                quantise_values(*v_waiting)
-            y = psum.tile([P, QB, DV], F32, name="y", tag="late")
+            y = psum.tile([P, QB, DV], F32, name="y", tag="mx", bufs=4)
             for j in range(QB):
                 blk = b * QB + j
                 nc.tensor.matmul_mx(

@@ -64,9 +64,9 @@ def tile_attend_rel2_gate_pgb2q256n512t2048_kernel(tc, q_words, q_scales, k_word
                 q_plane[32 * quad : 32 * quad + 16, :].bitcast(I32),
                 q_scales.rearrange("b o f q -> (b o) f q")[:, 4 * quad : 4 * quad + 4, :].bitcast(I32),
             )
-        for b in range(B):
-            nc.sync.dma_start(q_codes[b][:], q_words[b].rearrange("o p q r -> p o (q r)").bitcast(I32))
+        nc.sync.dma_start(q_codes[0][:], q_words[0].rearrange("o p q r -> p o (q r)").bitcast(I32))
         nc.sync.dma_start(v_pool[1][:], vT[P : 2 * P, :])
+        nc.sync.dma_start(q_codes[1][:], q_words[1].rearrange("o p q r -> p o (q r)").bitcast(I32))
         nc.sync.dma_start(
             gate_in[:].rearrange("p (b j) e -> p b j e", b=B), og.rearrange("b (j p) e -> p b j e", p=P)
         )
@@ -117,14 +117,19 @@ def tile_attend_rel2_gate_pgb2q256n512t2048_kernel(tc, q_words, q_scales, k_word
         def positive_part(blk):
             b, j = divmod(blk, QB)
             nc.scalar.activation(
-                pos[b][:, j, :].rearrange("p (t m) -> p t m", t=4),
-                score_banks[blk][:].rearrange("p (m t) -> p t m", t=4),
+                pos[b][:, j, :].rearrange("p (u g x) -> p u g x", u=2, g=16),
+                score_banks[blk][:].rearrange("p (g u x) -> p u g x", g=16, u=2),
                 ACT.Relu,
             )
 
         def square(blk):
             b, j = divmod(blk, QB)
-            nc.scalar.activation(probs[blk][:], pos[b][:, j, :], ACT.Square, accum_out=row_sum[:, blk : blk + 1])
+            nc.scalar.activation(
+                probs[blk][:].rearrange("p (u h m) -> p u h m", u=2, h=2),
+                pos[b][:, j, :].rearrange("p (u m h) -> p u h m", u=2, h=2),
+                ACT.Square,
+                accum_out=row_sum[:, blk : blk + 1],
+            )
 
         def weights(blk):
             prob_t = turned[blk]
@@ -144,7 +149,7 @@ def tile_attend_rel2_gate_pgb2q256n512t2048_kernel(tc, q_words, q_scales, k_word
         v_bf = [keep.tile([P, EB, P * 4], BF16, name="v_bf%d" % b, align_bytes=64) for b in range(B)]
 
         def gather_values(b, h, v_words):
-            gathered = v_words.bitcast(BF16).rearrange("p (u m h) -> p m u h", u=2, h=2)
+            gathered = v_words.bitcast(BF16).rearrange("p (u g x) -> p g u x", u=2, g=16)
             if h == 0:
                 nc.scalar.activation(gathered, v_pool_bf[:].indirect(seq_list(b)), ACT.Copy)
             else:
@@ -164,14 +169,21 @@ def tile_attend_rel2_gate_pgb2q256n512t2048_kernel(tc, q_words, q_scales, k_word
             )
 
         v_first = keep.tile([P, B, N // 2], F32, name="v_first")
+        vs_perm = keep.tile([P, B, N], F32, name="vs_perm")
         v_second = keep.tile([P, B, N // 2], F32, name="v_second")
         for b in range(B):
             gather_values(b, 0, v_first[:, b, :])
             turn_values(b, 0, v_first[:, b, :])
         for b in range(B):
+            for u in range(2):
+                nc.scalar.copy(
+                    vs_perm[:, b, u * 256 : (u + 1) * 256].rearrange("p (h g r) -> p h g r", h=2, g=16),
+                    vs_g[:, b * N : (b + 1) * N].rearrange("p (g u r h) -> p u h g r", g=16, u=2, r=8)[:, u],
+                )
+        for b in range(B):
             vs_ps = turned[b]
             for t in range(4):
-                nc.tensor.transpose(vs_ps[:, t, :], vs_g[:, b * N + t : (b + 1) * N : 4], ident[:])
+                nc.tensor.transpose(vs_ps[:, t, :], vs_perm[:, b, t * P : (t + 1) * P], ident[:])
             nc.scalar.copy(vs_t[:, b, 0, :], vs_ps[:, :, 0])
         score_banks = [scores(b, j) for b in range(B) for j in range(QB)]
         positive_part(0)

@@ -29,7 +29,7 @@ def tile_attend_rel2_gate_pgb2q256n512t2048_kernel(tc, q_words, q_scales, k_word
     with ExitStack() as ctx:
         keep = ctx.enter_context(tc.tile_pool(name="keep", bufs=1))
         work = ctx.enter_context(tc.tile_pool(name="work", bufs=2))
-        psum = ctx.enter_context(tc.psum_pool(name="psum", bufs=2))
+        psum = ctx.enter_context(tc.psum_pool(name="psum", bufs=1))
 
         offsets = keep.tile([P, B * LIST_COLS], U16, name="offsets")
         k_pool = [keep.tile([P, T], I32, name="k_pool%d" % o) for o in range(PASSES)]
@@ -49,24 +49,24 @@ def tile_attend_rel2_gate_pgb2q256n512t2048_kernel(tc, q_words, q_scales, k_word
         nc.scalar.activation(warm[:], ident[:, 0:8], ACT.Sigmoid)
 
         nc.sync.dma_start(offsets[:], offs)
+        nc.sync.dma_start(v_pool[0][:, 0 : T // 2], vT[0:P, 0 : T // 2])
         for quad in range(4):
             nc.sync.dma_start(
                 ks_pool[32 * quad + K_PLANE0 : 32 * quad + K_PLANE0 + 8, :].bitcast(I32),
                 k_scales[:, 4 * quad : 4 * quad + 4, :].bitcast(I32),
             )
-        nc.sync.dma_start(v_pool[0][:, 0 : T // 2], vT[0:P, 0 : T // 2])
         nc.sync.dma_start(v_pool[0][:, T // 2 : T], vT[0:P, T // 2 : T])
         nc.sync.dma_start(vs_pool[0:1, :], vs[0:1, :])
-        for o in range(PASSES):
-            nc.sync.dma_start(k_pool[o][:], k_words[o].rearrange("p t r -> p (t r)").bitcast(I32))
+        nc.sync.dma_start(k_pool[0][:], k_words[0].rearrange("p t r -> p (t r)").bitcast(I32))
+        nc.sync.dma_start(k_pool[1][:], k_words[1].rearrange("p t r -> p (t r)").bitcast(I32))
         for quad in range(4):
             nc.sync.dma_start(
                 q_plane[32 * quad : 32 * quad + 16, :].bitcast(I32),
                 q_scales.rearrange("b o f q -> (b o) f q")[:, 4 * quad : 4 * quad + 4, :].bitcast(I32),
             )
         nc.sync.dma_start(q_codes[0][:], q_words[0].rearrange("o p q r -> p o (q r)").bitcast(I32))
-        nc.sync.dma_start(v_pool[1][:], vT[P : 2 * P, :])
         nc.sync.dma_start(q_codes[1][:], q_words[1].rearrange("o p q r -> p o (q r)").bitcast(I32))
+        nc.sync.dma_start(v_pool[1][:], vT[P : 2 * P, :])
         nc.sync.dma_start(
             gate_in[:].rearrange("p (b j) e -> p b j e", b=B), og.rearrange("b (j p) e -> p b j e", p=P)
         )
@@ -77,34 +77,28 @@ def tile_attend_rel2_gate_pgb2q256n512t2048_kernel(tc, q_words, q_scales, k_word
         ks_g = keep.tile([P, B * N], U8, name="ks_g", align_bytes=64)
         vs_g = keep.tile([P, B * N], F32, name="vs_g")
         k_g = [keep.tile([P, B * N], U32, name="k_g%d" % o, align_bytes=64) for o in range(PASSES)]
-        nc.vector.tensor_copy(ks_g[:], ks_pool[:].indirect(offsets[:]))
-        nc.vector.tensor_copy(vs_g[:], vs_pool[:].indirect(offsets[:]))
-        nc.vector.tensor_copy(k_g[0][:], k_pool[0][:].bitcast(U32).indirect(offsets[:]))
-        for b in range(B):
-            nc.vector.tensor_copy(k_g[1][:, b * N : (b + 1) * N], k_pool[1][:].bitcast(U32).indirect(seq_list(b)))
+        score_banks = [psum.tile([P, N], F32, name="score%d" % i) for i in range(B * QB)]
+        turned = [psum.tile([P, 4, P], F32, name="turned%d" % i) for i in range(B * QB)]
 
-        v_pool_bf = keep.tile([P, T], BF16, name="v_pool_bf")
-        for c in range(2):
-            cols = slice(c * T // 2, (c + 1) * T // 2)
-            nc.scalar.copy(v_pool_bf[:, cols], v_pool[0][:, cols])
-
+        vs_perm = keep.tile([P, B, N], F32, name="vs_perm")
         vs_t = keep.tile([P, B, 1, 4], F32, name="vs_t")
+
         row_sum = keep.tile([P, B * QB], F32, name="row_sum")
         w_codes = keep.tile([P, B * QB, P], U32, name="w_codes", align_bytes=64)
         w_plane = keep.tile([P, B * QB, P], U8, name="w_plane", align_bytes=64)
         v_codes = keep.tile([P, B, DV], U32, name="v_codes", align_bytes=64)
         v_plane = keep.tile([P, B, DV], U8, name="v_plane", align_bytes=64)
-
         pos = [keep.tile([P, QB, N], F32, name="pos%d" % b) for b in range(B)]
         probs = [keep.tile([P, N], F32, name="prob%d" % blk) for blk in range(B * QB)]
+        w_bf = [keep.tile([P, P, 4], BF16, name="w_bf%d" % blk, align_bytes=64) for blk in range(B * QB)]
+        v_bf = [keep.tile([P, EB, P * 4], BF16, name="v_bf%d" % b, align_bytes=64) for b in range(B)]
+        v_words = keep.tile([P, EB, B, N // 2], F32, name="v_words")
 
-        turned = [psum.tile([P, 4, P], F32, name="turned%d" % i, bufs=1) for i in range(4)]
-
-        def scores(b, j):
-            score = psum.tile([P, N], F32, name="score", tag="mx", bufs=4)
+        def scores(blk):
+            b, j = divmod(blk, QB)
             for o in range(PASSES):
                 nc.tensor.matmul_mx(
-                    out=score[:],
+                    out=score_banks[blk][:],
                     lhsT=q_codes[b][:, o, j * P : (j + 1) * P].bitcast(FP8X4),
                     lhsT_scale=q_plane[4 * (b * PASSES + o) : P, j * P : (j + 1) * P],
                     rhs=k_g[o][:, b * N : (b + 1) * N].bitcast(FP8X4),
@@ -112,15 +106,15 @@ def tile_attend_rel2_gate_pgb2q256n512t2048_kernel(tc, q_words, q_scales, k_word
                     start=(o == 0),
                     stop=(o == PASSES - 1),
                 )
-            return score
 
         def positive_part(blk):
             b, j = divmod(blk, QB)
-            nc.scalar.activation(
-                pos[b][:, j, :].rearrange("p (u g x) -> p u g x", u=2, g=16),
-                score_banks[blk][:].rearrange("p (g u x) -> p u g x", g=16, u=2),
-                ACT.Relu,
-            )
+            kept = pos[b][:, j, :].rearrange("p (u g x) -> p u g x", u=2, g=16)
+            score = score_banks[blk][:].rearrange("p (g u x) -> p u g x", g=16, u=2)
+            if blk in (1, 2,):
+                nc.vector.tensor_scalar_max(kept, score, 0.0)
+            else:
+                nc.scalar.activation(kept, score, ACT.Relu)
 
         def square(blk):
             b, j = divmod(blk, QB)
@@ -132,97 +126,56 @@ def tile_attend_rel2_gate_pgb2q256n512t2048_kernel(tc, q_words, q_scales, k_word
             )
 
         def weights(blk):
-            prob_t = turned[blk]
             for t in range(4):
-                nc.tensor.transpose(prob_t[:, t, :], probs[blk][:, t * P : (t + 1) * P], ident[:])
-            w_bf = work.tile([P, P, 4], BF16, name="w_bf", align_bytes=64)
+                nc.tensor.transpose(turned[blk][:, t, :], probs[blk][:, t * P : (t + 1) * P], ident[:])
             nc.vector.tensor_tensor(
-                w_bf[:], prob_t[:].rearrange("p t q -> p q t"), vs_t[:, blk // QB, :, :].to_broadcast([P, P, 4]), ALU.mult
+                w_bf[blk][:],
+                turned[blk][:].rearrange("p t q -> p q t"),
+                vs_t[:, blk // QB, :, :].to_broadcast([P, P, 4]),
+                ALU.mult,
             )
-            return w_bf
 
-        def quantise_weights(blk, w_bf):
+        def quantise_weights(blk):
             nc.vector.quantize_mx(
-                out=w_codes[:, blk, :].bitcast(FP8X4), scales=w_plane[:, blk, :], in_=w_bf[:].rearrange("p q t -> p (q t)")
+                out=w_codes[:, blk, :].bitcast(FP8X4),
+                scales=w_plane[:, blk, :],
+                in_=w_bf[blk][:].rearrange("p q t -> p (q t)"),
             )
 
-        v_bf = [keep.tile([P, EB, P * 4], BF16, name="v_bf%d" % b, align_bytes=64) for b in range(B)]
+        def gather_values(b, h):
+            gathered = v_words[:, h, b, :].bitcast(BF16).rearrange("p (u g x) -> p g u x", u=2, g=16)
+            nc.vector.tensor_copy(gathered, v_pool[h][:].indirect(seq_list(b)))
 
-        def gather_values(b, h, v_words):
-            gathered = v_words.bitcast(BF16).rearrange("p (u g x) -> p g u x", u=2, g=16)
-            if h == 0:
-                nc.scalar.activation(gathered, v_pool_bf[:].indirect(seq_list(b)), ACT.Copy)
-            else:
-                nc.vector.tensor_copy(gathered, v_pool[h][:].indirect(seq_list(b)))
-
-        def turn_values(b, h, v_words):
-            v_ps = turned[b + 2 * (1 - h)]
+        def turn_values(b, h):
+            bank = turned[b + QB * (1 - h)][:, 0:2, :]
             for u in range(2):
-                nc.tensor.transpose(v_ps[:, u, :], v_words[:, u * P : (u + 1) * P], ident[:])
-            nc.scalar.copy(
-                v_bf[b][:, h, :].bitcast(F32).rearrange("p (e u) -> p e u", u=2), v_ps[:, 0:2, :].rearrange("p u e -> p e u")
-            )
+                nc.tensor.transpose(bank[:, u, :], v_words[:, h, b, u * P : (u + 1) * P], ident[:])
+            nc.scalar.copy(v_bf[b][:, h, :].bitcast(F32).rearrange("p (e u) -> p e u", u=2), bank.rearrange("p u e -> p e u"))
 
         def quantise_values(b):
             nc.vector.quantize_mx(
                 out=v_codes[:, b, :].bitcast(FP8X4), scales=v_plane[:, b, :], in_=v_bf[b][:].rearrange("p h x -> p (h x)")
             )
 
-        v_first = keep.tile([P, B, N // 2], F32, name="v_first")
-        vs_perm = keep.tile([P, B, N], F32, name="vs_perm")
-        v_second = keep.tile([P, B, N // 2], F32, name="v_second")
-        for b in range(B):
-            gather_values(b, 0, v_first[:, b, :])
-            turn_values(b, 0, v_first[:, b, :])
-        for b in range(B):
-            for u in range(2):
-                nc.scalar.copy(
-                    vs_perm[:, b, u * 256 : (u + 1) * 256].rearrange("p (h g r) -> p h g r", h=2, g=16),
-                    vs_g[:, b * N : (b + 1) * N].rearrange("p (g u r h) -> p u h g r", g=16, u=2, r=8)[:, u],
-                )
-        for b in range(B):
-            vs_ps = turned[b]
-            for t in range(4):
-                nc.tensor.transpose(vs_ps[:, t, :], vs_perm[:, b, t * P : (t + 1) * P], ident[:])
-            nc.scalar.copy(vs_t[:, b, 0, :], vs_ps[:, :, 0])
-        score_banks = [scores(b, j) for b in range(B) for j in range(QB)]
-        positive_part(0)
-        positive_part(1)
-        square(0)
-        positive_part(2)
-        square(1)
-        positive_part(3)
-        square(2)
-        square(3)
-        for b in range(B):
-            gather_values(b, 1, v_second[:, b, :])
-        w0 = weights(0)
-        w1 = weights(1)
-        turn_values(0, 1, v_second[:, 0, :])
-        quantise_weights(0, w0)
-        turn_values(1, 1, v_second[:, 1, :])
-        quantise_weights(1, w1)
-        w2 = weights(2)
-        quantise_values(0)
-        w3 = weights(3)
-        quantise_weights(2, w2)
-        quantise_values(1)
-        quantise_weights(3, w3)
-
         inv_sum = keep.tile([P, B * QB], F32, name="inv_sum")
         one_plus = keep.tile([P, B * QB], F32, name="one_plus")
-        nc.gpsimd.tensor_scalar(one_plus[:], row_sum[:], 1.0, 1.0, ALU.add, ALU.mult)
-        nc.vector.reciprocal(inv_sum[:], one_plus[:])
-
         result = keep.tile([P, B * QB, DV], F32, name="result")
-        for b in range(B):
-            gate = pos[1][:, :, b * DV : (b + 1) * DV]
-            nc.scalar.activation(gate, gate_in[:, b * QB : (b + 1) * QB, :], ACT.Sigmoid)
-            y = psum.tile([P, QB, DV], F32, name="y", tag="mx", bufs=4)
+
+        def row_factor():
+            nc.gpsimd.tensor_scalar(one_plus[:], row_sum[:], 1.0, 1.0, ALU.add, ALU.mult)
+            nc.vector.reciprocal(inv_sum[:], one_plus[:])
+
+        def gate_of(b):
+            return pos[1][:, :, b * DV : (b + 1) * DV]
+
+        def sigmoid(b):
+            nc.scalar.activation(gate_of(b), gate_in[:, b * QB : (b + 1) * QB, :], ACT.Sigmoid)
+
+        def product(b):
             for j in range(QB):
                 blk = b * QB + j
                 nc.tensor.matmul_mx(
-                    out=y[:, j, :],
+                    out=score_banks[QB + b][:, j * DV : (j + 1) * DV],
                     lhsT=w_codes[:, blk, :].bitcast(FP8X4),
                     lhsT_scale=w_plane[:, blk, :],
                     rhs=v_codes[:, b, :].bitcast(FP8X4),
@@ -230,9 +183,70 @@ def tile_attend_rel2_gate_pgb2q256n512t2048_kernel(tc, q_words, q_scales, k_word
                     start=True,
                     stop=True,
                 )
+
+        def finish(b):
             for j in range(QB):
                 blk = b * QB + j
                 nc.vector.scalar_tensor_tensor(
-                    result[:, blk, :], y[:, j, :], inv_sum[:, blk : blk + 1], gate[:, j, :], ALU.mult, ALU.mult
+                    result[:, blk, :],
+                    score_banks[QB + b][:, j * DV : (j + 1) * DV],
+                    inv_sum[:, blk : blk + 1],
+                    gate_of(b)[:, j, :],
+                    ALU.mult,
+                    ALU.mult,
                 )
                 nc.sync.dma_start(out[b, j * P : (j + 1) * P, :], result[:, blk, :])
+
+        nc.vector.tensor_copy(ks_g[:], ks_pool[:].indirect(offsets[:]))
+        for b in range(B):
+            nc.vector.tensor_copy(vs_g[:, b * N : (b + 1) * N], vs_pool[:].indirect(seq_list(b)))
+        for b in range(B):
+            gather_values(b, 0)
+        nc.vector.tensor_copy(k_g[0][:], k_pool[0][:].bitcast(U32).indirect(offsets[:]))
+        for b in range(B):
+            nc.vector.tensor_copy(k_g[1][:, b * N : (b + 1) * N], k_pool[1][:].bitcast(U32).indirect(seq_list(b)))
+        for b in range(B):
+            for u in range(2):
+                nc.scalar.copy(
+                    vs_perm[:, b, u * 256 : (u + 1) * 256].rearrange("p (h g r) -> p h g r", h=2, g=16),
+                    vs_g[:, b * N : (b + 1) * N].rearrange("p (g u r h) -> p u h g r", g=16, u=2, r=8)[:, u],
+                )
+            for t in range(4):
+                nc.tensor.transpose(turned[b][:, t, :], vs_perm[:, b, t * P : (t + 1) * P], ident[:])
+        for b in range(B):
+            nc.scalar.copy(vs_t[:, b, 0, :], turned[b][:, :, 0])
+        for b in range(B):
+            turn_values(b, 0)
+        scores(0)
+        scores(1)
+        scores(2)
+        scores(3)
+        positive_part(0)
+        square(0)
+        positive_part(1)
+        positive_part(2)
+        square(1)
+        positive_part(3)
+        square(2)
+        square(3)
+        gather_values(0, 1)
+        gather_values(1, 1)
+        weights(0)
+        weights(1)
+        turn_values(0, 1)
+        quantise_weights(0)
+        turn_values(1, 1)
+        quantise_weights(1)
+        weights(2)
+        quantise_values(0)
+        weights(3)
+        quantise_weights(2)
+        quantise_values(1)
+        quantise_weights(3)
+        row_factor()
+        sigmoid(0)
+        product(0)
+        sigmoid(1)
+        product(1)
+        finish(0)
+        finish(1)

@@ -28,7 +28,6 @@ def tile_attend_rel2_gate_pgb2q256n512t2048_kernel(tc, q_words, q_scales, k_word
     nc = tc.nc
     with ExitStack() as ctx:
         keep = ctx.enter_context(tc.tile_pool(name="keep", bufs=1))
-        work = ctx.enter_context(tc.tile_pool(name="work", bufs=2))
         psum = ctx.enter_context(tc.psum_pool(name="psum", bufs=1))
 
         offsets = keep.tile([P, B * LIST_COLS], U16, name="offsets")
@@ -38,7 +37,7 @@ def tile_attend_rel2_gate_pgb2q256n512t2048_kernel(tc, q_words, q_scales, k_word
         v_pool = [keep.tile([P, T], F32, name="v_pool%d" % h) for h in range(EB)]
         q_codes = [keep.tile([P, PASSES, NQ], I32, name="q_codes%d" % b, align_bytes=64) for b in range(B)]
         q_plane = keep.tile([P, NQ], U8, name="q_plane", align_bytes=64)
-        gate_in = keep.tile([P, B * QB, DV], F32, name="gate_in")
+        gate_in = [keep.tile([P, QB, DV], F32, name="gate_in%d" % b) for b in range(B)]
         ident = keep.tile([P, P], F32, name="ident")
         warm = keep.tile([P, 8], F32, name="warm")
 
@@ -48,28 +47,47 @@ def tile_attend_rel2_gate_pgb2q256n512t2048_kernel(tc, q_words, q_scales, k_word
         make_identity(nc, ident[:])
         nc.scalar.activation(warm[:], ident[:, 0:8], ACT.Sigmoid)
 
+        def load_key_scales():
+            for quad in range(4):
+                nc.sync.dma_start(
+                    ks_pool[32 * quad + K_PLANE0 : 32 * quad + K_PLANE0 + 8, :].bitcast(I32),
+                    k_scales[:, 4 * quad : 4 * quad + 4, :].bitcast(I32),
+                )
+
+        def load_query_scales():
+            for quad in range(4):
+                nc.sync.dma_start(
+                    q_plane[32 * quad : 32 * quad + 16, :].bitcast(I32),
+                    q_scales.rearrange("b o f q -> (b o) f q")[:, 4 * quad : 4 * quad + 4, :].bitcast(I32),
+                )
+
+        def load_keys(o):
+            nc.sync.dma_start(k_pool[o][:], k_words[o].rearrange("p t r -> p (t r)").bitcast(I32))
+
+        def load_queries(b):
+            nc.sync.dma_start(q_codes[b][:], q_words[b].rearrange("o p q r -> p o (q r)").bitcast(I32))
+
+        def load_values(h):
+            nc.sync.dma_start(v_pool[h][:], vT[h * P : (h + 1) * P, :])
+
+        def load_gate(b):
+            nc.sync.dma_start(gate_in[b][:], og[b].rearrange("(j p) e -> p j e", p=P))
+
+        def load_token_scales():
+            nc.sync.dma_start(vs_pool[0:1, :], vs[0:1, :])
+
         nc.sync.dma_start(offsets[:], offs)
-        nc.sync.dma_start(v_pool[0][:, 0 : T // 2], vT[0:P, 0 : T // 2])
-        for quad in range(4):
-            nc.sync.dma_start(
-                ks_pool[32 * quad + K_PLANE0 : 32 * quad + K_PLANE0 + 8, :].bitcast(I32),
-                k_scales[:, 4 * quad : 4 * quad + 4, :].bitcast(I32),
-            )
-        nc.sync.dma_start(v_pool[0][:, T // 2 : T], vT[0:P, T // 2 : T])
-        nc.sync.dma_start(vs_pool[0:1, :], vs[0:1, :])
-        nc.sync.dma_start(k_pool[0][:], k_words[0].rearrange("p t r -> p (t r)").bitcast(I32))
-        nc.sync.dma_start(k_pool[1][:], k_words[1].rearrange("p t r -> p (t r)").bitcast(I32))
-        for quad in range(4):
-            nc.sync.dma_start(
-                q_plane[32 * quad : 32 * quad + 16, :].bitcast(I32),
-                q_scales.rearrange("b o f q -> (b o) f q")[:, 4 * quad : 4 * quad + 4, :].bitcast(I32),
-            )
-        nc.sync.dma_start(q_codes[0][:], q_words[0].rearrange("o p q r -> p o (q r)").bitcast(I32))
-        nc.sync.dma_start(q_codes[1][:], q_words[1].rearrange("o p q r -> p o (q r)").bitcast(I32))
-        nc.sync.dma_start(v_pool[1][:], vT[P : 2 * P, :])
-        nc.sync.dma_start(
-            gate_in[:].rearrange("p (b j) e -> p b j e", b=B), og.rearrange("b (j p) e -> p b j e", p=P)
-        )
+        load_queries(0)
+        load_key_scales()
+        load_token_scales()
+        load_keys(0)
+        load_queries(1)
+        load_query_scales()
+        load_keys(1)
+        load_values(0)
+        load_values(1)
+        load_gate(0)
+        load_gate(1)
 
         def seq_list(b):
             return offsets[:, b * LIST_COLS : (b + 1) * LIST_COLS]
@@ -80,54 +98,64 @@ def tile_attend_rel2_gate_pgb2q256n512t2048_kernel(tc, q_words, q_scales, k_word
         score_banks = [psum.tile([P, N], F32, name="score%d" % i) for i in range(B * QB)]
         turned = [psum.tile([P, 4, P], F32, name="turned%d" % i) for i in range(B * QB)]
 
-        vs_perm = keep.tile([P, B, N], F32, name="vs_perm")
         vs_t = keep.tile([P, B, 1, 4], F32, name="vs_t")
-
         row_sum = keep.tile([P, B * QB], F32, name="row_sum")
-        w_codes = keep.tile([P, B * QB, P], U32, name="w_codes", align_bytes=64)
-        w_plane = keep.tile([P, B * QB, P], U8, name="w_plane", align_bytes=64)
-        v_codes = keep.tile([P, B, DV], U32, name="v_codes", align_bytes=64)
-        v_plane = keep.tile([P, B, DV], U8, name="v_plane", align_bytes=64)
-        pos = [keep.tile([P, QB, N], F32, name="pos%d" % b) for b in range(B)]
+        w_codes = [keep.tile([P, P], U32, name="w_codes%d" % blk, align_bytes=64) for blk in range(B * QB)]
+        w_plane = [keep.tile([P, P], U8, name="w_plane%d" % blk, align_bytes=64) for blk in range(B * QB)]
+        v_codes = [keep.tile([P, DV], U32, name="v_codes%d" % b, align_bytes=64) for b in range(B)]
+        v_plane = [keep.tile([P, DV], U8, name="v_plane%d" % b, align_bytes=64) for b in range(B)]
+        pos = [keep.tile([P, N], F32, name="pos%d" % blk) for blk in range(B * QB)]
         probs = [keep.tile([P, N], F32, name="prob%d" % blk) for blk in range(B * QB)]
         w_bf = [keep.tile([P, P, 4], BF16, name="w_bf%d" % blk, align_bytes=64) for blk in range(B * QB)]
-        v_bf = [keep.tile([P, EB, P * 4], BF16, name="v_bf%d" % b, align_bytes=64) for b in range(B)]
-        v_words = keep.tile([P, EB, B, N // 2], F32, name="v_words")
+        v_bf = [[keep.tile([P, P * 4], BF16, name="v_bf%d%d" % (b, h), align_bytes=64) for h in range(EB)] for b in range(B)]
+        v_g = [[keep.tile([P, N], BF16, name="v_g%d%d" % (b, h)) for h in range(EB)] for b in range(B)]
+        gate = [keep.tile([P, QB, DV], F32, name="gate%d" % b) for b in range(B)]
+        inv_sum = keep.tile([P, B * QB], F32, name="inv_sum")
+        one_plus = keep.tile([P, B * QB], F32, name="one_plus")
+        result = [keep.tile([P, DV], F32, name="result%d" % blk) for blk in range(B * QB)]
 
-        def scores(blk):
-            b, j = divmod(blk, QB)
-            for o in range(PASSES):
-                nc.tensor.matmul_mx(
-                    out=score_banks[blk][:],
-                    lhsT=q_codes[b][:, o, j * P : (j + 1) * P].bitcast(FP8X4),
-                    lhsT_scale=q_plane[4 * (b * PASSES + o) : P, j * P : (j + 1) * P],
-                    rhs=k_g[o][:, b * N : (b + 1) * N].bitcast(FP8X4),
-                    rhs_scale=ks_g[K_PLANE0 + 4 * o : P, b * N : (b + 1) * N],
-                    start=(o == 0),
-                    stop=(o == PASSES - 1),
-                )
+        def gather_key_scales():
+            nc.vector.tensor_copy(ks_g[:], ks_pool[:].indirect(offsets[:]))
 
-        def positive_part(blk):
+        def gather_token_scales():
+            nc.vector.tensor_copy(vs_g[:], vs_pool[:].indirect(offsets[:]))
+
+        def gather_keys(o, b):
+            nc.vector.tensor_copy(k_g[o][:, b * N : (b + 1) * N], k_pool[o][:].bitcast(U32).indirect(seq_list(b)))
+
+        def turn_token_scales(b):
+            for t in range(4):
+                nc.tensor.transpose(turned[b][:, t, :], vs_g[:, b * N + t : (b + 1) * N : 4], ident[:])
+            nc.scalar.copy(vs_t[:, b, 0, :], turned[b][:, :, 0])
+
+        def scores(blk, o):
             b, j = divmod(blk, QB)
-            kept = pos[b][:, j, :].rearrange("p (u g x) -> p u g x", u=2, g=16)
-            score = score_banks[blk][:].rearrange("p (g u x) -> p u g x", g=16, u=2)
-            if blk in (1, 2,):
+            nc.tensor.matmul_mx(
+                out=score_banks[blk][:],
+                lhsT=q_codes[b][:, o, j * P : (j + 1) * P].bitcast(FP8X4),
+                lhsT_scale=q_plane[4 * (b * PASSES + o) : P, j * P : (j + 1) * P],
+                rhs=k_g[o][:, b * N : (b + 1) * N].bitcast(FP8X4),
+                rhs_scale=ks_g[K_PLANE0 + 4 * o : P, b * N : (b + 1) * N],
+                start=(o == 0),
+                stop=(o == PASSES - 1),
+            )
+
+        def positive_part(blk, on_vector):
+            kept = pos[blk][:].rearrange("p (t m) -> p t m", t=4)
+            score = score_banks[blk][:].rearrange("p (m t) -> p t m", t=4)
+            if on_vector:
                 nc.vector.tensor_scalar_max(kept, score, 0.0)
             else:
                 nc.scalar.activation(kept, score, ACT.Relu)
 
         def square(blk):
-            b, j = divmod(blk, QB)
-            nc.scalar.activation(
-                probs[blk][:].rearrange("p (u h m) -> p u h m", u=2, h=2),
-                pos[b][:, j, :].rearrange("p (u m h) -> p u h m", u=2, h=2),
-                ACT.Square,
-                accum_out=row_sum[:, blk : blk + 1],
-            )
+            nc.scalar.activation(probs[blk][:], pos[blk][:], ACT.Square, accum_out=row_sum[:, blk : blk + 1])
 
-        def weights(blk):
+        def turn_probs(blk):
             for t in range(4):
                 nc.tensor.transpose(turned[blk][:, t, :], probs[blk][:, t * P : (t + 1) * P], ident[:])
+
+        def weights(blk):
             nc.vector.tensor_tensor(
                 w_bf[blk][:],
                 turned[blk][:].rearrange("p t q -> p q t"),
@@ -137,116 +165,108 @@ def tile_attend_rel2_gate_pgb2q256n512t2048_kernel(tc, q_words, q_scales, k_word
 
         def quantise_weights(blk):
             nc.vector.quantize_mx(
-                out=w_codes[:, blk, :].bitcast(FP8X4),
-                scales=w_plane[:, blk, :],
-                in_=w_bf[blk][:].rearrange("p q t -> p (q t)"),
+                out=w_codes[blk][:].bitcast(FP8X4), scales=w_plane[blk][:], in_=w_bf[blk][:].rearrange("p q t -> p (q t)")
             )
 
         def gather_values(b, h):
-            gathered = v_words[:, h, b, :].bitcast(BF16).rearrange("p (u g x) -> p g u x", u=2, g=16)
-            nc.vector.tensor_copy(gathered, v_pool[h][:].indirect(seq_list(b)))
+            nc.vector.tensor_copy(v_g[b][h][:], v_pool[h][:].indirect(seq_list(b)))
 
         def turn_values(b, h):
-            bank = turned[b + QB * (1 - h)][:, 0:2, :]
+            bank = score_banks[b][:, h * 256 : (h + 1) * 256].rearrange("p (u e) -> p u e", u=2)
             for u in range(2):
-                nc.tensor.transpose(bank[:, u, :], v_words[:, h, b, u * P : (u + 1) * P], ident[:])
-            nc.scalar.copy(v_bf[b][:, h, :].bitcast(F32).rearrange("p (e u) -> p e u", u=2), bank.rearrange("p u e -> p e u"))
+                nc.tensor.transpose(bank[:, u, :], v_g[b][h][:].bitcast(F32)[:, u : N // 2 : 2], ident[:])
+            nc.scalar.copy(v_bf[b][h][:].bitcast(F32).rearrange("p (e u) -> p e u", u=2), bank.rearrange("p u e -> p e u"))
 
-        def quantise_values(b):
+        def quantise_values(b, h):
             nc.vector.quantize_mx(
-                out=v_codes[:, b, :].bitcast(FP8X4), scales=v_plane[:, b, :], in_=v_bf[b][:].rearrange("p h x -> p (h x)")
+                out=v_codes[b][:, h * P : (h + 1) * P].bitcast(FP8X4), scales=v_plane[b][:, h * P : (h + 1) * P], in_=v_bf[b][h][:]
             )
 
-        inv_sum = keep.tile([P, B * QB], F32, name="inv_sum")
-        one_plus = keep.tile([P, B * QB], F32, name="one_plus")
-        result = keep.tile([P, B * QB, DV], F32, name="result")
-
-        def row_factor():
-            nc.gpsimd.tensor_scalar(one_plus[:], row_sum[:], 1.0, 1.0, ALU.add, ALU.mult)
-            nc.vector.reciprocal(inv_sum[:], one_plus[:])
-
-        def gate_of(b):
-            return pos[1][:, :, b * DV : (b + 1) * DV]
+        def row_factor(b):
+            cols = slice(b * QB, (b + 1) * QB)
+            nc.gpsimd.tensor_scalar(one_plus[:, cols], row_sum[:, cols], 1.0, 1.0, ALU.add, ALU.mult)
+            nc.vector.reciprocal(inv_sum[:, cols], one_plus[:, cols])
 
         def sigmoid(b):
-            nc.scalar.activation(gate_of(b), gate_in[:, b * QB : (b + 1) * QB, :], ACT.Sigmoid)
+            nc.scalar.activation(gate[b][:], gate_in[b][:], ACT.Sigmoid)
 
-        def product(b):
-            for j in range(QB):
-                blk = b * QB + j
-                nc.tensor.matmul_mx(
-                    out=score_banks[QB + b][:, j * DV : (j + 1) * DV],
-                    lhsT=w_codes[:, blk, :].bitcast(FP8X4),
-                    lhsT_scale=w_plane[:, blk, :],
-                    rhs=v_codes[:, b, :].bitcast(FP8X4),
-                    rhs_scale=v_plane[:, b, :],
-                    start=True,
-                    stop=True,
-                )
+        def product(blk):
+            b, j = divmod(blk, QB)
+            nc.tensor.matmul_mx(
+                out=score_banks[QB + b][:, j * DV : (j + 1) * DV],
+                lhsT=w_codes[blk][:].bitcast(FP8X4),
+                lhsT_scale=w_plane[blk][:],
+                rhs=v_codes[b][:].bitcast(FP8X4),
+                rhs_scale=v_plane[b][:],
+                start=True,
+                stop=True,
+            )
 
-        def finish(b):
-            for j in range(QB):
-                blk = b * QB + j
-                nc.vector.scalar_tensor_tensor(
-                    result[:, blk, :],
-                    score_banks[QB + b][:, j * DV : (j + 1) * DV],
-                    inv_sum[:, blk : blk + 1],
-                    gate_of(b)[:, j, :],
-                    ALU.mult,
-                    ALU.mult,
-                )
-                nc.sync.dma_start(out[b, j * P : (j + 1) * P, :], result[:, blk, :])
+        def finish(blk):
+            b, j = divmod(blk, QB)
+            nc.vector.scalar_tensor_tensor(
+                result[blk][:],
+                score_banks[QB + b][:, j * DV : (j + 1) * DV],
+                inv_sum[:, blk : blk + 1],
+                gate[b][:, j, :],
+                ALU.mult,
+                ALU.mult,
+            )
+            nc.sync.dma_start(out[b, j * P : (j + 1) * P, :], result[blk][:])
 
-        nc.vector.tensor_copy(ks_g[:], ks_pool[:].indirect(offsets[:]))
-        for b in range(B):
-            nc.vector.tensor_copy(vs_g[:, b * N : (b + 1) * N], vs_pool[:].indirect(seq_list(b)))
-        for b in range(B):
-            gather_values(b, 0)
-        nc.vector.tensor_copy(k_g[0][:], k_pool[0][:].bitcast(U32).indirect(offsets[:]))
-        for b in range(B):
-            nc.vector.tensor_copy(k_g[1][:, b * N : (b + 1) * N], k_pool[1][:].bitcast(U32).indirect(seq_list(b)))
-        for b in range(B):
-            for u in range(2):
-                nc.scalar.copy(
-                    vs_perm[:, b, u * 256 : (u + 1) * 256].rearrange("p (h g r) -> p h g r", h=2, g=16),
-                    vs_g[:, b * N : (b + 1) * N].rearrange("p (g u r h) -> p u h g r", g=16, u=2, r=8)[:, u],
-                )
-            for t in range(4):
-                nc.tensor.transpose(turned[b][:, t, :], vs_perm[:, b, t * P : (t + 1) * P], ident[:])
-        for b in range(B):
-            nc.scalar.copy(vs_t[:, b, 0, :], turned[b][:, :, 0])
-        for b in range(B):
-            turn_values(b, 0)
-        scores(0)
-        scores(1)
-        scores(2)
-        scores(3)
-        positive_part(0)
+        gather_key_scales()
+        gather_token_scales()
+        gather_keys(0, 0)
+        gather_keys(0, 1)
+        turn_token_scales(0)
+        turn_token_scales(1)
+        gather_keys(1, 0)
+        gather_keys(1, 1)
+        for blk in range(B * QB):
+            scores(blk, 0)
+        for blk in range(B * QB):
+            scores(blk, 1)
+        positive_part(0, False)
         square(0)
-        positive_part(1)
-        positive_part(2)
+        positive_part(1, True)
         square(1)
-        positive_part(3)
+        positive_part(2, False)
         square(2)
+        positive_part(3, False)
         square(3)
-        gather_values(0, 1)
-        gather_values(1, 1)
+        gather_values(0, 0)
+        gather_values(1, 0)
+        turn_probs(0)
+        turn_probs(1)
         weights(0)
         weights(1)
-        turn_values(0, 1)
+        turn_values(0, 0)
+        turn_values(1, 0)
         quantise_weights(0)
-        turn_values(1, 1)
         quantise_weights(1)
-        weights(2)
-        quantise_values(0)
-        weights(3)
-        quantise_weights(2)
-        quantise_values(1)
-        quantise_weights(3)
-        row_factor()
+        gather_values(0, 1)
+        gather_values(1, 1)
+        turn_probs(2)
+        turn_probs(3)
+        turn_values(0, 1)
+        turn_values(1, 1)
+        quantise_values(0, 0)
+        quantise_values(1, 0)
+        quantise_values(0, 1)
+        row_factor(0)
         sigmoid(0)
         product(0)
-        sigmoid(1)
         product(1)
+        weights(2)
+        weights(3)
         finish(0)
+        quantise_weights(2)
+        quantise_values(1, 1)
         finish(1)
+        quantise_weights(3)
+        row_factor(1)
+        sigmoid(1)
+        product(2)
+        product(3)
+        finish(2)
+        finish(3)

@@ -28,21 +28,22 @@ def tile_attend_rel2_gate_pgb2q256n512t2048_kernel(tc, q_words, q_scales, k_word
     nc = tc.nc
     with ExitStack() as ctx:
         keep = ctx.enter_context(tc.tile_pool(name="keep", bufs=1))
+        shared = ctx.enter_context(tc.tile_pool(name="shared", bufs=1))
         psum = ctx.enter_context(tc.psum_pool(name="psum", bufs=1))
 
         offsets = keep.tile([P, B * LIST_COLS], U16, name="offsets")
         k_pool = [keep.tile([P, T], I32, name="k_pool%d" % o) for o in range(PASSES)]
         ks_pool = keep.tile([P, T], U8, name="ks_pool")
         vs_pool = keep.tile([P, T], F32, name="vs_pool")
-        v_pool = [keep.tile([P, T], F32, name="v_pool%d" % h) for h in range(EB)]
+        v_pool = [shared.tile([P, T], F32, name="v_pool%d" % h, offset=h * T * 4, align_bytes=64) for h in range(EB)]
         q_codes = [keep.tile([P, PASSES, NQ], I32, name="q_codes%d" % b, align_bytes=64) for b in range(B)]
         q_plane = keep.tile([P, NQ], U8, name="q_plane", align_bytes=64)
         gate_in = [keep.tile([P, QB, DV], F32, name="gate_in%d" % b) for b in range(B)]
         ident = keep.tile([P, P], F32, name="ident")
         warm = keep.tile([P, 8], F32, name="warm")
 
-        nc.vector.memset(ks_pool[:].bitcast(I32), 0)
-        nc.vector.memset(vs_pool[:], 0.0)
+        nc.gpsimd.memset(ks_pool[:].bitcast(I32), 0)
+        nc.vector.memset(vs_pool[0 : P - 1, :], 0.0)
         nc.vector.memset(q_plane[:].bitcast(I32), 0)
         make_identity(nc, ident[:])
         nc.scalar.activation(warm[:], ident[:, 0:8], ACT.Sigmoid)
@@ -74,16 +75,16 @@ def tile_attend_rel2_gate_pgb2q256n512t2048_kernel(tc, q_words, q_scales, k_word
             nc.sync.dma_start(gate_in[b][:], og[b].rearrange("(j p) e -> p j e", p=P))
 
         def load_token_scales():
-            nc.sync.dma_start(vs_pool[0:1, :], vs[0:1, :])
+            nc.sync.dma_start(vs_pool[P - 1 : P, :], vs[0:1, :])
 
         nc.sync.dma_start(offsets[:], offs)
-        load_queries(0)
-        load_key_scales()
         load_token_scales()
         load_keys(0)
-        load_queries(1)
-        load_query_scales()
+        load_key_scales()
         load_keys(1)
+        load_query_scales()
+        load_queries(0)
+        load_queries(1)
         load_values(0)
         load_values(1)
         load_gate(0)
@@ -106,7 +107,10 @@ def tile_attend_rel2_gate_pgb2q256n512t2048_kernel(tc, q_words, q_scales, k_word
         v_plane = [keep.tile([P, DV], U8, name="v_plane%d" % b, align_bytes=64) for b in range(B)]
         pos = [keep.tile([P, N], F32, name="pos%d" % blk) for blk in range(B * QB)]
         probs = [keep.tile([P, N], F32, name="prob%d" % blk) for blk in range(B * QB)]
-        w_bf = [keep.tile([P, P, 4], BF16, name="w_bf%d" % blk, align_bytes=64) for blk in range(B * QB)]
+        w_bf = [
+            shared.tile([P, P, 4], BF16, name="w_bf%d" % blk, offset=(blk // QB) * T * 4 + (blk % QB) * N * 2, align_bytes=64)
+            for blk in range(B * QB)
+        ]
         v_bf = [[keep.tile([P, P * 4], BF16, name="v_bf%d%d" % (b, h), align_bytes=64) for h in range(EB)] for b in range(B)]
         v_g = [[keep.tile([P, N], BF16, name="v_g%d%d" % (b, h)) for h in range(EB)] for b in range(B)]
         gate = [keep.tile([P, QB, DV], F32, name="gate%d" % b) for b in range(B)]
@@ -126,7 +130,7 @@ def tile_attend_rel2_gate_pgb2q256n512t2048_kernel(tc, q_words, q_scales, k_word
         def turn_token_scales(b):
             for t in range(4):
                 nc.tensor.transpose(turned[b][:, t, :], vs_g[:, b * N + t : (b + 1) * N : 4], ident[:])
-            nc.scalar.copy(vs_t[:, b, 0, :], turned[b][:, :, 0])
+            nc.scalar.copy(vs_t[:, b, 0, :], turned[b][:, :, P - 1])
 
         def scores(blk, o):
             b, j = divmod(blk, QB)
@@ -172,7 +176,7 @@ def tile_attend_rel2_gate_pgb2q256n512t2048_kernel(tc, q_words, q_scales, k_word
             nc.vector.tensor_copy(v_g[b][h][:], v_pool[h][:].indirect(seq_list(b)))
 
         def turn_values(b, h):
-            bank = score_banks[b][:, h * 256 : (h + 1) * 256].rearrange("p (u e) -> p u e", u=2)
+            bank = score_banks[QB + b][:, h * 256 : (h + 1) * 256].rearrange("p (u e) -> p u e", u=2)
             for u in range(2):
                 nc.tensor.transpose(bank[:, u, :], v_g[b][h][:].bitcast(F32)[:, u : N // 2 : 2], ident[:])
             nc.scalar.copy(v_bf[b][h][:].bitcast(F32).rearrange("p (e u) -> p e u", u=2), bank.rearrange("p u e -> p e u"))
@@ -193,7 +197,7 @@ def tile_attend_rel2_gate_pgb2q256n512t2048_kernel(tc, q_words, q_scales, k_word
         def product(blk):
             b, j = divmod(blk, QB)
             nc.tensor.matmul_mx(
-                out=score_banks[QB + b][:, j * DV : (j + 1) * DV],
+                out=score_banks[b][:, j * DV : (j + 1) * DV],
                 lhsT=w_codes[blk][:].bitcast(FP8X4),
                 lhsT_scale=w_plane[blk][:],
                 rhs=v_codes[b][:].bitcast(FP8X4),
@@ -206,7 +210,7 @@ def tile_attend_rel2_gate_pgb2q256n512t2048_kernel(tc, q_words, q_scales, k_word
             b, j = divmod(blk, QB)
             nc.vector.scalar_tensor_tensor(
                 result[blk][:],
-                score_banks[QB + b][:, j * DV : (j + 1) * DV],
+                score_banks[b][:, j * DV : (j + 1) * DV],
                 inv_sum[:, blk : blk + 1],
                 gate[b][:, j, :],
                 ALU.mult,
@@ -214,59 +218,62 @@ def tile_attend_rel2_gate_pgb2q256n512t2048_kernel(tc, q_words, q_scales, k_word
             )
             nc.sync.dma_start(out[b, j * P : (j + 1) * P, :], result[blk][:])
 
-        gather_key_scales()
         gather_token_scales()
-        gather_keys(0, 0)
-        gather_keys(0, 1)
+        nc.vector.tensor_copy(k_g[0][:], k_pool[0][:].bitcast(U32).indirect(offsets[:]))
+        gather_key_scales()
         turn_token_scales(0)
         turn_token_scales(1)
         gather_keys(1, 0)
         gather_keys(1, 1)
-        for blk in range(B * QB):
-            scores(blk, 0)
-        for blk in range(B * QB):
-            scores(blk, 1)
-        positive_part(0, False)
-        square(0)
-        positive_part(1, True)
-        square(1)
-        positive_part(2, False)
-        square(2)
-        positive_part(3, False)
-        square(3)
+        scores(0, 0)
+        scores(1, 0)
+        scores(0, 1)
+        scores(1, 1)
+        scores(2, 0)
+        scores(3, 0)
+        scores(2, 1)
+        scores(3, 1)
         gather_values(0, 0)
         gather_values(1, 0)
+        positive_part(0, False)
+        square(0)
+        positive_part(1, False)
+        square(1)
         turn_probs(0)
         turn_probs(1)
+        positive_part(2, False)
+        square(2)
+        turn_values(0, 0)
+        turn_probs(2)
+        positive_part(3, False)
+        square(3)
+        turn_probs(3)
+        turn_values(1, 0)
         weights(0)
         weights(1)
-        turn_values(0, 0)
-        turn_values(1, 0)
-        quantise_weights(0)
-        quantise_weights(1)
         gather_values(0, 1)
         gather_values(1, 1)
-        turn_probs(2)
-        turn_probs(3)
         turn_values(0, 1)
         turn_values(1, 1)
+        row_factor(0)
+        row_factor(1)
+        sigmoid(0)
+        sigmoid(1)
+        quantise_weights(0)
+        quantise_weights(1)
         quantise_values(0, 0)
         quantise_values(1, 0)
+        weights(2)
         quantise_values(0, 1)
-        row_factor(0)
-        sigmoid(0)
+        weights(3)
         product(0)
         product(1)
-        weights(2)
-        weights(3)
-        finish(0)
         quantise_weights(2)
         quantise_values(1, 1)
-        finish(1)
         quantise_weights(3)
-        row_factor(1)
-        sigmoid(1)
         product(2)
         product(3)
+        finish(0)
+        finish(1)
         finish(2)
         finish(3)

@@ -33,7 +33,7 @@ def tile_attend_rel2_gate_pgb2q256n512t2048_kernel(tc, q_words, q_scales, k_word
 
         offsets = keep.tile([P, B * LIST_COLS], U16, name="offsets")
         k_pool = [keep.tile([P, T], I32, name="k_pool%d" % o) for o in range(PASSES)]
-        ks_pool = keep.tile([P, T], U8, name="ks_pool")
+        ks_pool = shared.tile([P, T], U8, name="ks_pool", offset=EB * T * 4, align_bytes=64)
         vs_pool = keep.tile([P, T], F32, name="vs_pool")
         v_pool = [shared.tile([P, T], F32, name="v_pool%d" % h, offset=h * T * 4, align_bytes=64) for h in range(EB)]
         q_codes = [keep.tile([P, PASSES, NQ], I32, name="q_codes%d" % b, align_bytes=64) for b in range(B)]
@@ -43,14 +43,14 @@ def tile_attend_rel2_gate_pgb2q256n512t2048_kernel(tc, q_words, q_scales, k_word
         warm = keep.tile([P, 8], F32, name="warm")
 
         nc.gpsimd.memset(ks_pool[:].bitcast(I32), 0)
-        nc.vector.memset(vs_pool[0 : P - 1, :], 0.0)
         nc.vector.memset(q_plane[:].bitcast(I32), 0)
-        make_identity(nc, ident[:])
-        nc.scalar.activation(warm[:], ident[:, 0:8], ACT.Sigmoid)
+        nc.vector.memset(vs_pool[0 : P - 1, 0 : T // 2 - 1], 0.0)
+        nc.vector.memset(vs_pool[0 : P - 1, T // 2 - 1 : T // 2], 0.0)
+        nc.vector.memset(vs_pool[0 : P - 1, T // 2 : T], 0.0)
 
-        def load_key_scales():
-            for quad in range(4):
-                nc.sync.dma_start(
+        def load_key_scales(queue, quads):
+            for quad in quads:
+                queue.dma_start(
                     ks_pool[32 * quad + K_PLANE0 : 32 * quad + K_PLANE0 + 8, :].bitcast(I32),
                     k_scales[:, 4 * quad : 4 * quad + 4, :].bitcast(I32),
                 )
@@ -77,13 +77,16 @@ def tile_attend_rel2_gate_pgb2q256n512t2048_kernel(tc, q_words, q_scales, k_word
         def load_token_scales():
             nc.sync.dma_start(vs_pool[P - 1 : P, :], vs[0:1, :])
 
+        load_key_scales(nc.gpsimd, range(2, 4))
+        make_identity(nc, ident[:])
+        nc.scalar.activation(warm[:], ident[:, 0:8], ACT.Sigmoid)
         nc.sync.dma_start(offsets[:], offs)
         load_token_scales()
         load_keys(0)
-        load_key_scales()
-        load_keys(1)
+        load_key_scales(nc.sync, range(2))
         load_query_scales()
         load_queries(0)
+        load_keys(1)
         load_queries(1)
         load_values(0)
         load_values(1)
@@ -112,14 +115,20 @@ def tile_attend_rel2_gate_pgb2q256n512t2048_kernel(tc, q_words, q_scales, k_word
             for blk in range(B * QB)
         ]
         v_bf = [[keep.tile([P, P * 4], BF16, name="v_bf%d%d" % (b, h), align_bytes=64) for h in range(EB)] for b in range(B)]
-        v_g = [[keep.tile([P, N], BF16, name="v_g%d%d" % (b, h)) for h in range(EB)] for b in range(B)]
+        v_g = [
+            [
+                shared.tile([P, N], BF16, name="v_g%d%d" % (b, h), offset=EB * T * 4 + (h * B + b) * N * 2, align_bytes=64)
+                for h in range(EB)
+            ]
+            for b in range(B)
+        ]
         gate = [keep.tile([P, QB, DV], F32, name="gate%d" % b) for b in range(B)]
         inv_sum = keep.tile([P, B * QB], F32, name="inv_sum")
         one_plus = keep.tile([P, B * QB], F32, name="one_plus")
         result = [keep.tile([P, DV], F32, name="result%d" % blk) for blk in range(B * QB)]
 
-        def gather_key_scales():
-            nc.vector.tensor_copy(ks_g[:], ks_pool[:].indirect(offsets[:]))
+        def gather_key_scales(b):
+            nc.vector.tensor_copy(ks_g[:, b * N : (b + 1) * N], ks_pool[:].indirect(seq_list(b)))
 
         def gather_token_scales():
             nc.vector.tensor_copy(vs_g[:], vs_pool[:].indirect(offsets[:]))
@@ -128,9 +137,10 @@ def tile_attend_rel2_gate_pgb2q256n512t2048_kernel(tc, q_words, q_scales, k_word
             nc.vector.tensor_copy(k_g[o][:, b * N : (b + 1) * N], k_pool[o][:].bitcast(U32).indirect(seq_list(b)))
 
         def turn_token_scales(b):
+            bank = score_banks[b][:].rearrange("p (t r) -> p t r", t=4)
             for t in range(4):
-                nc.tensor.transpose(turned[b][:, t, :], vs_g[:, b * N + t : (b + 1) * N : 4], ident[:])
-            nc.scalar.copy(vs_t[:, b, 0, :], turned[b][:, :, P - 1])
+                nc.tensor.transpose(bank[:, t, :], vs_g[:, b * N + t : (b + 1) * N : 4], ident[:])
+            nc.scalar.copy(vs_t[:, b, 0, :], bank[:, :, P - 1])
 
         def scores(blk, o):
             b, j = divmod(blk, QB)
@@ -220,7 +230,8 @@ def tile_attend_rel2_gate_pgb2q256n512t2048_kernel(tc, q_words, q_scales, k_word
 
         gather_token_scales()
         nc.vector.tensor_copy(k_g[0][:], k_pool[0][:].bitcast(U32).indirect(offsets[:]))
-        gather_key_scales()
+        gather_key_scales(0)
+        gather_key_scales(1)
         turn_token_scales(0)
         turn_token_scales(1)
         gather_keys(1, 0)
@@ -230,23 +241,23 @@ def tile_attend_rel2_gate_pgb2q256n512t2048_kernel(tc, q_words, q_scales, k_word
         scores(0, 1)
         scores(1, 1)
         scores(2, 0)
-        scores(3, 0)
         scores(2, 1)
+        scores(3, 0)
         scores(3, 1)
+        positive_part(0, False)
+        positive_part(1, True)
         gather_values(0, 0)
         gather_values(1, 0)
-        positive_part(0, False)
         square(0)
-        positive_part(1, False)
+        positive_part(2, False)
         square(1)
         turn_probs(0)
         turn_probs(1)
-        positive_part(2, False)
-        square(2)
-        turn_values(0, 0)
-        turn_probs(2)
         positive_part(3, False)
+        square(2)
         square(3)
+        turn_probs(2)
+        turn_values(0, 0)
         turn_probs(3)
         turn_values(1, 0)
         weights(0)

@@ -19,9 +19,20 @@ ALU = mybir.AluOpType
 P = 128
 PASSES = D // 512
 QB = NQ // P
+BLOCKS = B * QB
 EB = DV // P
 LIST_COLS = N // 16
 K_PLANE0 = 8
+
+V_POOL_BYTES = T * 4
+ROW_BF16 = N * 2
+ROW_F32 = N * 4
+KS_AT = EB * V_POOL_BYTES
+GATE_AT = 3 * V_POOL_BYTES
+POS_AT = 4 * V_POOL_BYTES
+W_CODES_AT = V_POOL_BYTES + QB * ROW_BF16
+V_CODES_AT = W_CODES_AT + BLOCKS * P * 4
+INV_SUM_AT = V_CODES_AT + B * DV * 4
 
 
 def tile_attend_rel2_gate_pgb2q256n512t2048_kernel(tc, q_words, q_scales, k_words, k_scales, vT, vs, og, offs, out):
@@ -31,34 +42,37 @@ def tile_attend_rel2_gate_pgb2q256n512t2048_kernel(tc, q_words, q_scales, k_word
         shared = ctx.enter_context(tc.tile_pool(name="shared", bufs=1))
         psum = ctx.enter_context(tc.psum_pool(name="psum", bufs=1))
 
+        def placed(shape, dtype, name, at):
+            return shared.tile(shape, dtype, name=name, offset=at, align_bytes=64)
+
         offsets = keep.tile([P, B * LIST_COLS], U16, name="offsets")
         k_pool = [keep.tile([P, T], I32, name="k_pool%d" % o) for o in range(PASSES)]
-        ks_pool = shared.tile([P, T], U8, name="ks_pool", offset=EB * T * 4, align_bytes=64)
+        ks_pool = placed([P, T], U8, "ks_pool", KS_AT)
         vs_pool = keep.tile([P, T], F32, name="vs_pool")
-        v_pool = [shared.tile([P, T], F32, name="v_pool%d" % h, offset=h * T * 4, align_bytes=64) for h in range(EB)]
+        v_pool = [placed([P, T], F32, "v_pool%d" % h, h * V_POOL_BYTES) for h in range(EB)]
         q_codes = [keep.tile([P, PASSES, NQ], I32, name="q_codes%d" % b, align_bytes=64) for b in range(B)]
         q_plane = keep.tile([P, NQ], U8, name="q_plane", align_bytes=64)
-        gate_in = [keep.tile([P, QB, DV], F32, name="gate_in%d" % b) for b in range(B)]
+        gate_in = [placed([P, QB, DV], F32, "gate_in%d" % b, GATE_AT + b * ROW_F32) for b in range(B)]
         ident = keep.tile([P, P], F32, name="ident")
         warm = keep.tile([P, 8], F32, name="warm")
 
         nc.gpsimd.memset(ks_pool[:].bitcast(I32), 0)
-        nc.vector.memset(q_plane[:].bitcast(I32), 0)
-        nc.vector.memset(vs_pool[0 : P - 1, 0 : T // 2 - 1], 0.0)
-        nc.vector.memset(vs_pool[0 : P - 1, T // 2 - 1 : T // 2], 0.0)
-        nc.vector.memset(vs_pool[0 : P - 1, T // 2 : T], 0.0)
+        nc.gpsimd.memset(q_plane[:].bitcast(I32), 0)
+        nc.vector.memset(vs_pool[0 : P - 1, :], 0.0)
+        make_identity(nc, ident[:])
+        nc.scalar.activation(warm[:], ident[:, 0:8], ACT.Sigmoid)
 
-        def load_key_scales(queue, quads):
-            for quad in quads:
-                queue.dma_start(
-                    ks_pool[32 * quad + K_PLANE0 : 32 * quad + K_PLANE0 + 8, :].bitcast(I32),
+        def load_key_scales():
+            for quad in range(4):
+                nc.sync.dma_start(
+                    ks_pool[32 * quad + K_PLANE0 : 32 * quad + K_PLANE0 + 4 * PASSES, :].bitcast(I32),
                     k_scales[:, 4 * quad : 4 * quad + 4, :].bitcast(I32),
                 )
 
         def load_query_scales():
             for quad in range(4):
                 nc.sync.dma_start(
-                    q_plane[32 * quad : 32 * quad + 16, :].bitcast(I32),
+                    q_plane[32 * quad : 32 * quad + 4 * B * PASSES, :].bitcast(I32),
                     q_scales.rearrange("b o f q -> (b o) f q")[:, 4 * quad : 4 * quad + 4, :].bitcast(I32),
                 )
 
@@ -68,30 +82,18 @@ def tile_attend_rel2_gate_pgb2q256n512t2048_kernel(tc, q_words, q_scales, k_word
         def load_queries(b):
             nc.sync.dma_start(q_codes[b][:], q_words[b].rearrange("o p q r -> p o (q r)").bitcast(I32))
 
-        def load_values(h):
-            nc.sync.dma_start(v_pool[h][:], vT[h * P : (h + 1) * P, :])
-
-        def load_gate(b):
-            nc.sync.dma_start(gate_in[b][:], og[b].rearrange("(j p) e -> p j e", p=P))
-
-        def load_token_scales():
-            nc.sync.dma_start(vs_pool[P - 1 : P, :], vs[0:1, :])
-
-        load_key_scales(nc.gpsimd, range(2, 4))
-        make_identity(nc, ident[:])
-        nc.scalar.activation(warm[:], ident[:, 0:8], ACT.Sigmoid)
         nc.sync.dma_start(offsets[:], offs)
-        load_token_scales()
-        load_keys(0)
-        load_key_scales(nc.sync, range(2))
-        load_query_scales()
+        nc.sync.dma_start(vs_pool[P - 1 : P, :], vs[0:1, :])
         load_queries(0)
+        load_key_scales()
+        load_keys(0)
+        load_query_scales()
         load_keys(1)
         load_queries(1)
-        load_values(0)
-        load_values(1)
-        load_gate(0)
-        load_gate(1)
+        for h in range(EB):
+            nc.sync.dma_start(v_pool[h][:], vT[h * P : (h + 1) * P, :])
+        for b in range(B):
+            nc.sync.dma_start(gate_in[b][:], og[b].rearrange("(j p) e -> p j e", p=P))
 
         def seq_list(b):
             return offsets[:, b * LIST_COLS : (b + 1) * LIST_COLS]
@@ -99,39 +101,36 @@ def tile_attend_rel2_gate_pgb2q256n512t2048_kernel(tc, q_words, q_scales, k_word
         ks_g = keep.tile([P, B * N], U8, name="ks_g", align_bytes=64)
         vs_g = keep.tile([P, B * N], F32, name="vs_g")
         k_g = [keep.tile([P, B * N], U32, name="k_g%d" % o, align_bytes=64) for o in range(PASSES)]
-        score_banks = [psum.tile([P, N], F32, name="score%d" % i) for i in range(B * QB)]
-        turned = [psum.tile([P, 4, P], F32, name="turned%d" % i) for i in range(B * QB)]
+        score_banks = [psum.tile([P, N], F32, name="score%d" % blk) for blk in range(BLOCKS)]
+        turned = [psum.tile([P, 4, P], F32, name="turned%d" % blk) for blk in range(BLOCKS)]
 
         vs_t = keep.tile([P, B, 1, 4], F32, name="vs_t")
-        row_sum = keep.tile([P, B * QB], F32, name="row_sum")
-        w_codes = [keep.tile([P, P], U32, name="w_codes%d" % blk, align_bytes=64) for blk in range(B * QB)]
-        w_plane = [keep.tile([P, P], U8, name="w_plane%d" % blk, align_bytes=64) for blk in range(B * QB)]
-        v_codes = [keep.tile([P, DV], U32, name="v_codes%d" % b, align_bytes=64) for b in range(B)]
+        row_sum = keep.tile([P, BLOCKS], F32, name="row_sum")
+        w_codes = [placed([P, P], U32, "w_codes%d" % blk, W_CODES_AT + blk * P * 4) for blk in range(BLOCKS)]
+        w_plane = [keep.tile([P, P], U8, name="w_plane%d" % blk, align_bytes=64) for blk in range(BLOCKS)]
+        v_codes = [placed([P, DV], U32, "v_codes%d" % b, V_CODES_AT + b * DV * 4) for b in range(B)]
         v_plane = [keep.tile([P, DV], U8, name="v_plane%d" % b, align_bytes=64) for b in range(B)]
-        pos = [keep.tile([P, N], F32, name="pos%d" % blk) for blk in range(B * QB)]
-        probs = [keep.tile([P, N], F32, name="prob%d" % blk) for blk in range(B * QB)]
+        pos = [placed([P, N], F32, "pos%d" % blk, POS_AT + blk * ROW_F32) for blk in range(BLOCKS)]
+        probs = [keep.tile([P, N], F32, name="prob%d" % blk) for blk in range(BLOCKS)]
         w_bf = [
-            shared.tile([P, P, 4], BF16, name="w_bf%d" % blk, offset=(blk // QB) * T * 4 + (blk % QB) * N * 2, align_bytes=64)
-            for blk in range(B * QB)
+            placed([P, P, 4], BF16, "w_bf%d" % blk, (blk // QB) * V_POOL_BYTES + (blk % QB) * ROW_BF16)
+            for blk in range(BLOCKS)
         ]
-        v_bf = [[keep.tile([P, P * 4], BF16, name="v_bf%d%d" % (b, h), align_bytes=64) for h in range(EB)] for b in range(B)]
-        v_g = [
+        v_bf = [
             [
-                shared.tile([P, N], BF16, name="v_g%d%d" % (b, h), offset=EB * T * 4 + (h * B + b) * N * 2, align_bytes=64)
-                for h in range(EB)
+                placed([P, N], BF16, "v_bf%d0" % b, POS_AT + (BLOCKS - 1) * ROW_F32 + b * ROW_BF16),
+                placed([P, N], BF16, "v_bf%d1" % b, GATE_AT + b * ROW_F32),
             ]
             for b in range(B)
         ]
+        v_g = [
+            [placed([P, N], BF16, "v_g%d%d" % (b, h), KS_AT + (h * B + b) * ROW_BF16) for h in range(EB)]
+            for b in range(B)
+        ]
         gate = [keep.tile([P, QB, DV], F32, name="gate%d" % b) for b in range(B)]
-        inv_sum = keep.tile([P, B * QB], F32, name="inv_sum")
-        one_plus = keep.tile([P, B * QB], F32, name="one_plus")
-        result = [keep.tile([P, DV], F32, name="result%d" % blk) for blk in range(B * QB)]
-
-        def gather_key_scales(b):
-            nc.vector.tensor_copy(ks_g[:, b * N : (b + 1) * N], ks_pool[:].indirect(seq_list(b)))
-
-        def gather_token_scales():
-            nc.vector.tensor_copy(vs_g[:], vs_pool[:].indirect(offsets[:]))
+        inv_sum = placed([P, BLOCKS], F32, "inv_sum", INV_SUM_AT)
+        one_plus = keep.tile([P, BLOCKS], F32, name="one_plus")
+        result = [keep.tile([P, DV], F32, name="result%d" % blk) for blk in range(BLOCKS)]
 
         def gather_keys(o, b):
             nc.vector.tensor_copy(k_g[o][:, b * N : (b + 1) * N], k_pool[o][:].bitcast(U32).indirect(seq_list(b)))
@@ -154,13 +153,14 @@ def tile_attend_rel2_gate_pgb2q256n512t2048_kernel(tc, q_words, q_scales, k_word
                 stop=(o == PASSES - 1),
             )
 
-        def positive_part(blk, on_vector):
-            kept = pos[blk][:].rearrange("p (t m) -> p t m", t=4)
-            score = score_banks[blk][:].rearrange("p (m t) -> p t m", t=4)
-            if on_vector:
-                nc.vector.tensor_scalar_max(kept, score, 0.0)
-            else:
-                nc.scalar.activation(kept, score, ACT.Relu)
+        def dealt(blk):
+            return pos[blk][:].rearrange("p (t m) -> p m t", t=4), score_banks[blk][:].rearrange("p (m t) -> p m t", t=4)
+
+        def positive_part_on_scalar(blk):
+            nc.scalar.activation(*dealt(blk), ACT.Relu)
+
+        def positive_part_on_vector(blk):
+            nc.vector.tensor_scalar_max(*dealt(blk), 0.0)
 
         def square(blk):
             nc.scalar.activation(probs[blk][:], pos[blk][:], ACT.Square, accum_out=row_sum[:, blk : blk + 1])
@@ -186,28 +186,29 @@ def tile_attend_rel2_gate_pgb2q256n512t2048_kernel(tc, q_words, q_scales, k_word
             nc.vector.tensor_copy(v_g[b][h][:], v_pool[h][:].indirect(seq_list(b)))
 
         def turn_values(b, h):
-            bank = score_banks[QB + b][:, h * 256 : (h + 1) * 256].rearrange("p (u e) -> p u e", u=2)
+            bank = score_banks[QB + b][:, h * 2 * P : (h + 1) * 2 * P].rearrange("p (u e) -> p u e", u=2)
             for u in range(2):
                 nc.tensor.transpose(bank[:, u, :], v_g[b][h][:].bitcast(F32)[:, u : N // 2 : 2], ident[:])
             nc.scalar.copy(v_bf[b][h][:].bitcast(F32).rearrange("p (e u) -> p e u", u=2), bank.rearrange("p u e -> p e u"))
 
         def quantise_values(b, h):
-            nc.vector.quantize_mx(
-                out=v_codes[b][:, h * P : (h + 1) * P].bitcast(FP8X4), scales=v_plane[b][:, h * P : (h + 1) * P], in_=v_bf[b][h][:]
-            )
+            cols = slice(h * P, (h + 1) * P)
+            nc.vector.quantize_mx(out=v_codes[b][:, cols].bitcast(FP8X4), scales=v_plane[b][:, cols], in_=v_bf[b][h][:])
 
-        def row_factor(b):
-            cols = slice(b * QB, (b + 1) * QB)
-            nc.gpsimd.tensor_scalar(one_plus[:, cols], row_sum[:, cols], 1.0, 1.0, ALU.add, ALU.mult)
-            nc.vector.reciprocal(inv_sum[:, cols], one_plus[:, cols])
+        def row_factor():
+            nc.gpsimd.tensor_scalar(one_plus[:], row_sum[:], 1.0, 1.0, ALU.add, ALU.mult)
+            nc.vector.reciprocal(inv_sum[:], one_plus[:])
 
         def sigmoid(b):
             nc.scalar.activation(gate[b][:], gate_in[b][:], ACT.Sigmoid)
 
+        def sums_of(blk):
+            return turned[blk][:].rearrange("p t q -> p (t q)")[:, 0:DV]
+
         def product(blk):
-            b, j = divmod(blk, QB)
+            b = blk // QB
             nc.tensor.matmul_mx(
-                out=score_banks[b][:, j * DV : (j + 1) * DV],
+                out=sums_of(blk),
                 lhsT=w_codes[blk][:].bitcast(FP8X4),
                 lhsT_scale=w_plane[blk][:],
                 rhs=v_codes[b][:].bitcast(FP8X4),
@@ -219,72 +220,63 @@ def tile_attend_rel2_gate_pgb2q256n512t2048_kernel(tc, q_words, q_scales, k_word
         def finish(blk):
             b, j = divmod(blk, QB)
             nc.vector.scalar_tensor_tensor(
-                result[blk][:],
-                score_banks[b][:, j * DV : (j + 1) * DV],
-                inv_sum[:, blk : blk + 1],
-                gate[b][:, j, :],
-                ALU.mult,
-                ALU.mult,
+                result[blk][:], sums_of(blk), inv_sum[:, blk : blk + 1], gate[b][:, j, :], ALU.mult, ALU.mult
             )
             nc.sync.dma_start(out[b, j * P : (j + 1) * P, :], result[blk][:])
 
-        gather_token_scales()
-        nc.vector.tensor_copy(k_g[0][:], k_pool[0][:].bitcast(U32).indirect(offsets[:]))
-        gather_key_scales(0)
-        gather_key_scales(1)
-        turn_token_scales(0)
-        turn_token_scales(1)
-        gather_keys(1, 0)
-        gather_keys(1, 1)
-        scores(0, 0)
-        scores(1, 0)
-        scores(0, 1)
-        scores(1, 1)
-        scores(2, 0)
-        scores(2, 1)
-        scores(3, 0)
-        scores(3, 1)
-        positive_part(0, False)
-        positive_part(1, True)
-        gather_values(0, 0)
-        gather_values(1, 0)
-        square(0)
-        positive_part(2, False)
-        square(1)
-        turn_probs(0)
-        turn_probs(1)
-        positive_part(3, False)
-        square(2)
-        square(3)
-        turn_probs(2)
-        turn_values(0, 0)
-        turn_probs(3)
-        turn_values(1, 0)
-        weights(0)
-        weights(1)
-        gather_values(0, 1)
-        gather_values(1, 1)
-        turn_values(0, 1)
-        turn_values(1, 1)
-        row_factor(0)
-        row_factor(1)
-        sigmoid(0)
-        sigmoid(1)
-        quantise_weights(0)
-        quantise_weights(1)
-        quantise_values(0, 0)
-        quantise_values(1, 0)
+        nc.vector.tensor_copy(vs_g[:], vs_pool[:].indirect(offsets[:]))
+        nc.vector.tensor_copy(ks_g[:], ks_pool[:].indirect(offsets[:]))
+        for b in range(B):
+            gather_keys(0, b)
+        for b in range(B):
+            turn_token_scales(b)
+        for b in range(B):
+            gather_keys(1, b)
+
+        for o in range(PASSES):
+            for blk in range(QB):
+                scores(blk, o)
+        for blk in range(QB, BLOCKS):
+            for o in range(PASSES):
+                scores(blk, o)
+
+        positive_part_on_scalar(0)
+        positive_part_on_vector(1)
+        for b in range(B):
+            gather_values(b, 0)
+        for j in range(QB):
+            square(j)
+            positive_part_on_scalar(QB + j)
+        for blk in range(QB):
+            turn_probs(blk)
+        for blk in range(QB, BLOCKS):
+            square(blk)
+        for blk in range(QB, BLOCKS):
+            turn_probs(blk)
+        for b in range(B):
+            turn_values(b, 0)
+
+        for blk in range(QB):
+            weights(blk)
+        for b in range(B):
+            gather_values(b, 1)
+        for b in range(B):
+            sigmoid(b)
+            turn_values(b, 1)
+
         weights(2)
-        quantise_values(0, 1)
+        for j in range(QB):
+            quantise_weights(j)
+            quantise_values(0, j)
+        for blk in range(QB):
+            product(blk)
         weights(3)
-        product(0)
-        product(1)
         quantise_weights(2)
+        quantise_values(1, 0)
+        row_factor()
         quantise_values(1, 1)
-        quantise_weights(3)
         product(2)
+        quantise_weights(3)
         product(3)
-        finish(0)
-        finish(1)
-        finish(2)
-        finish(3)
+        for blk in range(BLOCKS):
+            finish(blk)

@@ -22,17 +22,12 @@ QB = NQ // P
 BLOCKS = B * QB
 EB = DV // P
 LIST_COLS = N // 16
-K_PLANE0 = 8
-
-V_POOL_BYTES = T * 4
+PROB_BYTES = (N + 16) * 4
 ROW_BF16 = N * 2
-ROW_F32 = N * 4
-KS_AT = EB * V_POOL_BYTES
-GATE_AT = 3 * V_POOL_BYTES
-POS_AT = 4 * V_POOL_BYTES
-W_CODES_AT = V_POOL_BYTES + QB * ROW_BF16
-V_CODES_AT = W_CODES_AT + BLOCKS * P * 4
-INV_SUM_AT = V_CODES_AT + B * DV * 4
+V1_AT = BLOCKS * PROB_BYTES + ROW_BF16
+PLACES_AT = V1_AT + T * 4
+CODES_AT = V1_AT
+K_PLANE0 = 8
 
 
 def tile_attend_rel2_gate_pgb2q256n512t2048_kernel(tc, q_words, q_scales, k_words, k_scales, vT, vs, og, offs, out):
@@ -47,20 +42,22 @@ def tile_attend_rel2_gate_pgb2q256n512t2048_kernel(tc, q_words, q_scales, k_word
 
         offsets = keep.tile([P, B * LIST_COLS], U16, name="offsets")
         k_pool = [keep.tile([P, T], I32, name="k_pool%d" % o) for o in range(PASSES)]
-        ks_pool = placed([P, T], U8, "ks_pool", KS_AT)
+        ks_pool = keep.tile([P, T], U8, name="ks_pool", align_bytes=64)
         vs_pool = keep.tile([P, T], F32, name="vs_pool")
-        v_pool = [placed([P, T], F32, "v_pool%d" % h, h * V_POOL_BYTES) for h in range(EB)]
-        q_codes = [keep.tile([P, PASSES, NQ], I32, name="q_codes%d" % b, align_bytes=64) for b in range(B)]
+        v_pool = [keep.tile([P, T], F32, name="v_pool0"), placed([P, T], F32, "v_pool1", V1_AT)]
+        q_codes = [keep.tile([P, B, NQ], I32, name="q_codes%d" % o, align_bytes=64) for o in range(PASSES)]
         q_plane = keep.tile([P, NQ], U8, name="q_plane", align_bytes=64)
-        gate_in = [placed([P, QB, DV], F32, "gate_in%d" % b, GATE_AT + b * ROW_F32) for b in range(B)]
+        gate_in = [keep.tile([P, QB, DV], F32, name="gate_in%d" % b) for b in range(B)]
         ident = keep.tile([P, P], F32, name="ident")
         warm = keep.tile([P, 8], F32, name="warm")
+        pos = keep.tile([P, BLOCKS, N + 8], F32, name="pos")
 
         nc.gpsimd.memset(ks_pool[:].bitcast(I32), 0)
         nc.gpsimd.memset(q_plane[:].bitcast(I32), 0)
         nc.vector.memset(vs_pool[0 : P - 1, :], 0.0)
         make_identity(nc, ident[:])
-        nc.scalar.activation(warm[:], ident[:, 0:8], ACT.Sigmoid)
+        nc.gpsimd.memset(pos[:, :, N : N + 1], 1.0)
+        nc.scalar.activation(warm[0:96, :], vs_pool[0:96, 0:8], ACT.Sigmoid)
 
         def load_key_scales():
             for quad in range(4):
@@ -79,8 +76,8 @@ def tile_attend_rel2_gate_pgb2q256n512t2048_kernel(tc, q_words, q_scales, k_word
         def load_keys(o):
             nc.sync.dma_start(k_pool[o][:], k_words[o].rearrange("p t r -> p (t r)").bitcast(I32))
 
-        def load_queries(b):
-            nc.sync.dma_start(q_codes[b][:], q_words[b].rearrange("o p q r -> p o (q r)").bitcast(I32))
+        def load_queries(o):
+            nc.sync.dma_start(q_codes[o][:], q_words[:, o].rearrange("b p q r -> p b (q r)").bitcast(I32))
 
         nc.sync.dma_start(offsets[:], offs)
         nc.sync.dma_start(vs_pool[P - 1 : P, :], vs[0:1, :])
@@ -106,46 +103,47 @@ def tile_attend_rel2_gate_pgb2q256n512t2048_kernel(tc, q_words, q_scales, k_word
 
         vs_t = keep.tile([P, B, 1, 4], F32, name="vs_t")
         row_sum = keep.tile([P, BLOCKS], F32, name="row_sum")
-        w_codes = [placed([P, P], U32, "w_codes%d" % blk, W_CODES_AT + blk * P * 4) for blk in range(BLOCKS)]
-        w_plane = [keep.tile([P, P], U8, name="w_plane%d" % blk, align_bytes=64) for blk in range(BLOCKS)]
-        v_codes = [placed([P, DV], U32, "v_codes%d" % b, V_CODES_AT + b * DV * 4) for b in range(B)]
-        v_plane = [keep.tile([P, DV], U8, name="v_plane%d" % b, align_bytes=64) for b in range(B)]
-        pos = [placed([P, N], F32, "pos%d" % blk, POS_AT + blk * ROW_F32) for blk in range(BLOCKS)]
-        probs = [keep.tile([P, N], F32, name="prob%d" % blk) for blk in range(BLOCKS)]
-        w_bf = [
-            placed([P, P, 4], BF16, "w_bf%d" % blk, (blk // QB) * V_POOL_BYTES + (blk % QB) * ROW_BF16)
+        w_codes = [
+            placed([P, P], U32, "w_codes%d" % blk, CODES_AT + blk * P * 4)
+            if blk in (1, 2)
+            else keep.tile([P, P], U32, name="w_codes%d" % blk, align_bytes=64)
             for blk in range(BLOCKS)
         ]
-        v_bf = [
-            [
-                placed([P, N], BF16, "v_bf%d0" % b, POS_AT + (BLOCKS - 1) * ROW_F32 + b * ROW_BF16),
-                placed([P, N], BF16, "v_bf%d1" % b, GATE_AT + b * ROW_F32),
-            ]
+        w_plane = [keep.tile([P, P], U8, name="w_plane%d" % blk, align_bytes=64) for blk in range(BLOCKS)]
+        v_codes = [
+            [placed([P, P], U32, "v_codes%d%d" % (b, h), CODES_AT + (BLOCKS + b * EB + h) * P * 4) for h in range(EB)]
             for b in range(B)
+        ]
+        v_plane = [[keep.tile([P, P], U8, name="v_plane%d%d" % (b, h), align_bytes=64) for h in range(EB)] for b in range(B)]
+        probs = [placed([P, N + 8], F32, "prob%d" % blk, blk * PROB_BYTES) for blk in range(BLOCKS)]
+        w_bf = [keep.tile([P, P, 4], BF16, name="w_bf%d" % blk, align_bytes=64) for blk in range(BLOCKS)]
+        v_bf = [
+            [keep.tile([P, N], BF16, name="v_bf00", align_bytes=64), placed([P, N], BF16, "v_bf01", PLACES_AT)],
+            [keep.tile([P, N], BF16, name="v_bf1%d" % h, align_bytes=64) for h in range(EB)],
         ]
         v_g = [
-            [placed([P, N], BF16, "v_g%d%d" % (b, h), KS_AT + (h * B + b) * ROW_BF16) for h in range(EB)]
-            for b in range(B)
+            [placed([P, N], BF16, "v_g%d%d" % (b, h), (BLOCKS - 1) * h * PROB_BYTES + b * ROW_BF16) for h in range(EB)] for b in range(B)
         ]
-        gate = [keep.tile([P, QB, DV], F32, name="gate%d" % b) for b in range(B)]
-        inv_sum = placed([P, BLOCKS], F32, "inv_sum", INV_SUM_AT)
-        one_plus = keep.tile([P, BLOCKS], F32, name="one_plus")
+        w_places = {1: keep.tile([P, 4, P], BF16, name="w_places1"), 2: placed([P, 4, P], BF16, "w_places2", PLACES_AT)}
+        gate = [
+            placed([P, QB, DV], F32, "gate%d" % b, (BLOCKS - 1) * PROB_BYTES + (2 * b - 1) * ROW_BF16) for b in range(B)
+        ]
+        inv_sum = keep.tile([P, BLOCKS], F32, name="inv_sum")
         result = [keep.tile([P, DV], F32, name="result%d" % blk) for blk in range(BLOCKS)]
 
         def gather_keys(o, b):
             nc.vector.tensor_copy(k_g[o][:, b * N : (b + 1) * N], k_pool[o][:].bitcast(U32).indirect(seq_list(b)))
 
         def turn_token_scales(b):
-            bank = score_banks[b][:].rearrange("p (t r) -> p t r", t=4)
             for t in range(4):
-                nc.tensor.transpose(bank[:, t, :], vs_g[:, b * N + t : (b + 1) * N : 4], ident[:])
-            nc.scalar.copy(vs_t[:, b, 0, :], bank[:, :, P - 1])
+                nc.tensor.transpose(turned[b][:, t, :], vs_g[:, b * N + t : (b + 1) * N : 4], ident[:])
+            nc.scalar.copy(vs_t[:, b, 0, :], turned[b][:, :, P - 1])
 
         def scores(blk, o):
             b, j = divmod(blk, QB)
             nc.tensor.matmul_mx(
                 out=score_banks[blk][:],
-                lhsT=q_codes[b][:, o, j * P : (j + 1) * P].bitcast(FP8X4),
+                lhsT=q_codes[o][:, b, j * P : (j + 1) * P].bitcast(FP8X4),
                 lhsT_scale=q_plane[4 * (b * PASSES + o) : P, j * P : (j + 1) * P],
                 rhs=k_g[o][:, b * N : (b + 1) * N].bitcast(FP8X4),
                 rhs_scale=ks_g[K_PLANE0 + 4 * o : P, b * N : (b + 1) * N],
@@ -154,7 +152,7 @@ def tile_attend_rel2_gate_pgb2q256n512t2048_kernel(tc, q_words, q_scales, k_word
             )
 
         def dealt(blk):
-            return pos[blk][:].rearrange("p (t m) -> p m t", t=4), score_banks[blk][:].rearrange("p (m t) -> p m t", t=4)
+            return pos[:, blk, 0:N].rearrange("p (t m) -> p m t", t=4), score_banks[blk][:].rearrange("p (m t) -> p m t", t=4)
 
         def positive_part_on_scalar(blk):
             nc.scalar.activation(*dealt(blk), ACT.Relu)
@@ -163,7 +161,7 @@ def tile_attend_rel2_gate_pgb2q256n512t2048_kernel(tc, q_words, q_scales, k_word
             nc.vector.tensor_scalar_max(*dealt(blk), 0.0)
 
         def square(blk):
-            nc.scalar.activation(probs[blk][:], pos[blk][:], ACT.Square, accum_out=row_sum[:, blk : blk + 1])
+            nc.scalar.activation(probs[blk][:, 0 : N + 1], pos[:, blk, 0 : N + 1], ACT.Square, accum_out=row_sum[:, blk : blk + 1])
 
         def turn_probs(blk):
             for t in range(4):
@@ -177,6 +175,11 @@ def tile_attend_rel2_gate_pgb2q256n512t2048_kernel(tc, q_words, q_scales, k_word
                 ALU.mult,
             )
 
+        def weights_on_scalar(blk):
+            for t in range(4):
+                nc.scalar.activation(w_places[blk][:, t, :], turned[blk][:, t, :], ACT.Copy, scale=vs_t[:, blk // QB, 0, t : t + 1])
+            nc.scalar.copy(w_bf[blk][:], w_places[blk][:].rearrange("p t q -> p q t"))
+
         def quantise_weights(blk):
             nc.vector.quantize_mx(
                 out=w_codes[blk][:].bitcast(FP8X4), scales=w_plane[blk][:], in_=w_bf[blk][:].rearrange("p q t -> p (q t)")
@@ -186,97 +189,91 @@ def tile_attend_rel2_gate_pgb2q256n512t2048_kernel(tc, q_words, q_scales, k_word
             nc.vector.tensor_copy(v_g[b][h][:], v_pool[h][:].indirect(seq_list(b)))
 
         def turn_values(b, h):
-            bank = score_banks[QB + b][:, h * 2 * P : (h + 1) * 2 * P].rearrange("p (u e) -> p u e", u=2)
+            bank = score_banks[h * B + b][:, 0 : 2 * P].rearrange("p (u e) -> p u e", u=2)
             for u in range(2):
                 nc.tensor.transpose(bank[:, u, :], v_g[b][h][:].bitcast(F32)[:, u : N // 2 : 2], ident[:])
             nc.scalar.copy(v_bf[b][h][:].bitcast(F32).rearrange("p (e u) -> p e u", u=2), bank.rearrange("p u e -> p e u"))
 
         def quantise_values(b, h):
-            cols = slice(h * P, (h + 1) * P)
-            nc.vector.quantize_mx(out=v_codes[b][:, cols].bitcast(FP8X4), scales=v_plane[b][:, cols], in_=v_bf[b][h][:])
+            nc.vector.quantize_mx(out=v_codes[b][h][:].bitcast(FP8X4), scales=v_plane[b][h][:], in_=v_bf[b][h][:])
 
         def row_factor():
-            nc.gpsimd.tensor_scalar(one_plus[:], row_sum[:], 1.0, 1.0, ALU.add, ALU.mult)
-            nc.vector.reciprocal(inv_sum[:], one_plus[:])
+            nc.vector.reciprocal(inv_sum[:], row_sum[:])
 
-        def sigmoid(b):
-            nc.scalar.activation(gate[b][:], gate_in[b][:], ACT.Sigmoid)
+        def sigmoid(blk):
+            b, j = divmod(blk, QB)
+            nc.scalar.activation(gate[b][:, j, :], gate_in[b][:, j, :], ACT.Sigmoid)
 
-        def sums_of(blk):
-            return turned[blk][:].rearrange("p t q -> p (t q)")[:, 0:DV]
+        def sums_of(blk, h):
+            b, j = divmod(blk, QB)
+            return score_banks[b][:, j * P : (j + 1) * P] if h == 0 else turned[blk][:, 0, :]
 
-        def product(blk):
+        def product(blk, h):
             b = blk // QB
             nc.tensor.matmul_mx(
-                out=sums_of(blk),
+                out=sums_of(blk, h),
                 lhsT=w_codes[blk][:].bitcast(FP8X4),
                 lhsT_scale=w_plane[blk][:],
-                rhs=v_codes[b][:].bitcast(FP8X4),
-                rhs_scale=v_plane[b][:],
+                rhs=v_codes[b][h][:].bitcast(FP8X4),
+                rhs_scale=v_plane[b][h][:],
                 start=True,
                 stop=True,
             )
 
-        def finish(blk):
+        def finish(blk, h):
             b, j = divmod(blk, QB)
+            cols = slice(h * P, (h + 1) * P)
             nc.vector.scalar_tensor_tensor(
-                result[blk][:], sums_of(blk), inv_sum[:, blk : blk + 1], gate[b][:, j, :], ALU.mult, ALU.mult
+                result[blk][:, cols], sums_of(blk, h), inv_sum[:, blk : blk + 1], gate[b][:, j, cols], ALU.mult, ALU.mult
             )
+
+        def store(blk):
+            b, j = divmod(blk, QB)
             nc.sync.dma_start(out[b, j * P : (j + 1) * P, :], result[blk][:])
 
         nc.vector.tensor_copy(vs_g[:], vs_pool[:].indirect(offsets[:]))
         nc.vector.tensor_copy(ks_g[:], ks_pool[:].indirect(offsets[:]))
-        for b in range(B):
-            gather_keys(0, b)
+        for o in range(PASSES):
+            for b in range(B):
+                gather_keys(o, b)
         for b in range(B):
             turn_token_scales(b)
-        for b in range(B):
-            gather_keys(1, b)
-
         for o in range(PASSES):
-            for blk in range(QB):
-                scores(blk, o)
-        for blk in range(QB, BLOCKS):
-            for o in range(PASSES):
+            for blk in range(BLOCKS):
                 scores(blk, o)
 
         positive_part_on_scalar(0)
-        positive_part_on_vector(1)
-        for b in range(B):
-            gather_values(b, 0)
-        for j in range(QB):
-            square(j)
-            positive_part_on_scalar(QB + j)
-        for blk in range(QB):
-            turn_probs(blk)
-        for blk in range(QB, BLOCKS):
+        for blk in range(1, BLOCKS):
+            positive_part_on_vector(blk)
+        for blk in range(BLOCKS):
             square(blk)
-        for blk in range(QB, BLOCKS):
             turn_probs(blk)
+        weights(0)
+        weights(3)
+        quantise_weights(0)
+        row_factor()
+        quantise_weights(3)
+        for h in range(EB):
+            for b in range(B):
+                gather_values(b, h)
         for b in range(B):
             turn_values(b, 0)
-
-        for blk in range(QB):
-            weights(blk)
+        weights_on_scalar(1)
+        weights_on_scalar(2)
         for b in range(B):
-            gather_values(b, 1)
-        for b in range(B):
-            sigmoid(b)
             turn_values(b, 1)
-
-        weights(2)
-        for j in range(QB):
-            quantise_weights(j)
-            quantise_values(0, j)
-        for blk in range(QB):
-            product(blk)
-        weights(3)
-        quantise_weights(2)
-        quantise_values(1, 0)
-        row_factor()
+        quantise_values(0, 1)
+        quantise_values(0, 0)
+        quantise_weights(1)
         quantise_values(1, 1)
-        product(2)
-        quantise_weights(3)
-        product(3)
+        quantise_values(1, 0)
+        quantise_weights(2)
         for blk in range(BLOCKS):
-            finish(blk)
+            sigmoid(blk)
+        for h in (1, 0):
+            for blk in range(BLOCKS):
+                product(blk, h)
+        for blk in range(BLOCKS):
+            for h in range(EB):
+                finish(blk, h)
+            store(blk)

@@ -26,7 +26,8 @@ PROB_BYTES = (N + 16) * 4
 ROW_BF16 = N * 2
 V1_AT = BLOCKS * PROB_BYTES + ROW_BF16
 PLACES_AT = V1_AT + T * 4
-CODES_AT = V1_AT
+CODES_AT = V1_AT + ROW_BF16
+INV_AT = CODES_AT + (BLOCKS + B * EB) * P * 4
 K_PLANE0 = 8
 
 
@@ -96,19 +97,14 @@ def tile_attend_rel2_gate_pgb2q256n512t2048_kernel(tc, q_words, q_scales, k_word
             return offsets[:, b * LIST_COLS : (b + 1) * LIST_COLS]
 
         ks_g = keep.tile([P, B * N], U8, name="ks_g", align_bytes=64)
-        vs_g = keep.tile([P, B * N], F32, name="vs_g")
+        vs_g = [keep.tile([P, 4, P], F32, name="vs_g%d" % b) for b in range(B)]
         k_g = [keep.tile([P, B * N], U32, name="k_g%d" % o, align_bytes=64) for o in range(PASSES)]
         score_banks = [psum.tile([P, N], F32, name="score%d" % blk) for blk in range(BLOCKS)]
         turned = [psum.tile([P, 4, P], F32, name="turned%d" % blk) for blk in range(BLOCKS)]
 
         vs_t = keep.tile([P, B, 1, 4], F32, name="vs_t")
         row_sum = keep.tile([P, BLOCKS], F32, name="row_sum")
-        w_codes = [
-            placed([P, P], U32, "w_codes%d" % blk, CODES_AT + blk * P * 4)
-            if blk in (1, 2)
-            else keep.tile([P, P], U32, name="w_codes%d" % blk, align_bytes=64)
-            for blk in range(BLOCKS)
-        ]
+        w_codes = [placed([P, P], U32, "w_codes%d" % blk, CODES_AT + blk * P * 4) for blk in range(BLOCKS)]
         w_plane = [keep.tile([P, P], U8, name="w_plane%d" % blk, align_bytes=64) for blk in range(BLOCKS)]
         v_codes = [
             [placed([P, P], U32, "v_codes%d%d" % (b, h), CODES_AT + (BLOCKS + b * EB + h) * P * 4) for h in range(EB)]
@@ -116,19 +112,19 @@ def tile_attend_rel2_gate_pgb2q256n512t2048_kernel(tc, q_words, q_scales, k_word
         ]
         v_plane = [[keep.tile([P, P], U8, name="v_plane%d%d" % (b, h), align_bytes=64) for h in range(EB)] for b in range(B)]
         probs = [placed([P, N + 8], F32, "prob%d" % blk, blk * PROB_BYTES) for blk in range(BLOCKS)]
-        w_bf = [keep.tile([P, P, 4], BF16, name="w_bf%d" % blk, align_bytes=64) for blk in range(BLOCKS)]
+        w_bf = [keep.tile([P, P, 4], BF16, name="w_bf%d" % blk, align_bytes=64) for blk in range(BLOCKS - 1)]
+        w_bf.append(placed([P, P, 4], BF16, "w_bf3", V1_AT))
         v_bf = [
             [keep.tile([P, N], BF16, name="v_bf00", align_bytes=64), placed([P, N], BF16, "v_bf01", PLACES_AT)],
             [keep.tile([P, N], BF16, name="v_bf1%d" % h, align_bytes=64) for h in range(EB)],
         ]
         v_g = [
-            [placed([P, N], BF16, "v_g%d%d" % (b, h), (BLOCKS - 1) * h * PROB_BYTES + b * ROW_BF16) for h in range(EB)] for b in range(B)
+            [keep.tile([P, N], BF16, name="v_g%d0" % b), placed([P, N], BF16, "v_g%d1" % b, PROB_BYTES + b * ROW_BF16)]
+            for b in range(B)
         ]
-        w_places = {1: keep.tile([P, 4, P], BF16, name="w_places1"), 2: placed([P, 4, P], BF16, "w_places2", PLACES_AT)}
-        gate = [
-            placed([P, QB, DV], F32, "gate%d" % b, (BLOCKS - 1) * PROB_BYTES + (2 * b - 1) * ROW_BF16) for b in range(B)
-        ]
-        inv_sum = keep.tile([P, BLOCKS], F32, name="inv_sum")
+        w_places = placed([P, 4, P], BF16, "w_places", PLACES_AT)
+        gate = placed([P, BLOCKS, DV], F32, "gate", PROB_BYTES + ROW_BF16)
+        inv_sum = placed([P, BLOCKS], F32, "inv_sum", INV_AT)
         result = [keep.tile([P, DV], F32, name="result%d" % blk) for blk in range(BLOCKS)]
 
         def gather_keys(o, b):
@@ -136,7 +132,7 @@ def tile_attend_rel2_gate_pgb2q256n512t2048_kernel(tc, q_words, q_scales, k_word
 
         def turn_token_scales(b):
             for t in range(4):
-                nc.tensor.transpose(turned[b][:, t, :], vs_g[:, b * N + t : (b + 1) * N : 4], ident[:])
+                nc.tensor.transpose(turned[b][:, t, :], vs_g[b][:, t, :], ident[:])
             nc.scalar.copy(vs_t[:, b, 0, :], turned[b][:, :, P - 1])
 
         def scores(blk, o):
@@ -177,8 +173,8 @@ def tile_attend_rel2_gate_pgb2q256n512t2048_kernel(tc, q_words, q_scales, k_word
 
         def weights_on_scalar(blk):
             for t in range(4):
-                nc.scalar.activation(w_places[blk][:, t, :], turned[blk][:, t, :], ACT.Copy, scale=vs_t[:, blk // QB, 0, t : t + 1])
-            nc.scalar.copy(w_bf[blk][:], w_places[blk][:].rearrange("p t q -> p q t"))
+                nc.scalar.activation(w_places[:, t, :], turned[blk][:, t, :], ACT.Copy, scale=vs_t[:, blk // QB, 0, t : t + 1])
+            nc.scalar.copy(w_bf[blk][:], w_places[:].rearrange("p t q -> p q t"))
 
         def quantise_weights(blk):
             nc.vector.quantize_mx(
@@ -186,12 +182,12 @@ def tile_attend_rel2_gate_pgb2q256n512t2048_kernel(tc, q_words, q_scales, k_word
             )
 
         def gather_values(b, h):
-            nc.vector.tensor_copy(v_g[b][h][:], v_pool[h][:].indirect(seq_list(b)))
+            nc.vector.tensor_copy(v_g[b][h][:].rearrange("p (u m e) -> p m u e", u=2, e=2), v_pool[h][:].indirect(seq_list(b)))
 
         def turn_values(b, h):
             bank = score_banks[h * B + b][:, 0 : 2 * P].rearrange("p (u e) -> p u e", u=2)
             for u in range(2):
-                nc.tensor.transpose(bank[:, u, :], v_g[b][h][:].bitcast(F32)[:, u : N // 2 : 2], ident[:])
+                nc.tensor.transpose(bank[:, u, :], v_g[b][h][:].bitcast(F32)[:, u * P : (u + 1) * P], ident[:])
             nc.scalar.copy(v_bf[b][h][:].bitcast(F32).rearrange("p (e u) -> p e u", u=2), bank.rearrange("p u e -> p e u"))
 
         def quantise_values(b, h):
@@ -202,7 +198,7 @@ def tile_attend_rel2_gate_pgb2q256n512t2048_kernel(tc, q_words, q_scales, k_word
 
         def sigmoid(blk):
             b, j = divmod(blk, QB)
-            nc.scalar.activation(gate[b][:, j, :], gate_in[b][:, j, :], ACT.Sigmoid)
+            nc.scalar.activation(gate[:, blk, :], gate_in[b][:, j, :], ACT.Sigmoid)
 
         def sums_of(blk, h):
             b, j = divmod(blk, QB)
@@ -224,14 +220,15 @@ def tile_attend_rel2_gate_pgb2q256n512t2048_kernel(tc, q_words, q_scales, k_word
             b, j = divmod(blk, QB)
             cols = slice(h * P, (h + 1) * P)
             nc.vector.scalar_tensor_tensor(
-                result[blk][:, cols], sums_of(blk, h), inv_sum[:, blk : blk + 1], gate[b][:, j, cols], ALU.mult, ALU.mult
+                result[blk][:, cols], sums_of(blk, h), inv_sum[:, blk : blk + 1], gate[:, blk, cols], ALU.mult, ALU.mult
             )
 
         def store(blk):
             b, j = divmod(blk, QB)
             nc.sync.dma_start(out[b, j * P : (j + 1) * P, :], result[blk][:])
 
-        nc.vector.tensor_copy(vs_g[:], vs_pool[:].indirect(offsets[:]))
+        for b in range(B):
+            nc.vector.tensor_copy(vs_g[b][:].bitcast(U32).rearrange("p t m -> p m t"), vs_pool[:].bitcast(U32).indirect(seq_list(b)))
         nc.vector.tensor_copy(ks_g[:], ks_pool[:].indirect(offsets[:]))
         for o in range(PASSES):
             for b in range(B):
@@ -242,32 +239,30 @@ def tile_attend_rel2_gate_pgb2q256n512t2048_kernel(tc, q_words, q_scales, k_word
             for blk in range(BLOCKS):
                 scores(blk, o)
 
-        positive_part_on_scalar(0)
-        for blk in range(1, BLOCKS):
-            positive_part_on_vector(blk)
+        for b in range(B):
+            positive_part_on_scalar(b * QB)
+            positive_part_on_vector(b * QB + 1)
+        for b in range(B):
+            gather_values(b, 0)
         for blk in range(BLOCKS):
             square(blk)
             turn_probs(blk)
         weights(0)
-        weights(3)
-        quantise_weights(0)
-        row_factor()
-        quantise_weights(3)
-        for h in range(EB):
-            for b in range(B):
-                gather_values(b, h)
+        weights(1)
         for b in range(B):
+            gather_values(b, 1)
             turn_values(b, 0)
-        weights_on_scalar(1)
         weights_on_scalar(2)
         for b in range(B):
             turn_values(b, 1)
-        quantise_values(0, 1)
-        quantise_values(0, 0)
-        quantise_weights(1)
-        quantise_values(1, 1)
-        quantise_values(1, 0)
-        quantise_weights(2)
+        weights(3)
+        for b in range(B):
+            quantise_values(b, 1)
+        for b in range(B):
+            quantise_values(b, 0)
+            for j in range(QB):
+                quantise_weights(b * QB + j)
+        row_factor()
         for blk in range(BLOCKS):
             sigmoid(blk)
         for h in (1, 0):

@@ -55,7 +55,7 @@ def tile_attend_rel2_gate_pgb2q256n512t2048_kernel(tc, q_words, q_scales, k_word
 
         nc.gpsimd.memset(ks_pool[:].bitcast(I32), 0)
         nc.gpsimd.memset(q_plane[:].bitcast(I32), 0)
-        nc.vector.memset(vs_pool[0 : P - 1, :], 0.0)
+        nc.gpsimd.memset(vs_pool[0 : P - 1, :], 0.0)
         make_identity(nc, ident[:])
         nc.gpsimd.memset(pos[:, :, N : N + 1], 1.0)
         nc.scalar.activation(warm[0:96, :], vs_pool[0:96, 0:8], ACT.Sigmoid)
@@ -80,9 +80,9 @@ def tile_attend_rel2_gate_pgb2q256n512t2048_kernel(tc, q_words, q_scales, k_word
         def load_queries(o):
             nc.sync.dma_start(q_codes[o][:], q_words[:, o].rearrange("b p q r -> p b (q r)").bitcast(I32))
 
+        load_queries(0)
         nc.sync.dma_start(offsets[:], offs)
         nc.sync.dma_start(vs_pool[P - 1 : P, :], vs[0:1, :])
-        load_queries(0)
         load_key_scales()
         load_keys(0)
         load_query_scales()
@@ -123,7 +123,8 @@ def tile_attend_rel2_gate_pgb2q256n512t2048_kernel(tc, q_words, q_scales, k_word
             for b in range(B)
         ]
         w_places = placed([P, 4, P], BF16, "w_places", PLACES_AT)
-        gate = placed([P, BLOCKS, DV], F32, "gate", PROB_BYTES + ROW_BF16)
+        gate = placed([P, BLOCKS - 1, DV], F32, "gate", PROB_BYTES + ROW_BF16)
+        gates = [placed([P, DV], F32, "gate0", PROB_BYTES)[:]] + [gate[:, j, :] for j in range(BLOCKS - 1)]
         inv_sum = placed([P, BLOCKS], F32, "inv_sum", INV_AT)
         result = [keep.tile([P, DV], F32, name="result%d" % blk) for blk in range(BLOCKS)]
 
@@ -198,7 +199,7 @@ def tile_attend_rel2_gate_pgb2q256n512t2048_kernel(tc, q_words, q_scales, k_word
 
         def sigmoid(blk):
             b, j = divmod(blk, QB)
-            nc.scalar.activation(gate[:, blk, :], gate_in[b][:, j, :], ACT.Sigmoid)
+            nc.scalar.activation(gates[blk], gate_in[b][:, j, :], ACT.Sigmoid)
 
         def sums_of(blk, h):
             b, j = divmod(blk, QB)
@@ -220,7 +221,7 @@ def tile_attend_rel2_gate_pgb2q256n512t2048_kernel(tc, q_words, q_scales, k_word
             b, j = divmod(blk, QB)
             cols = slice(h * P, (h + 1) * P)
             nc.vector.scalar_tensor_tensor(
-                result[blk][:, cols], sums_of(blk, h), inv_sum[:, blk : blk + 1], gate[:, blk, cols], ALU.mult, ALU.mult
+                result[blk][:, cols], sums_of(blk, h), inv_sum[:, blk : blk + 1], gates[blk][:, cols], ALU.mult, ALU.mult
             )
 
         def store(blk):

@@ -51,7 +51,7 @@ def tile_attend_rel2_gate_pgb2q256n512t2048_kernel(tc, q_words, q_scales, k_word
         gate_in = [keep.tile([P, QB, DV], F32, name="gate_in%d" % b) for b in range(B)]
         ident = keep.tile([P, P], F32, name="ident")
         warm = keep.tile([P, 8], F32, name="warm")
-        pos = keep.tile([P, BLOCKS, N + 8], F32, name="pos")
+        pos = keep.tile([P, BLOCKS - 1, N + 8], F32, name="pos")
 
         nc.gpsimd.memset(ks_pool[:].bitcast(I32), 0)
         nc.gpsimd.memset(q_plane[:].bitcast(I32), 0)
@@ -149,7 +149,7 @@ def tile_attend_rel2_gate_pgb2q256n512t2048_kernel(tc, q_words, q_scales, k_word
             )
 
         def dealt(blk):
-            return pos[:, blk, 0:N].rearrange("p (t m) -> p m t", t=4), score_banks[blk][:].rearrange("p (m t) -> p m t", t=4)
+            return pos[:, blk % (BLOCKS - 1), 0:N].rearrange("p (t m) -> p m t", t=4), score_banks[blk][:].rearrange("p (m t) -> p m t", t=4)
 
         def positive_part_on_scalar(blk):
             nc.scalar.activation(*dealt(blk), ACT.Relu)
@@ -158,7 +158,7 @@ def tile_attend_rel2_gate_pgb2q256n512t2048_kernel(tc, q_words, q_scales, k_word
             nc.vector.tensor_scalar_max(*dealt(blk), 0.0)
 
         def square(blk):
-            nc.scalar.activation(probs[blk][:, 0 : N + 1], pos[:, blk, 0 : N + 1], ACT.Square, accum_out=row_sum[:, blk : blk + 1])
+            nc.scalar.activation(probs[blk][:, 0 : N + 1], pos[:, blk % (BLOCKS - 1), 0 : N + 1], ACT.Square, accum_out=row_sum[:, blk : blk + 1])
 
         def turn_probs(blk):
             for t in range(4):
@@ -240,14 +240,17 @@ def tile_attend_rel2_gate_pgb2q256n512t2048_kernel(tc, q_words, q_scales, k_word
             for blk in range(BLOCKS):
                 scores(blk, o)
 
-        for b in range(B):
-            positive_part_on_scalar(b * QB)
-            positive_part_on_vector(b * QB + 1)
+        positive_part_on_scalar(0)
+        positive_part_on_vector(1)
+        positive_part_on_vector(2)
         for b in range(B):
             gather_values(b, 0)
-        for blk in range(BLOCKS):
+        for blk in range(BLOCKS - 1):
             square(blk)
             turn_probs(blk)
+        positive_part_on_scalar(3)
+        square(3)
+        turn_probs(3)
         weights(0)
         weights(1)
         for b in range(B):
@@ -257,13 +260,13 @@ def tile_attend_rel2_gate_pgb2q256n512t2048_kernel(tc, q_words, q_scales, k_word
         for b in range(B):
             turn_values(b, 1)
         weights(3)
-        for b in range(B):
-            quantise_values(b, 1)
+        quantise_values(0, 1)
         for b in range(B):
             quantise_values(b, 0)
             for j in range(QB):
                 quantise_weights(b * QB + j)
         row_factor()
+        quantise_values(1, 1)
         for blk in range(BLOCKS):
             sigmoid(blk)
         for h in (1, 0):

@@ -51,7 +51,7 @@ def tile_attend_rel2_gate_pgb2q256n512t2048_kernel(tc, q_words, q_scales, k_word
         gate_in = [keep.tile([P, QB, DV], F32, name="gate_in%d" % b) for b in range(B)]
         ident = keep.tile([P, P], F32, name="ident")
         warm = keep.tile([P, 8], F32, name="warm")
-        pos = keep.tile([P, BLOCKS - 1, N + 8], F32, name="pos")
+        pos = keep.tile([P, BLOCKS, N + 8], F32, name="pos")
 
         nc.gpsimd.memset(ks_pool[:].bitcast(I32), 0)
         nc.gpsimd.memset(q_plane[:].bitcast(I32), 0)
@@ -106,11 +106,8 @@ def tile_attend_rel2_gate_pgb2q256n512t2048_kernel(tc, q_words, q_scales, k_word
         row_sum = keep.tile([P, BLOCKS], F32, name="row_sum")
         w_codes = [placed([P, P], U32, "w_codes%d" % blk, CODES_AT + blk * P * 4) for blk in range(BLOCKS)]
         w_plane = [keep.tile([P, P], U8, name="w_plane%d" % blk, align_bytes=64) for blk in range(BLOCKS)]
-        v_codes = [
-            [placed([P, P], U32, "v_codes%d%d" % (b, h), CODES_AT + (BLOCKS + b * EB + h) * P * 4) for h in range(EB)]
-            for b in range(B)
-        ]
-        v_plane = [[keep.tile([P, P], U8, name="v_plane%d%d" % (b, h), align_bytes=64) for h in range(EB)] for b in range(B)]
+        v_codes = [placed([P, DV], U32, "v_codes%d" % b, CODES_AT + (BLOCKS + b * EB) * P * 4) for b in range(B)]
+        v_plane = [keep.tile([P, DV], U8, name="v_plane%d" % b, align_bytes=64) for b in range(B)]
         probs = [placed([P, N + 8], F32, "prob%d" % blk, blk * PROB_BYTES) for blk in range(BLOCKS)]
         w_bf = [keep.tile([P, P, 4], BF16, name="w_bf%d" % blk, align_bytes=64) for blk in range(BLOCKS - 1)]
         w_bf.append(placed([P, P, 4], BF16, "w_bf3", V1_AT))
@@ -149,7 +146,7 @@ def tile_attend_rel2_gate_pgb2q256n512t2048_kernel(tc, q_words, q_scales, k_word
             )
 
         def dealt(blk):
-            return pos[:, blk % (BLOCKS - 1), 0:N].rearrange("p (t m) -> p m t", t=4), score_banks[blk][:].rearrange("p (m t) -> p m t", t=4)
+            return pos[:, blk, 0:N].rearrange("p (t m) -> p m t", t=4), score_banks[blk][:].rearrange("p (m t) -> p m t", t=4)
 
         def positive_part_on_scalar(blk):
             nc.scalar.activation(*dealt(blk), ACT.Relu)
@@ -158,7 +155,7 @@ def tile_attend_rel2_gate_pgb2q256n512t2048_kernel(tc, q_words, q_scales, k_word
             nc.vector.tensor_scalar_max(*dealt(blk), 0.0)
 
         def square(blk):
-            nc.scalar.activation(probs[blk][:, 0 : N + 1], pos[:, blk % (BLOCKS - 1), 0 : N + 1], ACT.Square, accum_out=row_sum[:, blk : blk + 1])
+            nc.scalar.activation(probs[blk][:, 0 : N + 1], pos[:, blk, 0 : N + 1], ACT.Square, accum_out=row_sum[:, blk : blk + 1])
 
         def turn_probs(blk):
             for t in range(4):
@@ -192,7 +189,8 @@ def tile_attend_rel2_gate_pgb2q256n512t2048_kernel(tc, q_words, q_scales, k_word
             nc.scalar.copy(v_bf[b][h][:].bitcast(F32).rearrange("p (e u) -> p e u", u=2), bank.rearrange("p u e -> p e u"))
 
         def quantise_values(b, h):
-            nc.vector.quantize_mx(out=v_codes[b][h][:].bitcast(FP8X4), scales=v_plane[b][h][:], in_=v_bf[b][h][:])
+            cols = slice(h * P, (h + 1) * P)
+            nc.vector.quantize_mx(out=v_codes[b][:, cols].bitcast(FP8X4), scales=v_plane[b][:, cols], in_=v_bf[b][h][:])
 
         def row_factor():
             nc.vector.reciprocal(inv_sum[:], row_sum[:])
@@ -201,28 +199,23 @@ def tile_attend_rel2_gate_pgb2q256n512t2048_kernel(tc, q_words, q_scales, k_word
             b, j = divmod(blk, QB)
             nc.scalar.activation(gates[blk], gate_in[b][:, j, :], ACT.Sigmoid)
 
-        def sums_of(blk, h):
-            b, j = divmod(blk, QB)
-            return score_banks[b][:, j * P : (j + 1) * P] if h == 0 else turned[blk][:, 0, :]
+        def sums_of(blk):
+            return turned[blk][:, 0:EB, :].rearrange("p h e -> p (h e)")
 
-        def product(blk, h):
+        def product(blk):
             b = blk // QB
             nc.tensor.matmul_mx(
-                out=sums_of(blk, h),
+                out=sums_of(blk),
                 lhsT=w_codes[blk][:].bitcast(FP8X4),
                 lhsT_scale=w_plane[blk][:],
-                rhs=v_codes[b][h][:].bitcast(FP8X4),
-                rhs_scale=v_plane[b][h][:],
+                rhs=v_codes[b][:].bitcast(FP8X4),
+                rhs_scale=v_plane[b][:],
                 start=True,
                 stop=True,
             )
 
-        def finish(blk, h):
-            b, j = divmod(blk, QB)
-            cols = slice(h * P, (h + 1) * P)
-            nc.vector.scalar_tensor_tensor(
-                result[blk][:, cols], sums_of(blk, h), inv_sum[:, blk : blk + 1], gates[blk][:, cols], ALU.mult, ALU.mult
-            )
+        def finish(blk):
+            nc.vector.scalar_tensor_tensor(result[blk][:], sums_of(blk), inv_sum[:, blk : blk + 1], gates[blk], ALU.mult, ALU.mult)
 
         def store(blk):
             b, j = divmod(blk, QB)
@@ -240,17 +233,15 @@ def tile_attend_rel2_gate_pgb2q256n512t2048_kernel(tc, q_words, q_scales, k_word
             for blk in range(BLOCKS):
                 scores(blk, o)
 
-        positive_part_on_scalar(0)
-        positive_part_on_vector(1)
-        positive_part_on_vector(2)
+        positive_part_on_vector(0)
+        positive_part_on_scalar(1)
+        for blk in range(2, BLOCKS):
+            positive_part_on_vector(blk)
         for b in range(B):
             gather_values(b, 0)
-        for blk in range(BLOCKS - 1):
+        for blk in range(BLOCKS):
             square(blk)
             turn_probs(blk)
-        positive_part_on_scalar(3)
-        square(3)
-        turn_probs(3)
         weights(0)
         weights(1)
         for b in range(B):
@@ -260,19 +251,16 @@ def tile_attend_rel2_gate_pgb2q256n512t2048_kernel(tc, q_words, q_scales, k_word
         for b in range(B):
             turn_values(b, 1)
         weights(3)
-        quantise_values(0, 1)
         for b in range(B):
-            quantise_values(b, 0)
             for j in range(QB):
+                quantise_values(b, j)
                 quantise_weights(b * QB + j)
-        row_factor()
-        quantise_values(1, 1)
+            if b == 0:
+                row_factor()
         for blk in range(BLOCKS):
             sigmoid(blk)
-        for h in (1, 0):
-            for blk in range(BLOCKS):
-                product(blk, h)
         for blk in range(BLOCKS):
-            for h in range(EB):
-                finish(blk, h)
+            product(blk)
+        for blk in range(BLOCKS):
+            finish(blk)
             store(blk)

@@ -57,6 +57,7 @@ def tile_attend_rel2_gate_pgb2q256n512t2048_kernel(tc, q_words, q_scales, k_word
         nc.gpsimd.memset(q_plane[:].bitcast(I32), 0)
         nc.gpsimd.memset(vs_pool[0 : P - 1, :], 0.0)
         make_identity(nc, ident[:])
+        nc.gpsimd.memset(pos[:, :, N + 1 : N + 4], 0.0)
         nc.gpsimd.memset(pos[:, :, N : N + 1], 1.0)
         nc.scalar.activation(warm[0:96, :], vs_pool[0:96, 0:8], ACT.Sigmoid)
 
@@ -108,7 +109,7 @@ def tile_attend_rel2_gate_pgb2q256n512t2048_kernel(tc, q_words, q_scales, k_word
         w_plane = [keep.tile([P, P], U8, name="w_plane%d" % blk, align_bytes=64) for blk in range(BLOCKS)]
         v_codes = [placed([P, DV], U32, "v_codes%d" % b, CODES_AT + (BLOCKS + b * EB) * P * 4) for b in range(B)]
         v_plane = [keep.tile([P, DV], U8, name="v_plane%d" % b, align_bytes=64) for b in range(B)]
-        probs = [placed([P, N + 8], F32, "prob%d" % blk, blk * PROB_BYTES) for blk in range(BLOCKS)]
+        probs = [placed([P, 4, P + 4], F32, "prob%d" % blk, blk * PROB_BYTES) for blk in range(BLOCKS)]
         w_bf = [keep.tile([P, P, 4], BF16, name="w_bf%d" % blk, align_bytes=64) for blk in range(BLOCKS - 1)]
         w_bf.append(placed([P, P, 4], BF16, "w_bf3", V1_AT))
         v_bf = [
@@ -145,21 +146,23 @@ def tile_attend_rel2_gate_pgb2q256n512t2048_kernel(tc, q_words, q_scales, k_word
                 stop=(o == PASSES - 1),
             )
 
-        def dealt(blk):
-            return pos[:, blk, 0:N].rearrange("p (t m) -> p m t", t=4), score_banks[blk][:].rearrange("p (m t) -> p m t", t=4)
-
         def positive_part_on_scalar(blk):
-            nc.scalar.activation(*dealt(blk), ACT.Relu)
+            nc.scalar.activation(pos[:, blk, 0:N], score_banks[blk][:], ACT.Relu)
 
         def positive_part_on_vector(blk):
-            nc.vector.tensor_scalar_max(*dealt(blk), 0.0)
+            nc.vector.tensor_scalar_max(pos[:, blk, 0:N], score_banks[blk][:], 0.0)
 
         def square(blk):
-            nc.scalar.activation(probs[blk][:, 0 : N + 1], pos[:, blk, 0 : N + 1], ACT.Square, accum_out=row_sum[:, blk : blk + 1])
+            nc.scalar.activation(
+                probs[blk][:, :, 0 : P + 1].rearrange("p t m -> p m t"),
+                pos[:, blk, 0 : N + 4].rearrange("p (m t) -> p m t", t=4),
+                ACT.Square,
+                accum_out=row_sum[:, blk : blk + 1],
+            )
 
         def turn_probs(blk):
             for t in range(4):
-                nc.tensor.transpose(turned[blk][:, t, :], probs[blk][:, t * P : (t + 1) * P], ident[:])
+                nc.tensor.transpose(turned[blk][:, t, :], probs[blk][:, t, 0:P], ident[:])
 
         def weights(blk):
             nc.vector.tensor_tensor(

@@ -22,13 +22,9 @@ QB = NQ // P
 BLOCKS = B * QB
 EB = DV // P
 LIST_COLS = N // 16
-PROB_BYTES = (N + 16) * 4
-ROW_BF16 = N * 2
-V1_AT = BLOCKS * PROB_BYTES + ROW_BF16
-PLACES_AT = V1_AT + T * 4
-CODES_AT = V1_AT + ROW_BF16
-INV_AT = CODES_AT + (BLOCKS + B * EB) * P * 4
-K_PLANE0 = 8
+KB = 1024
+LAST_ROWS_AT = T * 4
+SCALES_AT = LAST_ROWS_AT + BLOCKS * DV * 4
 
 
 def tile_attend_rel2_gate_pgb2q256n512t2048_kernel(tc, q_words, q_scales, k_words, k_scales, vT, vs, og, offs, out):
@@ -45,48 +41,41 @@ def tile_attend_rel2_gate_pgb2q256n512t2048_kernel(tc, q_words, q_scales, k_word
         k_pool = [keep.tile([P, T], I32, name="k_pool%d" % o) for o in range(PASSES)]
         ks_pool = keep.tile([P, T], U8, name="ks_pool", align_bytes=64)
         vs_pool = keep.tile([P, T], F32, name="vs_pool")
-        v_pool = [keep.tile([P, T], F32, name="v_pool0"), placed([P, T], F32, "v_pool1", V1_AT)]
+        v_pool = [keep.tile([P, T], F32, name="v_pool0"), placed([P, T], F32, "v_pool1", 0)]
         q_codes = [keep.tile([P, B, NQ], I32, name="q_codes%d" % o, align_bytes=64) for o in range(PASSES)]
-        q_plane = keep.tile([P, NQ], U8, name="q_plane", align_bytes=64)
+        q_plane = keep.tile([P, B * PASSES, NQ], U8, name="q_plane", align_bytes=64)
         gate_in = [keep.tile([P, QB, DV], F32, name="gate_in%d" % b) for b in range(B)]
         ident = keep.tile([P, P], F32, name="ident")
         warm = keep.tile([P, 8], F32, name="warm")
         pos = keep.tile([P, BLOCKS, N + 8], F32, name="pos")
 
         nc.gpsimd.memset(ks_pool[:].bitcast(I32), 0)
-        nc.gpsimd.memset(q_plane[:].bitcast(I32), 0)
+        nc.gpsimd.memset(q_plane[:].rearrange("p g q -> p (g q)").bitcast(I32), 0)
         nc.gpsimd.memset(vs_pool[0 : P - 1, :], 0.0)
         make_identity(nc, ident[:])
-        nc.gpsimd.memset(pos[:, :, N + 1 : N + 4], 0.0)
         nc.gpsimd.memset(pos[:, :, N : N + 1], 1.0)
         nc.scalar.activation(warm[0:96, :], vs_pool[0:96, 0:8], ACT.Sigmoid)
-
-        def load_key_scales():
-            for quad in range(4):
-                nc.sync.dma_start(
-                    ks_pool[32 * quad + K_PLANE0 : 32 * quad + K_PLANE0 + 4 * PASSES, :].bitcast(I32),
-                    k_scales[:, 4 * quad : 4 * quad + 4, :].bitcast(I32),
-                )
-
-        def load_query_scales():
-            for quad in range(4):
-                nc.sync.dma_start(
-                    q_plane[32 * quad : 32 * quad + 4 * B * PASSES, :].bitcast(I32),
-                    q_scales.rearrange("b o f q -> (b o) f q")[:, 4 * quad : 4 * quad + 4, :].bitcast(I32),
-                )
-
-        def load_keys(o):
-            nc.sync.dma_start(k_pool[o][:], k_words[o].rearrange("p t r -> p (t r)").bitcast(I32))
 
         def load_queries(o):
             nc.sync.dma_start(q_codes[o][:], q_words[:, o].rearrange("b p q r -> p b (q r)").bitcast(I32))
 
+        def load_keys(o):
+            nc.sync.dma_start(k_pool[o][:], k_words[o].rearrange("p t r -> p (t r)").bitcast(I32))
+
         load_queries(0)
         nc.sync.dma_start(offsets[:], offs)
         nc.sync.dma_start(vs_pool[P - 1 : P, :], vs[0:1, :])
-        load_key_scales()
+        for quad in (2, 3, 0, 1):
+            nc.sync.dma_start(
+                ks_pool[32 * quad : 32 * quad + 4 * PASSES, :].bitcast(I32),
+                k_scales[:, 4 * quad : 4 * quad + 4, :].bitcast(I32),
+            )
         load_keys(0)
-        load_query_scales()
+        for r in range(4):
+            nc.sync.dma_start(
+                q_plane[r:P:32, :, :].bitcast(I32),
+                q_scales.rearrange("b o (c r) q -> r c (b o) q", r=4)[r].bitcast(I32),
+            )
         load_keys(1)
         load_queries(1)
         for h in range(EB):
@@ -102,110 +91,126 @@ def tile_attend_rel2_gate_pgb2q256n512t2048_kernel(tc, q_words, q_scales, k_word
         k_g = [keep.tile([P, B * N], U32, name="k_g%d" % o, align_bytes=64) for o in range(PASSES)]
         score_banks = [psum.tile([P, N], F32, name="score%d" % blk) for blk in range(BLOCKS)]
         turned = [psum.tile([P, 4, P], F32, name="turned%d" % blk) for blk in range(BLOCKS)]
-
-        vs_t = keep.tile([P, B, 1, 4], F32, name="vs_t")
+        vs_t = [placed([P, 1, 4], F32, "vs_t0", SCALES_AT), keep.tile([P, 1, 4], F32, name="vs_t1")]
         row_sum = keep.tile([P, BLOCKS], F32, name="row_sum")
-        w_codes = [placed([P, P], U32, "w_codes%d" % blk, CODES_AT + blk * P * 4) for blk in range(BLOCKS)]
+        inv_sum = keep.tile([P, BLOCKS], F32, name="inv_sum")
+        probs = [keep.tile([P, N + 8], F32, name="prob%d" % blk) for blk in range(BLOCKS)]
+        w_bf = [keep.tile([P, P, 4], BF16, name="w_bf%d" % blk, align_bytes=64) for blk in range(QB)]
+        w_bf.extend(placed([P, P, 4], BF16, "w_bf%d" % blk, blk * KB) for blk in range(QB, BLOCKS))
+        w_codes = [placed([P, P], U32, "w_codes0", SCALES_AT)]
+        w_codes.extend(keep.tile([P, P], U32, name="w_codes%d" % blk, align_bytes=64) for blk in range(1, BLOCKS))
         w_plane = [keep.tile([P, P], U8, name="w_plane%d" % blk, align_bytes=64) for blk in range(BLOCKS)]
-        v_codes = [placed([P, DV], U32, "v_codes%d" % b, CODES_AT + (BLOCKS + b * EB) * P * 4) for b in range(B)]
-        v_plane = [keep.tile([P, DV], U8, name="v_plane%d" % b, align_bytes=64) for b in range(B)]
-        probs = [placed([P, 4, P + 4], F32, "prob%d" % blk, blk * PROB_BYTES) for blk in range(BLOCKS)]
-        w_bf = [keep.tile([P, P, 4], BF16, name="w_bf%d" % blk, align_bytes=64) for blk in range(BLOCKS - 1)]
-        w_bf.append(placed([P, P, 4], BF16, "w_bf3", V1_AT))
-        v_bf = [
-            [keep.tile([P, N], BF16, name="v_bf00", align_bytes=64), placed([P, N], BF16, "v_bf01", PLACES_AT)],
-            [keep.tile([P, N], BF16, name="v_bf1%d" % h, align_bytes=64) for h in range(EB)],
-        ]
         v_g = [
-            [keep.tile([P, N], BF16, name="v_g%d0" % b), placed([P, N], BF16, "v_g%d1" % b, PROB_BYTES + b * ROW_BF16)]
-            for b in range(B)
+            [keep.tile([P, N], BF16, name="v_g0%d" % h) for h in range(EB)],
+            [keep.tile([P, N], BF16, name="v_g10"), placed([P, N], BF16, "v_g11", LAST_ROWS_AT)],
         ]
-        w_places = placed([P, 4, P], BF16, "w_places", PLACES_AT)
-        gate = placed([P, BLOCKS - 1, DV], F32, "gate", PROB_BYTES + ROW_BF16)
-        gates = [placed([P, DV], F32, "gate0", PROB_BYTES)[:]] + [gate[:, j, :] for j in range(BLOCKS - 1)]
-        inv_sum = placed([P, BLOCKS], F32, "inv_sum", INV_AT)
+        v_bf = [[placed([P, N], BF16, "v_bf%d0" % b, b * KB), keep.tile([P, N], BF16, name="v_bf%d1" % b, align_bytes=64)] for b in range(B)]
+        v_codes = [keep.tile([P, DV], U32, name="v_codes%d" % b, align_bytes=64) for b in range(B)]
+        v_plane = [keep.tile([P, DV], U8, name="v_plane%d" % b, align_bytes=64) for b in range(B)]
+        gates = placed([P, BLOCKS, DV], F32, "gates", LAST_ROWS_AT)
         result = [keep.tile([P, DV], F32, name="result%d" % blk) for blk in range(BLOCKS)]
-
-        def gather_keys(o, b):
-            nc.vector.tensor_copy(k_g[o][:, b * N : (b + 1) * N], k_pool[o][:].bitcast(U32).indirect(seq_list(b)))
-
-        def turn_token_scales(b):
-            for t in range(4):
-                nc.tensor.transpose(turned[b][:, t, :], vs_g[b][:, t, :], ident[:])
-            nc.scalar.copy(vs_t[:, b, 0, :], turned[b][:, :, P - 1])
 
         def scores(blk, o):
             b, j = divmod(blk, QB)
             nc.tensor.matmul_mx(
                 out=score_banks[blk][:],
                 lhsT=q_codes[o][:, b, j * P : (j + 1) * P].bitcast(FP8X4),
-                lhsT_scale=q_plane[4 * (b * PASSES + o) : P, j * P : (j + 1) * P],
+                lhsT_scale=q_plane[:, b * PASSES + o, j * P : (j + 1) * P],
                 rhs=k_g[o][:, b * N : (b + 1) * N].bitcast(FP8X4),
-                rhs_scale=ks_g[K_PLANE0 + 4 * o : P, b * N : (b + 1) * N],
+                rhs_scale=ks_g[4 * o : P, b * N : (b + 1) * N],
                 start=(o == 0),
                 stop=(o == PASSES - 1),
             )
 
-        def positive_part_on_scalar(blk):
-            nc.scalar.activation(pos[:, blk, 0:N], score_banks[blk][:], ACT.Relu)
-
-        def positive_part_on_vector(blk):
-            nc.vector.tensor_scalar_max(pos[:, blk, 0:N], score_banks[blk][:], 0.0)
-
-        def square(blk):
+        def square_and_turn(blk):
             nc.scalar.activation(
-                probs[blk][:, :, 0 : P + 1].rearrange("p t m -> p m t"),
-                pos[:, blk, 0 : N + 4].rearrange("p (m t) -> p m t", t=4),
+                probs[blk][:, 0 : N + 1],
+                pos[:, blk, 0 : N + 1],
                 ACT.Square,
                 accum_out=row_sum[:, blk : blk + 1],
             )
-
-        def turn_probs(blk):
             for t in range(4):
-                nc.tensor.transpose(turned[blk][:, t, :], probs[blk][:, t, 0:P], ident[:])
+                nc.tensor.transpose(turned[blk][:, t, :], probs[blk][:, t * P : (t + 1) * P], ident[:])
 
         def weights(blk):
             nc.vector.tensor_tensor(
                 w_bf[blk][:],
                 turned[blk][:].rearrange("p t q -> p q t"),
-                vs_t[:, blk // QB, :, :].to_broadcast([P, P, 4]),
+                vs_t[blk // QB][:].to_broadcast([P, P, 4]),
                 ALU.mult,
             )
 
-        def weights_on_scalar(blk):
-            for t in range(4):
-                nc.scalar.activation(w_places[:, t, :], turned[blk][:, t, :], ACT.Copy, scale=vs_t[:, blk // QB, 0, t : t + 1])
-            nc.scalar.copy(w_bf[blk][:], w_places[:].rearrange("p t q -> p q t"))
+        def gather_values(b, h):
+            window = v_pool[h][:].indirect(seq_list(b))
+            if b == 0:
+                nc.vector.tensor_copy(v_g[b][h][:].rearrange("p (u m e) -> p m u e", u=2, e=2), window)
+            else:
+                nc.scalar.activation(v_g[b][h][:], window, ACT.Copy)
+
+        def turn_values(b, h):
+            bank = turned[b][:, 0:2, :] if h == 0 else score_banks[QB + b][:, 0 : 2 * P].rearrange("p (u e) -> p u e", u=2)
+            words = v_g[b][h][:].bitcast(F32)
+            for u in range(2):
+                nc.tensor.transpose(bank[:, u, :], words[:, u * P : (u + 1) * P] if b == 0 else words[:, u : 2 * P : 2], ident[:])
+            nc.scalar.copy(v_bf[b][h][:].bitcast(F32).rearrange("p (e u) -> p e u", u=2), bank.rearrange("p u e -> p e u"))
 
         def quantise_weights(blk):
             nc.vector.quantize_mx(
                 out=w_codes[blk][:].bitcast(FP8X4), scales=w_plane[blk][:], in_=w_bf[blk][:].rearrange("p q t -> p (q t)")
             )
 
-        def gather_values(b, h):
-            nc.vector.tensor_copy(v_g[b][h][:].rearrange("p (u m e) -> p m u e", u=2, e=2), v_pool[h][:].indirect(seq_list(b)))
-
-        def turn_values(b, h):
-            bank = score_banks[h * B + b][:, 0 : 2 * P].rearrange("p (u e) -> p u e", u=2)
-            for u in range(2):
-                nc.tensor.transpose(bank[:, u, :], v_g[b][h][:].bitcast(F32)[:, u * P : (u + 1) * P], ident[:])
-            nc.scalar.copy(v_bf[b][h][:].bitcast(F32).rearrange("p (e u) -> p e u", u=2), bank.rearrange("p u e -> p e u"))
-
         def quantise_values(b, h):
             cols = slice(h * P, (h + 1) * P)
             nc.vector.quantize_mx(out=v_codes[b][:, cols].bitcast(FP8X4), scales=v_plane[b][:, cols], in_=v_bf[b][h][:])
 
-        def row_factor():
-            nc.vector.reciprocal(inv_sum[:], row_sum[:])
-
-        def sigmoid(blk):
-            b, j = divmod(blk, QB)
-            nc.scalar.activation(gates[blk], gate_in[b][:, j, :], ACT.Sigmoid)
-
         def sums_of(blk):
-            return turned[blk][:, 0:EB, :].rearrange("p h e -> p (h e)")
+            return score_banks[blk][:, 0:DV] if blk < QB else turned[blk - QB][:, 0:EB, :].rearrange("p h e -> p (h e)")
 
-        def product(blk):
+        for b in range(B):
+            nc.vector.tensor_copy(vs_g[b][:].bitcast(U32).rearrange("p t m -> p m t"), vs_pool[:].bitcast(U32).indirect(seq_list(b)))
+        nc.vector.tensor_copy(ks_g[:].rearrange("p (b t m) -> p b m t", b=B, t=4), ks_pool[:].indirect(offsets[:]))
+        for o in range(PASSES):
+            for b in range(B):
+                nc.vector.tensor_copy(k_g[o][:, b * N : (b + 1) * N].rearrange("p (t m) -> p m t", t=4), k_pool[o][:].bitcast(U32).indirect(seq_list(b)))
+        for b in range(B):
+            for t in range(4):
+                nc.tensor.transpose(turned[b][:, t, :], vs_g[b][:, t, :], ident[:])
+            nc.scalar.copy(vs_t[b][:, 0, :], turned[b][:, :, P - 1])
+        for o in range(PASSES):
+            for blk in range(BLOCKS):
+                scores(blk, o)
+
+        for blk in range(BLOCKS):
+            if blk == 1:
+                nc.scalar.activation(pos[:, blk, 0:N], score_banks[blk][:], ACT.Relu)
+            else:
+                nc.vector.tensor_scalar_max(pos[:, blk, 0:N], score_banks[blk][:], 0.0)
+        gather_values(0, 0)
+        for blk in range(BLOCKS):
+            square_and_turn(blk)
+        gather_values(1, 0)
+        for blk in range(QB):
+            weights(blk)
+        for blk in range(QB):
+            quantise_weights(blk)
+        nc.vector.reciprocal(inv_sum[:], row_sum[:])
+        for b in range(B):
+            gather_values(b, 1)
+        for blk in range(QB, BLOCKS):
+            weights(blk)
+        for h in range(EB):
+            for b in range(B):
+                turn_values(b, h)
+        quantise_values(0, 0)
+        quantise_weights(2)
+        quantise_values(1, 0)
+        quantise_values(0, 1)
+        quantise_weights(3)
+        quantise_values(1, 1)
+        for blk in range(BLOCKS):
+            b, j = divmod(blk, QB)
+            nc.scalar.activation(gates[:, blk, :], gate_in[b][:, j, :], ACT.Sigmoid)
+        for blk in range(BLOCKS):
             b = blk // QB
             nc.tensor.matmul_mx(
                 out=sums_of(blk),
@@ -216,54 +221,7 @@ def tile_attend_rel2_gate_pgb2q256n512t2048_kernel(tc, q_words, q_scales, k_word
                 start=True,
                 stop=True,
             )
-
-        def finish(blk):
-            nc.vector.scalar_tensor_tensor(result[blk][:], sums_of(blk), inv_sum[:, blk : blk + 1], gates[blk], ALU.mult, ALU.mult)
-
-        def store(blk):
+        for blk in range(BLOCKS):
             b, j = divmod(blk, QB)
+            nc.vector.scalar_tensor_tensor(result[blk][:], sums_of(blk), inv_sum[:, blk : blk + 1], gates[:, blk, :], ALU.mult, ALU.mult)
             nc.sync.dma_start(out[b, j * P : (j + 1) * P, :], result[blk][:])
-
-        for b in range(B):
-            nc.vector.tensor_copy(vs_g[b][:].bitcast(U32).rearrange("p t m -> p m t"), vs_pool[:].bitcast(U32).indirect(seq_list(b)))
-        nc.vector.tensor_copy(ks_g[:], ks_pool[:].indirect(offsets[:]))
-        for o in range(PASSES):
-            for b in range(B):
-                gather_keys(o, b)
-        for b in range(B):
-            turn_token_scales(b)
-        for o in range(PASSES):
-            for blk in range(BLOCKS):
-                scores(blk, o)
-
-        positive_part_on_vector(0)
-        positive_part_on_scalar(1)
-        for blk in range(2, BLOCKS):
-            positive_part_on_vector(blk)
-        for b in range(B):
-            gather_values(b, 0)
-        for blk in range(BLOCKS):
-            square(blk)
-            turn_probs(blk)
-        weights(0)
-        weights(1)
-        for b in range(B):
-            gather_values(b, 1)
-            turn_values(b, 0)
-        weights_on_scalar(2)
-        for b in range(B):
-            turn_values(b, 1)
-        weights(3)
-        for b in range(B):
-            for j in range(QB):
-                quantise_values(b, j)
-                quantise_weights(b * QB + j)
-            if b == 0:
-                row_factor()
-        for blk in range(BLOCKS):
-            sigmoid(blk)
-        for blk in range(BLOCKS):
-            product(blk)
-        for blk in range(BLOCKS):
-            finish(blk)
-            store(blk)

@@ -53,6 +53,7 @@ def tile_attend_rel2_gate_pgb2q256n512t2048_kernel(tc, q_words, q_scales, k_word
         nc.gpsimd.memset(q_plane[:].rearrange("p g q -> p (g q)").bitcast(I32), 0)
         nc.gpsimd.memset(vs_pool[0 : P - 1, :], 0.0)
         make_identity(nc, ident[:])
+        nc.gpsimd.memset(pos[:, :, N + 1 : N + 4], 0.0)
         nc.gpsimd.memset(pos[:, :, N : N + 1], 1.0)
         nc.scalar.activation(warm[0:96, :], vs_pool[0:96, 0:8], ACT.Sigmoid)
 
@@ -94,7 +95,7 @@ def tile_attend_rel2_gate_pgb2q256n512t2048_kernel(tc, q_words, q_scales, k_word
         vs_t = [placed([P, 1, 4], F32, "vs_t0", SCALES_AT), keep.tile([P, 1, 4], F32, name="vs_t1")]
         row_sum = keep.tile([P, BLOCKS], F32, name="row_sum")
         inv_sum = keep.tile([P, BLOCKS], F32, name="inv_sum")
-        probs = [keep.tile([P, N + 8], F32, name="prob%d" % blk) for blk in range(BLOCKS)]
+        probs = [keep.tile([P, 4, P + 4], F32, name="prob%d" % blk) for blk in range(BLOCKS)]
         w_bf = [keep.tile([P, P, 4], BF16, name="w_bf%d" % blk, align_bytes=64) for blk in range(QB)]
         w_bf.extend(placed([P, P, 4], BF16, "w_bf%d" % blk, blk * KB) for blk in range(QB, BLOCKS))
         w_codes = [placed([P, P], U32, "w_codes0", SCALES_AT)]
@@ -124,13 +125,13 @@ def tile_attend_rel2_gate_pgb2q256n512t2048_kernel(tc, q_words, q_scales, k_word
 
         def square_and_turn(blk):
             nc.scalar.activation(
-                probs[blk][:, 0 : N + 1],
-                pos[:, blk, 0 : N + 1],
+                probs[blk][:, :, 0 : P + 1].rearrange("p t m -> p m t"),
+                pos[:, blk, 0 : N + 4].rearrange("p (m t) -> p m t", t=4),
                 ACT.Square,
                 accum_out=row_sum[:, blk : blk + 1],
             )
             for t in range(4):
-                nc.tensor.transpose(turned[blk][:, t, :], probs[blk][:, t * P : (t + 1) * P], ident[:])
+                nc.tensor.transpose(turned[blk][:, t, :], probs[blk][:, t, 0:P], ident[:])
 
         def weights(blk):
             nc.vector.tensor_tensor(
@@ -168,10 +169,10 @@ def tile_attend_rel2_gate_pgb2q256n512t2048_kernel(tc, q_words, q_scales, k_word
 
         for b in range(B):
             nc.vector.tensor_copy(vs_g[b][:].bitcast(U32).rearrange("p t m -> p m t"), vs_pool[:].bitcast(U32).indirect(seq_list(b)))
-        nc.vector.tensor_copy(ks_g[:].rearrange("p (b t m) -> p b m t", b=B, t=4), ks_pool[:].indirect(offsets[:]))
+        nc.vector.tensor_copy(ks_g[:], ks_pool[:].indirect(offsets[:]))
         for o in range(PASSES):
             for b in range(B):
-                nc.vector.tensor_copy(k_g[o][:, b * N : (b + 1) * N].rearrange("p (t m) -> p m t", t=4), k_pool[o][:].bitcast(U32).indirect(seq_list(b)))
+                nc.vector.tensor_copy(k_g[o][:, b * N : (b + 1) * N], k_pool[o][:].bitcast(U32).indirect(seq_list(b)))
         for b in range(B):
             for t in range(4):
                 nc.tensor.transpose(turned[b][:, t, :], vs_g[b][:, t, :], ident[:])

@@ -24,7 +24,8 @@ EB = DV // P
 LIST_COLS = N // 16
 KB = 1024
 LAST_ROWS_AT = T * 4
-SCALES_AT = LAST_ROWS_AT + BLOCKS * DV * 4
+THIRD_ROWS_AT = LAST_ROWS_AT + BLOCKS * DV * 4
+PLACES_AT = THIRD_ROWS_AT + KB
 
 
 def tile_attend_rel2_gate_pgb2q256n512t2048_kernel(tc, q_words, q_scales, k_words, k_scales, vT, vs, og, offs, out):
@@ -92,21 +93,24 @@ def tile_attend_rel2_gate_pgb2q256n512t2048_kernel(tc, q_words, q_scales, k_word
         k_g = [keep.tile([P, B * N], U32, name="k_g%d" % o, align_bytes=64) for o in range(PASSES)]
         score_banks = [psum.tile([P, N], F32, name="score%d" % blk) for blk in range(BLOCKS)]
         turned = [psum.tile([P, 4, P], F32, name="turned%d" % blk) for blk in range(BLOCKS)]
-        vs_t = [placed([P, 1, 4], F32, "vs_t0", SCALES_AT), keep.tile([P, 1, 4], F32, name="vs_t1")]
+        vs_t = [keep.tile([P, 1, 4], F32, name="vs_t%d" % b) for b in range(B)]
         row_sum = keep.tile([P, BLOCKS], F32, name="row_sum")
-        inv_sum = keep.tile([P, BLOCKS], F32, name="inv_sum")
+        inv_sum = placed([P, BLOCKS], F32, "inv_sum", 5 * KB)
         probs = [keep.tile([P, 4, P + 4], F32, name="prob%d" % blk) for blk in range(BLOCKS)]
-        w_bf = [keep.tile([P, P, 4], BF16, name="w_bf%d" % blk, align_bytes=64) for blk in range(QB)]
-        w_bf.extend(placed([P, P, 4], BF16, "w_bf%d" % blk, blk * KB) for blk in range(QB, BLOCKS))
-        w_codes = [placed([P, P], U32, "w_codes0", SCALES_AT)]
-        w_codes.extend(keep.tile([P, P], U32, name="w_codes%d" % blk, align_bytes=64) for blk in range(1, BLOCKS))
+        w_bf = [keep.tile([P, P, 4], BF16, name="w_bf%d" % blk, align_bytes=64) for blk in range(BLOCKS - 1)]
+        w_bf.append(placed([P, P, 4], BF16, "w_bf3", 0))
+        w_codes = [placed([P, P], U32, "w_codes%d" % blk, KB + blk * P * 4) for blk in range(BLOCKS)]
         w_plane = [keep.tile([P, P], U8, name="w_plane%d" % blk, align_bytes=64) for blk in range(BLOCKS)]
+        w_places = placed([P, 4, P], BF16, "w_places", PLACES_AT)
         v_g = [
-            [keep.tile([P, N], BF16, name="v_g0%d" % h) for h in range(EB)],
+            [keep.tile([P, N], BF16, name="v_g00"), placed([P, N], BF16, "v_g01", THIRD_ROWS_AT)],
             [keep.tile([P, N], BF16, name="v_g10"), placed([P, N], BF16, "v_g11", LAST_ROWS_AT)],
         ]
-        v_bf = [[placed([P, N], BF16, "v_bf%d0" % b, b * KB), keep.tile([P, N], BF16, name="v_bf%d1" % b, align_bytes=64)] for b in range(B)]
-        v_codes = [keep.tile([P, DV], U32, name="v_codes%d" % b, align_bytes=64) for b in range(B)]
+        v_bf = [
+            [keep.tile([P, N], BF16, name="v_bf00", align_bytes=64), placed([P, N], BF16, "v_bf01", PLACES_AT)],
+            [placed([P, N], BF16, "v_bf10", THIRD_ROWS_AT), keep.tile([P, N], BF16, name="v_bf11", align_bytes=64)],
+        ]
+        v_codes = [placed([P, DV], U32, "v_codes%d" % b, (3 + b) * KB) for b in range(B)]
         v_plane = [keep.tile([P, DV], U8, name="v_plane%d" % b, align_bytes=64) for b in range(B)]
         gates = placed([P, BLOCKS, DV], F32, "gates", LAST_ROWS_AT)
         result = [keep.tile([P, DV], F32, name="result%d" % blk) for blk in range(BLOCKS)]
@@ -142,18 +146,22 @@ def tile_attend_rel2_gate_pgb2q256n512t2048_kernel(tc, q_words, q_scales, k_word
             )
 
         def gather_values(b, h):
-            window = v_pool[h][:].indirect(seq_list(b))
-            if b == 0:
-                nc.vector.tensor_copy(v_g[b][h][:].rearrange("p (u m e) -> p m u e", u=2, e=2), window)
-            else:
-                nc.scalar.activation(v_g[b][h][:], window, ACT.Copy)
+            nc.vector.tensor_copy(v_g[b][h][:].rearrange("p (u m e) -> p m u e", u=2, e=2), v_pool[h][:].indirect(seq_list(b)))
+
+        def weights_on_scalar(blk):
+            for t in range(4):
+                nc.scalar.activation(w_places[:, t, :], turned[blk][:, t, :], ACT.Copy, scale=vs_t[blk // QB][:, 0, t : t + 1])
+            nc.scalar.copy(w_bf[blk][:], w_places[:].rearrange("p t q -> p q t"))
+
+        def value_bank(b, h):
+            return turned[b][:, 0:2, :] if h == 0 else score_banks[QB + b][:, 0 : 2 * P].rearrange("p (u e) -> p u e", u=2)
 
         def turn_values(b, h):
-            bank = turned[b][:, 0:2, :] if h == 0 else score_banks[QB + b][:, 0 : 2 * P].rearrange("p (u e) -> p u e", u=2)
-            words = v_g[b][h][:].bitcast(F32)
             for u in range(2):
-                nc.tensor.transpose(bank[:, u, :], words[:, u * P : (u + 1) * P] if b == 0 else words[:, u : 2 * P : 2], ident[:])
-            nc.scalar.copy(v_bf[b][h][:].bitcast(F32).rearrange("p (e u) -> p e u", u=2), bank.rearrange("p u e -> p e u"))
+                nc.tensor.transpose(value_bank(b, h)[:, u, :], v_g[b][h][:].bitcast(F32)[:, u * P : (u + 1) * P], ident[:])
+
+        def copy_values(b, h):
+            nc.scalar.copy(v_bf[b][h][:].bitcast(F32).rearrange("p (e u) -> p e u", u=2), value_bank(b, h).rearrange("p u e -> p e u"))
 
         def quantise_weights(blk):
             nc.vector.quantize_mx(
@@ -186,27 +194,31 @@ def tile_attend_rel2_gate_pgb2q256n512t2048_kernel(tc, q_words, q_scales, k_word
                 nc.scalar.activation(pos[:, blk, 0:N], score_banks[blk][:], ACT.Relu)
             else:
                 nc.vector.tensor_scalar_max(pos[:, blk, 0:N], score_banks[blk][:], 0.0)
-        gather_values(0, 0)
+        for b in range(B):
+            gather_values(b, 0)
         for blk in range(BLOCKS):
             square_and_turn(blk)
-        gather_values(1, 0)
         for blk in range(QB):
             weights(blk)
-        for blk in range(QB):
-            quantise_weights(blk)
-        nc.vector.reciprocal(inv_sum[:], row_sum[:])
         for b in range(B):
             gather_values(b, 1)
-        for blk in range(QB, BLOCKS):
-            weights(blk)
+        weights(3)
         for h in range(EB):
             for b in range(B):
                 turn_values(b, h)
-        quantise_values(0, 0)
-        quantise_weights(2)
-        quantise_values(1, 0)
-        quantise_values(0, 1)
+        copy_values(0, 0)
+        weights_on_scalar(2)
+        copy_values(0, 1)
+        for h in range(EB):
+            copy_values(1, h)
+        for j in range(QB):
+            quantise_weights(j)
+        for h in range(EB):
+            quantise_values(0, h)
+        nc.vector.reciprocal(inv_sum[:], row_sum[:])
         quantise_weights(3)
+        quantise_values(1, 0)
+        quantise_weights(2)
         quantise_values(1, 1)
         for blk in range(BLOCKS):
             b, j = divmod(blk, QB)

@@ -185,6 +185,15 @@ def tile_attend_rel2_gate_pgb2q256n512t2048_kernel(tc, q_words, q_scales, k_word
             for t in range(4):
                 nc.tensor.transpose(turned[b][:, t, :], vs_g[b][:, t, :], ident[:])
             nc.scalar.copy(vs_t[b][:, 0, :], turned[b][:, :, P - 1])
+        nc.tensor.matmul_mx(
+            out=turned[BLOCKS - 1][:].rearrange("p t q -> p (t q)"),
+            lhsT=q_codes[0][:, 0, 0:P].bitcast(FP8X4),
+            lhsT_scale=q_plane[:, 0, 0:P],
+            rhs=q_codes[0][:].rearrange("p b q -> p (b q)").bitcast(FP8X4),
+            rhs_scale=q_plane[:, 0:B, :].rearrange("p g q -> p (g q)"),
+            start=True,
+            stop=True,
+        )
         for o in range(PASSES):
             for blk in range(BLOCKS):
                 scores(blk, o)

@@ -24,8 +24,6 @@ EB = DV // P
 LIST_COLS = N // 16
 KB = 1024
 LAST_ROWS_AT = T * 4
-THIRD_ROWS_AT = LAST_ROWS_AT + BLOCKS * DV * 4
-PLACES_AT = THIRD_ROWS_AT + KB
 
 
 def tile_attend_rel2_gate_pgb2q256n512t2048_kernel(tc, q_words, q_scales, k_words, k_scales, vT, vs, og, offs, out):
@@ -54,7 +52,6 @@ def tile_attend_rel2_gate_pgb2q256n512t2048_kernel(tc, q_words, q_scales, k_word
         nc.gpsimd.memset(q_plane[:].rearrange("p g q -> p (g q)").bitcast(I32), 0)
         nc.gpsimd.memset(vs_pool[0 : P - 1, :], 0.0)
         make_identity(nc, ident[:])
-        nc.gpsimd.memset(pos[:, :, N + 1 : N + 4], 0.0)
         nc.gpsimd.memset(pos[:, :, N : N + 1], 1.0)
         nc.scalar.activation(warm[0:96, :], vs_pool[0:96, 0:8], ACT.Sigmoid)
 
@@ -85,33 +82,33 @@ def tile_attend_rel2_gate_pgb2q256n512t2048_kernel(tc, q_words, q_scales, k_word
         for b in range(B):
             nc.sync.dma_start(gate_in[b][:], og[b].rearrange("(j p) e -> p j e", p=P))
 
-        def seq_list(b):
-            return offsets[:, b * LIST_COLS : (b + 1) * LIST_COLS]
+        def slots(b, first=0, count=N):
+            at = b * LIST_COLS + first // 16
+            return offsets[:, at : at + count // 16]
 
-        ks_g = keep.tile([P, B * N], U8, name="ks_g", align_bytes=64)
+        ks_g = keep.tile([P, B, 4, P], U8, name="ks_g", align_bytes=64)
         vs_g = [keep.tile([P, 4, P], F32, name="vs_g%d" % b) for b in range(B)]
-        k_g = [keep.tile([P, B * N], U32, name="k_g%d" % o, align_bytes=64) for o in range(PASSES)]
+        k_g = [keep.tile([P, B, 4, P], U32, name="k_g%d" % o, align_bytes=64) for o in range(PASSES)]
         score_banks = [psum.tile([P, N], F32, name="score%d" % blk) for blk in range(BLOCKS)]
         turned = [psum.tile([P, 4, P], F32, name="turned%d" % blk) for blk in range(BLOCKS)]
         vs_t = [keep.tile([P, 1, 4], F32, name="vs_t%d" % b) for b in range(B)]
         row_sum = keep.tile([P, BLOCKS], F32, name="row_sum")
-        inv_sum = placed([P, BLOCKS], F32, "inv_sum", 5 * KB)
-        probs = [keep.tile([P, 4, P + 4], F32, name="prob%d" % blk) for blk in range(BLOCKS)]
+        probs = [keep.tile([P, N + 8], F32, name="prob%d" % blk) for blk in range(BLOCKS)]
         w_bf = [keep.tile([P, P, 4], BF16, name="w_bf%d" % blk, align_bytes=64) for blk in range(BLOCKS - 1)]
         w_bf.append(placed([P, P, 4], BF16, "w_bf3", 0))
         w_codes = [placed([P, P], U32, "w_codes%d" % blk, KB + blk * P * 4) for blk in range(BLOCKS)]
         w_plane = [keep.tile([P, P], U8, name="w_plane%d" % blk, align_bytes=64) for blk in range(BLOCKS)]
-        w_places = placed([P, 4, P], BF16, "w_places", PLACES_AT)
-        v_g = [
-            [keep.tile([P, N], BF16, name="v_g00"), placed([P, N], BF16, "v_g01", THIRD_ROWS_AT)],
-            [keep.tile([P, N], BF16, name="v_g10"), placed([P, N], BF16, "v_g11", LAST_ROWS_AT)],
-        ]
-        v_bf = [
-            [keep.tile([P, N], BF16, name="v_bf00", align_bytes=64), placed([P, N], BF16, "v_bf01", PLACES_AT)],
-            [placed([P, N], BF16, "v_bf10", THIRD_ROWS_AT), keep.tile([P, N], BF16, name="v_bf11", align_bytes=64)],
-        ]
         v_codes = [placed([P, DV], U32, "v_codes%d" % b, (3 + b) * KB) for b in range(B)]
         v_plane = [keep.tile([P, DV], U8, name="v_plane%d" % b, align_bytes=64) for b in range(B)]
+        v_g = [
+            [keep.tile([P, 2, P, 2], BF16, name="v_g00"), keep.tile([P, 2, P, 2], BF16, name="v_g01")],
+            [keep.tile([P, 2, P, 2], BF16, name="v_g10"), placed([P, 2, P, 2], BF16, "v_g11", LAST_ROWS_AT)],
+        ]
+        v_bf = [
+            [placed([P, N], BF16, "v_bf%d0" % b, (5 + b) * KB), keep.tile([P, N], BF16, name="v_bf%d1" % b, align_bytes=64)]
+            for b in range(B)
+        ]
+        inv_sum = placed([P, BLOCKS], F32, "inv_sum", 7 * KB)
         gates = placed([P, BLOCKS, DV], F32, "gates", LAST_ROWS_AT)
         result = [keep.tile([P, DV], F32, name="result%d" % blk) for blk in range(BLOCKS)]
 
@@ -121,21 +118,16 @@ def tile_attend_rel2_gate_pgb2q256n512t2048_kernel(tc, q_words, q_scales, k_word
                 out=score_banks[blk][:],
                 lhsT=q_codes[o][:, b, j * P : (j + 1) * P].bitcast(FP8X4),
                 lhsT_scale=q_plane[:, b * PASSES + o, j * P : (j + 1) * P],
-                rhs=k_g[o][:, b * N : (b + 1) * N].bitcast(FP8X4),
-                rhs_scale=ks_g[4 * o : P, b * N : (b + 1) * N],
+                rhs=k_g[o][:, b].rearrange("p t m -> p (t m)").bitcast(FP8X4),
+                rhs_scale=ks_g[4 * o : P, b].rearrange("p t m -> p (t m)"),
                 start=(o == 0),
                 stop=(o == PASSES - 1),
             )
 
         def square_and_turn(blk):
-            nc.scalar.activation(
-                probs[blk][:, :, 0 : P + 1].rearrange("p t m -> p m t"),
-                pos[:, blk, 0 : N + 4].rearrange("p (m t) -> p m t", t=4),
-                ACT.Square,
-                accum_out=row_sum[:, blk : blk + 1],
-            )
+            nc.scalar.activation(probs[blk][:, 0 : N + 1], pos[:, blk, 0 : N + 1], ACT.Square, accum_out=row_sum[:, blk : blk + 1])
             for t in range(4):
-                nc.tensor.transpose(turned[blk][:, t, :], probs[blk][:, t, 0:P], ident[:])
+                nc.tensor.transpose(turned[blk][:, t, :], probs[blk][:, t * P : (t + 1) * P], ident[:])
 
         def weights(blk):
             nc.vector.tensor_tensor(
@@ -145,20 +137,22 @@ def tile_attend_rel2_gate_pgb2q256n512t2048_kernel(tc, q_words, q_scales, k_word
                 ALU.mult,
             )
 
-        def gather_values(b, h):
-            nc.vector.tensor_copy(v_g[b][h][:].rearrange("p (u m e) -> p m u e", u=2, e=2), v_pool[h][:].indirect(seq_list(b)))
+        def value_rows(b, h, first, count):
+            return v_g[b][h][:, :, first // 4 : (first + count) // 4, :].rearrange("p u m e -> p m u e")
 
-        def weights_on_scalar(blk):
-            for t in range(4):
-                nc.scalar.activation(w_places[:, t, :], turned[blk][:, t, :], ACT.Copy, scale=vs_t[blk // QB][:, 0, t : t + 1])
-            nc.scalar.copy(w_bf[blk][:], w_places[:].rearrange("p t q -> p q t"))
+        def gather_values_on_vector(b, h, first, count):
+            nc.vector.tensor_copy(value_rows(b, h, first, count), v_pool[h][:].indirect(slots(b, first, count)))
+
+        def gather_values_on_scalar(b, h, first, count):
+            nc.scalar.activation(value_rows(b, h, first, count), v_pool[h][:].indirect(slots(b, first, count)), ACT.Copy)
 
         def value_bank(b, h):
-            return turned[b][:, 0:2, :] if h == 0 else score_banks[QB + b][:, 0 : 2 * P].rearrange("p (u e) -> p u e", u=2)
+            return turned[b][:, 0:2, :] if h == 0 else score_banks[b][:, 0 : 2 * P].rearrange("p (u e) -> p u e", u=2)
 
         def turn_values(b, h):
             for u in range(2):
-                nc.tensor.transpose(value_bank(b, h)[:, u, :], v_g[b][h][:].bitcast(F32)[:, u * P : (u + 1) * P], ident[:])
+                words = v_g[b][h][:, u].rearrange("p m e -> p (m e)").bitcast(F32)
+                nc.tensor.transpose(value_bank(b, h)[:, u, :], words, ident[:])
 
         def copy_values(b, h):
             nc.scalar.copy(v_bf[b][h][:].bitcast(F32).rearrange("p (e u) -> p e u", u=2), value_bank(b, h).rearrange("p u e -> p e u"))
@@ -173,14 +167,14 @@ def tile_attend_rel2_gate_pgb2q256n512t2048_kernel(tc, q_words, q_scales, k_word
             nc.vector.quantize_mx(out=v_codes[b][:, cols].bitcast(FP8X4), scales=v_plane[b][:, cols], in_=v_bf[b][h][:])
 
         def sums_of(blk):
-            return score_banks[blk][:, 0:DV] if blk < QB else turned[blk - QB][:, 0:EB, :].rearrange("p h e -> p (h e)")
+            return score_banks[QB + blk][:, 0:DV] if blk < QB else turned[blk - QB][:, 0:EB, :].rearrange("p h e -> p (h e)")
 
         for b in range(B):
-            nc.vector.tensor_copy(vs_g[b][:].bitcast(U32).rearrange("p t m -> p m t"), vs_pool[:].bitcast(U32).indirect(seq_list(b)))
-        nc.vector.tensor_copy(ks_g[:], ks_pool[:].indirect(offsets[:]))
+            nc.vector.tensor_copy(vs_g[b][:].bitcast(U32).rearrange("p t m -> p m t"), vs_pool[:].bitcast(U32).indirect(slots(b)))
+        nc.vector.tensor_copy(ks_g[:].rearrange("p b t m -> p b m t"), ks_pool[:].indirect(offsets[:]))
         for o in range(PASSES):
             for b in range(B):
-                nc.vector.tensor_copy(k_g[o][:, b * N : (b + 1) * N], k_pool[o][:].bitcast(U32).indirect(seq_list(b)))
+                nc.vector.tensor_copy(k_g[o][:, b].rearrange("p t m -> p m t"), k_pool[o][:].bitcast(U32).indirect(slots(b)))
         for b in range(B):
             for t in range(4):
                 nc.tensor.transpose(turned[b][:, t, :], vs_g[b][:, t, :], ident[:])
@@ -203,31 +197,30 @@ def tile_attend_rel2_gate_pgb2q256n512t2048_kernel(tc, q_words, q_scales, k_word
                 nc.scalar.activation(pos[:, blk, 0:N], score_banks[blk][:], ACT.Relu)
             else:
                 nc.vector.tensor_scalar_max(pos[:, blk, 0:N], score_banks[blk][:], 0.0)
-        for b in range(B):
-            gather_values(b, 0)
+        gather_values_on_vector(0, 0, 0, N)
         for blk in range(BLOCKS):
             square_and_turn(blk)
-        for blk in range(QB):
+        gather_values_on_scalar(1, 0, 0, N)
+        for blk in range(BLOCKS - 1):
             weights(blk)
         for b in range(B):
-            gather_values(b, 1)
-        weights(3)
+            gather_values_on_vector(b, 1, 0, N // 2)
+            gather_values_on_scalar(b, 1, N // 2, N // 2)
+        weights(BLOCKS - 1)
         for h in range(EB):
             for b in range(B):
                 turn_values(b, h)
-        copy_values(0, 0)
-        weights_on_scalar(2)
-        copy_values(0, 1)
-        for h in range(EB):
-            copy_values(1, h)
+        for b in range(B):
+            for h in range(EB):
+                copy_values(b, h)
         for j in range(QB):
             quantise_weights(j)
         for h in range(EB):
             quantise_values(0, h)
         nc.vector.reciprocal(inv_sum[:], row_sum[:])
-        quantise_weights(3)
-        quantise_values(1, 0)
         quantise_weights(2)
+        quantise_values(1, 0)
+        quantise_weights(3)
         quantise_values(1, 1)
         for blk in range(BLOCKS):
             b, j = divmod(blk, QB)

@@ -24,6 +24,8 @@ EB = DV // P
 LIST_COLS = N // 16
 KB = 1024
 LAST_ROWS_AT = T * 4
+THIRD_ROWS_AT = LAST_ROWS_AT + BLOCKS * DV * 4
+SECOND_ROWS_AT = THIRD_ROWS_AT + KB
 
 
 def tile_attend_rel2_gate_pgb2q256n512t2048_kernel(tc, q_words, q_scales, k_words, k_scales, vT, vs, og, offs, out):
@@ -95,18 +97,18 @@ def tile_attend_rel2_gate_pgb2q256n512t2048_kernel(tc, q_words, q_scales, k_word
         row_sum = keep.tile([P, BLOCKS], F32, name="row_sum")
         probs = [keep.tile([P, N + 8], F32, name="prob%d" % blk) for blk in range(BLOCKS)]
         w_bf = [keep.tile([P, P, 4], BF16, name="w_bf%d" % blk, align_bytes=64) for blk in range(BLOCKS - 1)]
-        w_bf.append(placed([P, P, 4], BF16, "w_bf3", 0))
+        w_bf.append(placed([P, P, 4], BF16, "w_bf3", THIRD_ROWS_AT))
         w_codes = [placed([P, P], U32, "w_codes%d" % blk, KB + blk * P * 4) for blk in range(BLOCKS)]
         w_plane = [keep.tile([P, P], U8, name="w_plane%d" % blk, align_bytes=64) for blk in range(BLOCKS)]
         v_codes = [placed([P, DV], U32, "v_codes%d" % b, (3 + b) * KB) for b in range(B)]
         v_plane = [keep.tile([P, DV], U8, name="v_plane%d" % b, align_bytes=64) for b in range(B)]
         v_g = [
-            [keep.tile([P, 2, P, 2], BF16, name="v_g00"), keep.tile([P, 2, P, 2], BF16, name="v_g01")],
-            [keep.tile([P, 2, P, 2], BF16, name="v_g10"), placed([P, 2, P, 2], BF16, "v_g11", LAST_ROWS_AT)],
+            [keep.tile([P, 2, P, 2], BF16, name="v_g00"), placed([P, 2, P, 2], BF16, "v_g01", SECOND_ROWS_AT)],
+            [placed([P, 2, P, 2], BF16, "v_g10", THIRD_ROWS_AT), placed([P, 2, P, 2], BF16, "v_g11", LAST_ROWS_AT)],
         ]
         v_bf = [
-            [placed([P, N], BF16, "v_bf%d0" % b, (5 + b) * KB), keep.tile([P, N], BF16, name="v_bf%d1" % b, align_bytes=64)]
-            for b in range(B)
+            [placed([P, N], BF16, "v_bf00", 5 * KB), keep.tile([P, N], BF16, name="v_bf01", align_bytes=64)],
+            [placed([P, N], BF16, "v_bf10", SECOND_ROWS_AT), keep.tile([P, N], BF16, name="v_bf11", align_bytes=64)],
         ]
         inv_sum = placed([P, BLOCKS], F32, "inv_sum", 7 * KB)
         gates = placed([P, BLOCKS, DV], F32, "gates", LAST_ROWS_AT)
@@ -167,7 +169,18 @@ def tile_attend_rel2_gate_pgb2q256n512t2048_kernel(tc, q_words, q_scales, k_word
             nc.vector.quantize_mx(out=v_codes[b][:, cols].bitcast(FP8X4), scales=v_plane[b][:, cols], in_=v_bf[b][h][:])
 
         def sums_of(blk):
-            return score_banks[QB + blk][:, 0:DV] if blk < QB else turned[blk - QB][:, 0:EB, :].rearrange("p h e -> p (h e)")
+            return score_banks[QB + blk][:, 0:DV] if blk < QB else turned[blk][:, 0:EB, :].rearrange("p h e -> p (h e)")
+
+        def product(blk, cols):
+            nc.tensor.matmul_mx(
+                out=sums_of(blk)[:, cols],
+                lhsT=w_codes[blk][:].bitcast(FP8X4),
+                lhsT_scale=w_plane[blk][:],
+                rhs=v_codes[blk // QB][:, cols].bitcast(FP8X4),
+                rhs_scale=v_plane[blk // QB][:, cols],
+                start=True,
+                stop=True,
+            )
 
         for b in range(B):
             nc.vector.tensor_copy(vs_g[b][:].bitcast(U32).rearrange("p t m -> p m t"), vs_pool[:].bitcast(U32).indirect(slots(b)))
@@ -213,11 +226,11 @@ def tile_attend_rel2_gate_pgb2q256n512t2048_kernel(tc, q_words, q_scales, k_word
         for b in range(B):
             for h in range(EB):
                 copy_values(b, h)
-        for j in range(QB):
-            quantise_weights(j)
-        for h in range(EB):
-            quantise_values(0, h)
+        quantise_weights(0)
+        quantise_values(0, 0)
+        quantise_weights(1)
         nc.vector.reciprocal(inv_sum[:], row_sum[:])
+        quantise_values(0, 1)
         quantise_weights(2)
         quantise_values(1, 0)
         quantise_weights(3)
@@ -225,17 +238,10 @@ def tile_attend_rel2_gate_pgb2q256n512t2048_kernel(tc, q_words, q_scales, k_word
         for blk in range(BLOCKS):
             b, j = divmod(blk, QB)
             nc.scalar.activation(gates[:, blk, :], gate_in[b][:, j, :], ACT.Sigmoid)
-        for blk in range(BLOCKS):
-            b = blk // QB
-            nc.tensor.matmul_mx(
-                out=sums_of(blk),
-                lhsT=w_codes[blk][:].bitcast(FP8X4),
-                lhsT_scale=w_plane[blk][:],
-                rhs=v_codes[b][:].bitcast(FP8X4),
-                rhs_scale=v_plane[b][:],
-                start=True,
-                stop=True,
-            )
+        for b in range(B):
+            for h in range(EB):
+                for j in range(QB):
+                    product(b * QB + j, slice(h * P, (h + 1) * P))
         for blk in range(BLOCKS):
             b, j = divmod(blk, QB)
             nc.vector.scalar_tensor_tensor(result[blk][:], sums_of(blk), inv_sum[:, blk : blk + 1], gates[:, blk, :], ALU.mult, ALU.mult)

@@ -24,8 +24,9 @@ EB = DV // P
 LIST_COLS = N // 16
 KB = 1024
 LAST_ROWS_AT = T * 4
-THIRD_ROWS_AT = LAST_ROWS_AT + BLOCKS * DV * 4
-SECOND_ROWS_AT = THIRD_ROWS_AT + KB
+SECOND_ROWS_AT = LAST_ROWS_AT + (BLOCKS - 1) * DV * 4
+SECOND_VALUES_AT = SECOND_ROWS_AT + KB
+LAST_VALUES_AT = SECOND_VALUES_AT + KB
 
 
 def tile_attend_rel2_gate_pgb2q256n512t2048_kernel(tc, q_words, q_scales, k_words, k_scales, vT, vs, og, offs, out):
@@ -84,9 +85,8 @@ def tile_attend_rel2_gate_pgb2q256n512t2048_kernel(tc, q_words, q_scales, k_word
         for b in range(B):
             nc.sync.dma_start(gate_in[b][:], og[b].rearrange("(j p) e -> p j e", p=P))
 
-        def slots(b, first=0, count=N):
-            at = b * LIST_COLS + first // 16
-            return offsets[:, at : at + count // 16]
+        def slots(b):
+            return offsets[:, b * LIST_COLS : (b + 1) * LIST_COLS]
 
         ks_g = keep.tile([P, B, 4, P], U8, name="ks_g", align_bytes=64)
         vs_g = [keep.tile([P, 4, P], F32, name="vs_g%d" % b) for b in range(B)]
@@ -96,23 +96,26 @@ def tile_attend_rel2_gate_pgb2q256n512t2048_kernel(tc, q_words, q_scales, k_word
         vs_t = [keep.tile([P, 1, 4], F32, name="vs_t%d" % b) for b in range(B)]
         row_sum = keep.tile([P, BLOCKS], F32, name="row_sum")
         probs = [keep.tile([P, N + 8], F32, name="prob%d" % blk) for blk in range(BLOCKS)]
-        w_bf = [keep.tile([P, P, 4], BF16, name="w_bf%d" % blk, align_bytes=64) for blk in range(BLOCKS - 1)]
-        w_bf.append(placed([P, P, 4], BF16, "w_bf3", THIRD_ROWS_AT))
-        w_codes = [placed([P, P], U32, "w_codes%d" % blk, KB + blk * P * 4) for blk in range(BLOCKS)]
+        w_bf = [keep.tile([P, P, 4], BF16, name="w_bf%d" % blk, align_bytes=64) for blk in range(BLOCKS)]
+        w_codes = [keep.tile([P, P], U32, name="w_codes%d" % j, align_bytes=64) for j in range(QB)]
+        w_codes += [placed([P, P], U32, "w_codes%d" % (QB + j), SECOND_VALUES_AT + j * P * 4) for j in range(QB)]
         w_plane = [keep.tile([P, P], U8, name="w_plane%d" % blk, align_bytes=64) for blk in range(BLOCKS)]
-        v_codes = [placed([P, DV], U32, "v_codes%d" % b, (3 + b) * KB) for b in range(B)]
+        v_codes = [keep.tile([P, DV], U32, name="v_codes%d" % b, align_bytes=64) for b in range(B)]
         v_plane = [keep.tile([P, DV], U8, name="v_plane%d" % b, align_bytes=64) for b in range(B)]
         v_g = [
             [keep.tile([P, 2, P, 2], BF16, name="v_g00"), placed([P, 2, P, 2], BF16, "v_g01", SECOND_ROWS_AT)],
-            [placed([P, 2, P, 2], BF16, "v_g10", THIRD_ROWS_AT), placed([P, 2, P, 2], BF16, "v_g11", LAST_ROWS_AT)],
+            [keep.tile([P, 2, P, 2], BF16, name="v_g10"), placed([P, 2, P, 2], BF16, "v_g11", LAST_ROWS_AT)],
         ]
         v_bf = [
-            [placed([P, N], BF16, "v_bf00", 5 * KB), keep.tile([P, N], BF16, name="v_bf01", align_bytes=64)],
-            [placed([P, N], BF16, "v_bf10", SECOND_ROWS_AT), keep.tile([P, N], BF16, name="v_bf11", align_bytes=64)],
+            [placed([P, N], BF16, "v_bf00", 0), placed([P, N], BF16, "v_bf01", SECOND_VALUES_AT)],
+            [placed([P, N], BF16, "v_bf10", SECOND_ROWS_AT), placed([P, N], BF16, "v_bf11", LAST_VALUES_AT)],
         ]
-        inv_sum = placed([P, BLOCKS], F32, "inv_sum", 7 * KB)
-        gates = placed([P, BLOCKS, DV], F32, "gates", LAST_ROWS_AT)
-        result = [keep.tile([P, DV], F32, name="result%d" % blk) for blk in range(BLOCKS)]
+        inv_sum = keep.tile([P, BLOCKS], F32, name="inv_sum")
+        first_gate = keep.tile([P, DV], F32, name="first_gate")
+        later_gates = placed([P, BLOCKS - 1, DV], F32, "later_gates", LAST_ROWS_AT)
+        gates = [first_gate[:]] + [later_gates[:, blk, :] for blk in range(BLOCKS - 1)]
+        result = [placed([P, DV], F32, "result0", LAST_VALUES_AT)]
+        result += [keep.tile([P, DV], F32, name="result%d" % blk) for blk in range(1, BLOCKS)]
 
         def scores(blk, o):
             b, j = divmod(blk, QB)
@@ -139,17 +142,15 @@ def tile_attend_rel2_gate_pgb2q256n512t2048_kernel(tc, q_words, q_scales, k_word
                 ALU.mult,
             )
 
-        def value_rows(b, h, first, count):
-            return v_g[b][h][:, :, first // 4 : (first + count) // 4, :].rearrange("p u m e -> p m u e")
-
-        def gather_values_on_vector(b, h, first, count):
-            nc.vector.tensor_copy(value_rows(b, h, first, count), v_pool[h][:].indirect(slots(b, first, count)))
-
-        def gather_values_on_scalar(b, h, first, count):
-            nc.scalar.activation(value_rows(b, h, first, count), v_pool[h][:].indirect(slots(b, first, count)), ACT.Copy)
+        def gather_values(b, h):
+            rows = v_g[b][h][:].rearrange("p u m e -> p m u e")
+            if h == 0:
+                nc.vector.tensor_copy(rows, v_pool[h][:].indirect(slots(b)))
+            else:
+                nc.scalar.activation(rows, v_pool[h][:].indirect(slots(b)), ACT.Copy)
 
         def value_bank(b, h):
-            return turned[b][:, 0:2, :] if h == 0 else score_banks[b][:, 0 : 2 * P].rearrange("p (u e) -> p u e", u=2)
+            return score_banks[b * EB + h][:, 0 : 2 * P].rearrange("p (u e) -> p u e", u=2)
 
         def turn_values(b, h):
             for u in range(2):
@@ -169,7 +170,7 @@ def tile_attend_rel2_gate_pgb2q256n512t2048_kernel(tc, q_words, q_scales, k_word
             nc.vector.quantize_mx(out=v_codes[b][:, cols].bitcast(FP8X4), scales=v_plane[b][:, cols], in_=v_bf[b][h][:])
 
         def sums_of(blk):
-            return score_banks[QB + blk][:, 0:DV] if blk < QB else turned[blk][:, 0:EB, :].rearrange("p h e -> p (h e)")
+            return turned[blk][:, 0:EB, :].rearrange("p h e -> p (h e)")
 
         def product(blk, cols):
             nc.tensor.matmul_mx(
@@ -210,39 +211,38 @@ def tile_attend_rel2_gate_pgb2q256n512t2048_kernel(tc, q_words, q_scales, k_word
                 nc.scalar.activation(pos[:, blk, 0:N], score_banks[blk][:], ACT.Relu)
             else:
                 nc.vector.tensor_scalar_max(pos[:, blk, 0:N], score_banks[blk][:], 0.0)
-        gather_values_on_vector(0, 0, 0, N)
+        for b in range(B):
+            gather_values(b, 0)
         for blk in range(BLOCKS):
             square_and_turn(blk)
-        gather_values_on_scalar(1, 0, 0, N)
-        for blk in range(BLOCKS - 1):
+        for blk in range(BLOCKS):
             weights(blk)
         for b in range(B):
-            gather_values_on_vector(b, 1, 0, N // 2)
-            gather_values_on_scalar(b, 1, N // 2, N // 2)
-        weights(BLOCKS - 1)
+            gather_values(b, 1)
         for h in range(EB):
             for b in range(B):
                 turn_values(b, h)
         for b in range(B):
             for h in range(EB):
                 copy_values(b, h)
-        quantise_weights(0)
-        quantise_values(0, 0)
-        quantise_weights(1)
+        for j in range(QB):
+            quantise_weights(j)
         nc.vector.reciprocal(inv_sum[:], row_sum[:])
-        quantise_values(0, 1)
-        quantise_weights(2)
+        for h in range(EB):
+            quantise_values(0, h)
         quantise_values(1, 0)
-        quantise_weights(3)
+        quantise_weights(2)
         quantise_values(1, 1)
+        quantise_weights(3)
         for blk in range(BLOCKS):
             b, j = divmod(blk, QB)
-            nc.scalar.activation(gates[:, blk, :], gate_in[b][:, j, :], ACT.Sigmoid)
-        for b in range(B):
-            for h in range(EB):
-                for j in range(QB):
-                    product(b * QB + j, slice(h * P, (h + 1) * P))
+            nc.scalar.activation(gates[blk], gate_in[b][:, j, :], ACT.Sigmoid)
+        for h in range(EB):
+            for j in range(QB):
+                product(j, slice(h * P, (h + 1) * P))
+        for j in range(QB):
+            product(QB + j, slice(0, DV))
         for blk in range(BLOCKS):
             b, j = divmod(blk, QB)
-            nc.vector.scalar_tensor_tensor(result[blk][:], sums_of(blk), inv_sum[:, blk : blk + 1], gates[:, blk, :], ALU.mult, ALU.mult)
+            nc.vector.scalar_tensor_tensor(result[blk][:], sums_of(blk), inv_sum[:, blk : blk + 1], gates[blk], ALU.mult, ALU.mult)
             nc.sync.dma_start(out[b, j * P : (j + 1) * P, :], result[blk][:])

@@ -48,15 +48,17 @@ def tile_attend_rel2_gate_pgb2q256n512t2048_kernel(tc, q_words, q_scales, k_word
         q_plane = keep.tile([P, B * PASSES, NQ], U8, name="q_plane", align_bytes=64)
         gate_in = [keep.tile([P, QB, DV], F32, name="gate_in%d" % b) for b in range(B)]
         ident = keep.tile([P, P], F32, name="ident")
+        warm_in = keep.tile([P, 8], F32, name="warm_in")
         warm = keep.tile([P, 8], F32, name="warm")
         pos = keep.tile([P, BLOCKS, N + 8], F32, name="pos")
 
         nc.gpsimd.memset(ks_pool[:].bitcast(I32), 0)
         nc.gpsimd.memset(q_plane[:].rearrange("p g q -> p (g q)").bitcast(I32), 0)
         nc.gpsimd.memset(vs_pool[0 : P - 1, :], 0.0)
+        nc.gpsimd.memset(warm_in[:], 0.0)
         make_identity(nc, ident[:])
         nc.gpsimd.memset(pos[:, :, N : N + 1], 1.0)
-        nc.scalar.activation(warm[0:96, :], vs_pool[0:96, 0:8], ACT.Sigmoid)
+        nc.scalar.activation(warm[:], warm_in[:], ACT.Sigmoid)
 
         def load_queries(o):
             nc.sync.dma_start(q_codes[o][:], q_words[:, o].rearrange("b p q r -> p b (q r)").bitcast(I32))

@@ -66,20 +66,24 @@ def tile_attend_rel2_gate_pgb2q256n512t2048_kernel(tc, q_words, q_scales, k_word
         def load_keys(o):
             nc.sync.dma_start(k_pool[o][:], k_words[o].rearrange("p t r -> p (t r)").bitcast(I32))
 
-        load_queries(0)
+        def load_query_scales(r):
+            nc.sync.dma_start(
+                q_plane[r:P:32, :, :].bitcast(I32),
+                q_scales.rearrange("b o (c r) q -> r c (b o) q", r=4)[r].bitcast(I32),
+            )
+
         nc.sync.dma_start(offsets[:], offs)
+        load_queries(0)
         nc.sync.dma_start(vs_pool[P - 1 : P, :], vs[0:1, :])
         for quad in (2, 3, 0, 1):
             nc.sync.dma_start(
                 ks_pool[32 * quad : 32 * quad + 4 * PASSES, :].bitcast(I32),
                 k_scales[:, 4 * quad : 4 * quad + 4, :].bitcast(I32),
             )
+        load_query_scales(0)
         load_keys(0)
-        for r in range(4):
-            nc.sync.dma_start(
-                q_plane[r:P:32, :, :].bitcast(I32),
-                q_scales.rearrange("b o (c r) q -> r c (b o) q", r=4)[r].bitcast(I32),
-            )
+        for r in range(1, 4):
+            load_query_scales(r)
         load_keys(1)
         load_queries(1)
         for h in range(EB):

@@ -103,8 +103,8 @@ def tile_attend_rel2_gate_pgb2q256n512t2048_kernel(tc, q_words, q_scales, k_word
         row_sum = keep.tile([P, BLOCKS], F32, name="row_sum")
         probs = [keep.tile([P, N + 8], F32, name="prob%d" % blk) for blk in range(BLOCKS)]
         w_bf = [keep.tile([P, P, 4], BF16, name="w_bf%d" % blk, align_bytes=64) for blk in range(BLOCKS)]
-        w_codes = [keep.tile([P, P], U32, name="w_codes%d" % j, align_bytes=64) for j in range(QB)]
-        w_codes += [placed([P, P], U32, "w_codes%d" % (QB + j), SECOND_VALUES_AT + j * P * 4) for j in range(QB)]
+        w_codes = [keep.tile([P, P], U32, name="w_codes%d" % blk, align_bytes=64) for blk in range(BLOCKS - 1)]
+        w_codes.append(placed([P, P], U32, "w_codes3", SECOND_VALUES_AT))
         w_plane = [keep.tile([P, P], U8, name="w_plane%d" % blk, align_bytes=64) for blk in range(BLOCKS)]
         v_codes = [keep.tile([P, DV], U32, name="v_codes%d" % b, align_bytes=64) for b in range(B)]
         v_plane = [keep.tile([P, DV], U8, name="v_plane%d" % b, align_bytes=64) for b in range(B)]
@@ -120,8 +120,8 @@ def tile_attend_rel2_gate_pgb2q256n512t2048_kernel(tc, q_words, q_scales, k_word
         first_gate = keep.tile([P, DV], F32, name="first_gate")
         later_gates = placed([P, BLOCKS - 1, DV], F32, "later_gates", LAST_ROWS_AT)
         gates = [first_gate[:]] + [later_gates[:, blk, :] for blk in range(BLOCKS - 1)]
-        result = [placed([P, DV], F32, "result0", LAST_VALUES_AT)]
-        result += [keep.tile([P, DV], F32, name="result%d" % blk) for blk in range(1, BLOCKS)]
+        first_result = [placed([P, P], F32, "result00", SECOND_ROWS_AT), placed([P, P], F32, "result01", LAST_VALUES_AT)]
+        result = {blk: keep.tile([P, DV], F32, name="result%d" % blk) for blk in range(1, BLOCKS)}
 
         def scores(blk, o):
             b, j = divmod(blk, QB)
@@ -175,12 +175,14 @@ def tile_attend_rel2_gate_pgb2q256n512t2048_kernel(tc, q_words, q_scales, k_word
             cols = slice(h * P, (h + 1) * P)
             nc.vector.quantize_mx(out=v_codes[b][:, cols].bitcast(FP8X4), scales=v_plane[b][:, cols], in_=v_bf[b][h][:])
 
-        def sums_of(blk):
-            return turned[blk][:, 0:EB, :].rearrange("p h e -> p (h e)")
+        def sums_of(blk, cols):
+            if blk == 0 and cols.start == P:
+                return score_banks[0][:, 0:P]
+            return turned[blk][:, 0:EB, :].rearrange("p h e -> p (h e)")[:, cols]
 
         def product(blk, cols):
             nc.tensor.matmul_mx(
-                out=sums_of(blk)[:, cols],
+                out=sums_of(blk, cols),
                 lhsT=w_codes[blk][:].bitcast(FP8X4),
                 lhsT_scale=w_plane[blk][:],
                 rhs=v_codes[blk // QB][:, cols].bitcast(FP8X4),
@@ -231,24 +233,28 @@ def tile_attend_rel2_gate_pgb2q256n512t2048_kernel(tc, q_words, q_scales, k_word
         for b in range(B):
             for h in range(EB):
                 copy_values(b, h)
-        for j in range(QB):
-            quantise_weights(j)
+        for blk in range(BLOCKS - 1):
+            quantise_weights(blk)
         nc.vector.reciprocal(inv_sum[:], row_sum[:])
         for h in range(EB):
             quantise_values(0, h)
         quantise_values(1, 0)
-        quantise_weights(2)
-        quantise_values(1, 1)
         quantise_weights(3)
+        quantise_values(1, 1)
         for blk in range(BLOCKS):
             b, j = divmod(blk, QB)
             nc.scalar.activation(gates[blk], gate_in[b][:, j, :], ACT.Sigmoid)
-        for h in range(EB):
-            for j in range(QB):
-                product(j, slice(h * P, (h + 1) * P))
-        for j in range(QB):
-            product(QB + j, slice(0, DV))
-        for blk in range(BLOCKS):
+        for b in range(B):
+            for h in range(EB):
+                for j in range(QB):
+                    product(b * QB + j, slice(h * P, (h + 1) * P))
+
+        def finish(blk, cols, into):
             b, j = divmod(blk, QB)
-            nc.vector.scalar_tensor_tensor(result[blk][:], sums_of(blk), inv_sum[:, blk : blk + 1], gates[blk], ALU.mult, ALU.mult)
-            nc.sync.dma_start(out[b, j * P : (j + 1) * P, :], result[blk][:])
+            nc.vector.scalar_tensor_tensor(into, sums_of(blk, cols), inv_sum[:, blk : blk + 1], gates[blk][:, cols], ALU.mult, ALU.mult)
+            nc.sync.dma_start(out[b, j * P : (j + 1) * P, cols], into)
+
+        for h in range(EB):
+            finish(0, slice(h * P, (h + 1) * P), first_result[h][:])
+        for blk in range(1, BLOCKS):
+            finish(blk, slice(0, DV), result[blk][:])

from contextlib import ExitStack

import concourse.mybir as mybir
from concourse.masks import make_identity

B, N, T, D, DV, NQ = 2, 512, 2048, 1024, 256, 256
FLOPS = 2 * B * NQ * N * (D + DV)

F32 = mybir.dt.float32
BF16 = mybir.dt.bfloat16
I32 = mybir.dt.int32
U32 = mybir.dt.uint32
U16 = mybir.dt.uint16
U8 = mybir.dt.uint8
FP8X4 = mybir.dt.float8_e4m3fn_x4
ACT = mybir.ActivationFunctionType
ALU = mybir.AluOpType

P = 128
PASSES = D // 512
QB = NQ // P
BLOCKS = B * QB
EB = DV // P
LIST_COLS = N // 16
KB = 1024
LAST_ROWS_AT = T * 4
SECOND_ROWS_AT = LAST_ROWS_AT + (BLOCKS - 1) * DV * 4
SECOND_VALUES_AT = SECOND_ROWS_AT + KB
LAST_VALUES_AT = SECOND_VALUES_AT + KB


def tile_attend_rel2_gate_pgb2q256n512t2048_kernel(tc, q_words, q_scales, k_words, k_scales, vT, vs, og, offs, out):
    nc = tc.nc
    with ExitStack() as ctx:
        keep = ctx.enter_context(tc.tile_pool(name="keep", bufs=1))
        shared = ctx.enter_context(tc.tile_pool(name="shared", bufs=1))
        psum = ctx.enter_context(tc.psum_pool(name="psum", bufs=1))

        def placed(shape, dtype, name, at):
            return shared.tile(shape, dtype, name=name, offset=at, align_bytes=64)

        offsets = keep.tile([P, B * LIST_COLS], U16, name="offsets")
        k_pool = [keep.tile([P, T], I32, name="k_pool%d" % o) for o in range(PASSES)]
        ks_pool = keep.tile([P, T], U8, name="ks_pool", align_bytes=64)
        vs_pool = keep.tile([P, T], F32, name="vs_pool")
        v_pool = [keep.tile([P, T], F32, name="v_pool0"), placed([P, T], F32, "v_pool1", 0)]
        q_codes = [keep.tile([P, B, NQ], I32, name="q_codes%d" % o, align_bytes=64) for o in range(PASSES)]
        q_plane = keep.tile([P, B * PASSES, NQ], U8, name="q_plane", align_bytes=64)
        gate_in = [keep.tile([P, QB, DV], F32, name="gate_in%d" % b) for b in range(B)]
        ident = keep.tile([P, P], F32, name="ident")
        warm_in = keep.tile([P, 8], F32, name="warm_in")
        warm = keep.tile([P, 8], F32, name="warm")
        pos = keep.tile([P, BLOCKS, N + 8], F32, name="pos")

        nc.gpsimd.memset(ks_pool[:].bitcast(I32), 0)
        nc.gpsimd.memset(q_plane[:].rearrange("p g q -> p (g q)").bitcast(I32), 0)
        nc.gpsimd.memset(vs_pool[0 : P - 1, :], 0.0)
        nc.gpsimd.memset(warm_in[:], 0.0)
        make_identity(nc, ident[:])
        nc.gpsimd.memset(pos[:, :, N : N + 1], 1.0)
        nc.scalar.activation(warm[:], warm_in[:], ACT.Sigmoid)

        def load_queries(o):
            nc.sync.dma_start(q_codes[o][:], q_words[:, o].rearrange("b p q r -> p b (q r)").bitcast(I32))

        def load_keys(o):
            nc.sync.dma_start(k_pool[o][:], k_words[o].rearrange("p t r -> p (t r)").bitcast(I32))

        def load_query_scales(r):
            nc.sync.dma_start(
                q_plane[r:P:32, :, :].bitcast(I32),
                q_scales.rearrange("b o (c r) q -> r c (b o) q", r=4)[r].bitcast(I32),
            )

        nc.sync.dma_start(offsets[:], offs)
        load_queries(0)
        nc.sync.dma_start(vs_pool[P - 1 : P, :], vs[0:1, :])
        for quad in (2, 3, 0, 1):
            nc.sync.dma_start(
                ks_pool[32 * quad : 32 * quad + 4 * PASSES, :].bitcast(I32),
                k_scales[:, 4 * quad : 4 * quad + 4, :].bitcast(I32),
            )
        load_query_scales(0)
        load_keys(0)
        for r in range(1, 4):
            load_query_scales(r)
        load_keys(1)
        load_queries(1)
        for h in range(EB):
            nc.sync.dma_start(v_pool[h][:], vT[h * P : (h + 1) * P, :])
        for b in range(B):
            nc.sync.dma_start(gate_in[b][:], og[b].rearrange("(j p) e -> p j e", p=P))

        def slots(b):
            return offsets[:, b * LIST_COLS : (b + 1) * LIST_COLS]

        ks_g = keep.tile([P, B, 4, P], U8, name="ks_g", align_bytes=64)
        vs_g = [keep.tile([P, 4, P], F32, name="vs_g%d" % b) for b in range(B)]
        k_g = [keep.tile([P, B, 4, P], U32, name="k_g%d" % o, align_bytes=64) for o in range(PASSES)]
        score_banks = [psum.tile([P, N], F32, name="score%d" % blk) for blk in range(BLOCKS)]
        turned = [psum.tile([P, 4, P], F32, name="turned%d" % blk) for blk in range(BLOCKS)]
        vs_t = [keep.tile([P, 1, 4], F32, name="vs_t%d" % b) for b in range(B)]
        row_sum = keep.tile([P, BLOCKS], F32, name="row_sum")
        probs = [keep.tile([P, N + 8], F32, name="prob%d" % blk) for blk in range(BLOCKS)]
        w_bf = [keep.tile([P, P, 4], BF16, name="w_bf%d" % blk, align_bytes=64) for blk in range(BLOCKS)]
        w_codes = [keep.tile([P, P], U32, name="w_codes%d" % blk, align_bytes=64) for blk in range(BLOCKS - 1)]
        w_codes.append(placed([P, P], U32, "w_codes3", SECOND_VALUES_AT))
        w_plane = [keep.tile([P, P], U8, name="w_plane%d" % blk, align_bytes=64) for blk in range(BLOCKS)]
        v_codes = [keep.tile([P, DV], U32, name="v_codes%d" % b, align_bytes=64) for b in range(B)]
        v_plane = [keep.tile([P, DV], U8, name="v_plane%d" % b, align_bytes=64) for b in range(B)]
        v_g = [
            [keep.tile([P, 2, P, 2], BF16, name="v_g00"), placed([P, 2, P, 2], BF16, "v_g01", SECOND_ROWS_AT)],
            [keep.tile([P, 2, P, 2], BF16, name="v_g10"), placed([P, 2, P, 2], BF16, "v_g11", LAST_ROWS_AT)],
        ]
        v_bf = [
            [placed([P, N], BF16, "v_bf00", 0), placed([P, N], BF16, "v_bf01", SECOND_VALUES_AT)],
            [placed([P, N], BF16, "v_bf10", SECOND_ROWS_AT), placed([P, N], BF16, "v_bf11", LAST_VALUES_AT)],
        ]
        inv_sum = keep.tile([P, BLOCKS], F32, name="inv_sum")
        first_gate = keep.tile([P, DV], F32, name="first_gate")
        later_gates = placed([P, BLOCKS - 1, DV], F32, "later_gates", LAST_ROWS_AT)
        gates = [first_gate[:]] + [later_gates[:, blk, :] for blk in range(BLOCKS - 1)]
        first_result = [placed([P, P], F32, "result00", SECOND_ROWS_AT), placed([P, P], F32, "result01", LAST_VALUES_AT)]
        result = {blk: keep.tile([P, DV], F32, name="result%d" % blk) for blk in range(1, BLOCKS)}

        def scores(blk, o):
            b, j = divmod(blk, QB)
            nc.tensor.matmul_mx(
                out=score_banks[blk][:],
                lhsT=q_codes[o][:, b, j * P : (j + 1) * P].bitcast(FP8X4),
                lhsT_scale=q_plane[:, b * PASSES + o, j * P : (j + 1) * P],
                rhs=k_g[o][:, b].rearrange("p t m -> p (t m)").bitcast(FP8X4),
                rhs_scale=ks_g[4 * o : P, b].rearrange("p t m -> p (t m)"),
                start=(o == 0),
                stop=(o == PASSES - 1),
            )

        def square_and_turn(blk):
            nc.scalar.activation(probs[blk][:, 0 : N + 1], pos[:, blk, 0 : N + 1], ACT.Square, accum_out=row_sum[:, blk : blk + 1])
            for t in range(4):
                nc.tensor.transpose(turned[blk][:, t, :], probs[blk][:, t * P : (t + 1) * P], ident[:])

        def weights(blk):
            nc.vector.tensor_tensor(
                w_bf[blk][:],
                turned[blk][:].rearrange("p t q -> p q t"),
                vs_t[blk // QB][:].to_broadcast([P, P, 4]),
                ALU.mult,
            )

        def gather_values(b, h):
            rows = v_g[b][h][:].rearrange("p u m e -> p m u e")
            if h == 0:
                nc.vector.tensor_copy(rows, v_pool[h][:].indirect(slots(b)))
            else:
                nc.scalar.activation(rows, v_pool[h][:].indirect(slots(b)), ACT.Copy)

        def value_bank(b, h):
            return score_banks[b * EB + h][:, 0 : 2 * P].rearrange("p (u e) -> p u e", u=2)

        def turn_values(b, h):
            for u in range(2):
                words = v_g[b][h][:, u].rearrange("p m e -> p (m e)").bitcast(F32)
                nc.tensor.transpose(value_bank(b, h)[:, u, :], words, ident[:])

        def copy_values(b, h):
            nc.scalar.copy(v_bf[b][h][:].bitcast(F32).rearrange("p (e u) -> p e u", u=2), value_bank(b, h).rearrange("p u e -> p e u"))

        def quantise_weights(blk):
            nc.vector.quantize_mx(
                out=w_codes[blk][:].bitcast(FP8X4), scales=w_plane[blk][:], in_=w_bf[blk][:].rearrange("p q t -> p (q t)")
            )

        def quantise_values(b, h):
            cols = slice(h * P, (h + 1) * P)
            nc.vector.quantize_mx(out=v_codes[b][:, cols].bitcast(FP8X4), scales=v_plane[b][:, cols], in_=v_bf[b][h][:])

        def sums_of(blk, cols):
            if blk == 0 and cols.start == P:
                return score_banks[0][:, 0:P]
            return turned[blk][:, 0:EB, :].rearrange("p h e -> p (h e)")[:, cols]

        def product(blk, cols):
            nc.tensor.matmul_mx(
                out=sums_of(blk, cols),
                lhsT=w_codes[blk][:].bitcast(FP8X4),
                lhsT_scale=w_plane[blk][:],
                rhs=v_codes[blk // QB][:, cols].bitcast(FP8X4),
                rhs_scale=v_plane[blk // QB][:, cols],
                start=True,
                stop=True,
            )

        for b in range(B):
            nc.vector.tensor_copy(vs_g[b][:].bitcast(U32).rearrange("p t m -> p m t"), vs_pool[:].bitcast(U32).indirect(slots(b)))
        nc.vector.tensor_copy(ks_g[:].rearrange("p b t m -> p b m t"), ks_pool[:].indirect(offsets[:]))
        for o in range(PASSES):
            for b in range(B):
                nc.vector.tensor_copy(k_g[o][:, b].rearrange("p t m -> p m t"), k_pool[o][:].bitcast(U32).indirect(slots(b)))
        for b in range(B):
            for t in range(4):
                nc.tensor.transpose(turned[b][:, t, :], vs_g[b][:, t, :], ident[:])
            nc.scalar.copy(vs_t[b][:, 0, :], turned[b][:, :, P - 1])
        nc.tensor.matmul_mx(
            out=turned[BLOCKS - 1][:].rearrange("p t q -> p (t q)"),
            lhsT=q_codes[0][:, 0, 0:P].bitcast(FP8X4),
            lhsT_scale=q_plane[:, 0, 0:P],
            rhs=q_codes[0][:].rearrange("p b q -> p (b q)").bitcast(FP8X4),
            rhs_scale=q_plane[:, 0:B, :].rearrange("p g q -> p (g q)"),
            start=True,
            stop=True,
        )
        for o in range(PASSES):
            for blk in range(BLOCKS):
                scores(blk, o)

        for blk in range(BLOCKS):
            if blk == 1:
                nc.scalar.activation(pos[:, blk, 0:N], score_banks[blk][:], ACT.Relu)
            else:
                nc.vector.tensor_scalar_max(pos[:, blk, 0:N], score_banks[blk][:], 0.0)
        for b in range(B):
            gather_values(b, 0)
        for blk in range(BLOCKS):
            square_and_turn(blk)
        for blk in range(BLOCKS):
            weights(blk)
        for b in range(B):
            gather_values(b, 1)
        for h in range(EB):
            for b in range(B):
                turn_values(b, h)
        for b in range(B):
            for h in range(EB):
                copy_values(b, h)
        for blk in range(BLOCKS - 1):
            quantise_weights(blk)
        nc.vector.reciprocal(inv_sum[:], row_sum[:])
        for h in range(EB):
            quantise_values(0, h)
        quantise_values(1, 0)
        quantise_weights(3)
        quantise_values(1, 1)
        for blk in range(BLOCKS):
            b, j = divmod(blk, QB)
            nc.scalar.activation(gates[blk], gate_in[b][:, j, :], ACT.Sigmoid)
        for b in range(B):
            for h in range(EB):
                for j in range(QB):
                    product(b * QB + j, slice(h * P, (h + 1) * P))

        def finish(blk, cols, into):
            b, j = divmod(blk, QB)
            nc.vector.scalar_tensor_tensor(into, sums_of(blk, cols), inv_sum[:, blk : blk + 1], gates[blk][:, cols], ALU.mult, ALU.mult)
            nc.sync.dma_start(out[b, j * P : (j + 1) * P, cols], into)

        for h in range(EB):
            finish(0, slice(h * P, (h + 1) * P), first_result[h][:])
        for blk in range(1, BLOCKS):
            finish(blk, slice(0, DV), result[blk][:])
